import numpy as np
import ml_dtypes


def mxq(x, axis, fmt="e4m3"):
    dtype, down = {"e4m3": (ml_dtypes.float8_e4m3fn, 7), "e5m2": (ml_dtypes.float8_e5m2, 14)}[fmt]
    v = np.moveaxis(np.asarray(x, np.float32).astype(ml_dtypes.bfloat16).astype(np.float64), axis, -1)
    blocks = v.reshape(v.shape[:-1] + (-1, 32))
    amax = np.abs(blocks).max(-1, keepdims=True)
    byte = np.maximum(np.where(amax > 0, np.frexp(amax)[1] - 1 + 127, 0) - down, 1)
    scale = np.exp2(byte - 127.0)
    codes = (blocks / scale).astype(np.float32).astype(dtype).astype(np.float64)
    return np.moveaxis((codes * scale).reshape(v.shape), -1, axis)


WIDE = False


def mx_kscale(k):
    if not WIDE:
        return np.ones(k)
    levels = np.array([10, -10, 5, -5, 0])
    if k % 512:
        return np.exp2(np.random.permutation(np.resize(levels, k // 32))).repeat(32)
    a = np.empty((k // 512, 16))
    for p in range(k // 512):
        a[p, :8] = np.random.permutation(np.resize(levels, 8))
        for g in range(8):
            far = levels[np.abs(levels - a[p, g]) >= 10]
            a[p, g + 8] = far[np.random.randint(len(far))]
    return np.exp2(a.ravel()).repeat(32)


def f64(x):
    return np.asarray(x).astype(np.float64)


def striped(idx):
    return np.tile(idx.reshape(-1, 16).T, (8, 1)).astype(np.uint16)


def unstriped(offs):
    return offs[:16].T.reshape(-1).astype(np.int64)


E2M1 = np.array([0.0, 0.5, 1.0, 1.5, 2.0, 3.0, 4.0, 6.0, -0.0, -0.5, -1.0, -1.5, -2.0, -3.0, -4.0, -6.0])


def pack_weight(w, fmt):
    k, n = w.shape
    w = f64(np.asarray(w, np.float32).astype(ml_dtypes.bfloat16)).reshape(k // 32, 32, n)
    amax = np.abs(w).max(1)
    if fmt == "e4m3":
        byte = np.frexp(amax)[1] - 1 + 127 - 7
    else:
        mant, ex = np.frexp(amax / 6.0)
        byte = np.where(mant > 0.5, ex, ex - 1) + 127
    byte = np.clip(np.where(amax > 0, byte, 1), 1, 254)
    scaled = (w * np.exp2(127.0 - byte)[:, None, :]).reshape(k, n).astype(np.float32)
    by_word = np.ascontiguousarray(scaled.reshape(k // 512, 128, 4, n).transpose(0, 1, 3, 2))
    if fmt == "e4m3":
        words = by_word.astype(ml_dtypes.float8_e4m3fn).view(np.uint8)
    else:
        c = by_word.astype(ml_dtypes.float4_e2m1fn).view(np.uint8) & 0xF
        words = (c[..., 0::2] | (c[..., 1::2] << 4)).reshape(k // 512, 128, 2 * n)
    return np.ascontiguousarray(words), np.ascontiguousarray(byte.astype(np.uint8).reshape(k // 512, 16, n))


def unpack_weight(words, scales, fmt):
    g, _, n = scales.shape
    words = np.ascontiguousarray(words).reshape(g, 128, n, -1)
    if fmt == "e4m3":
        vals = words.view(ml_dtypes.float8_e4m3fn).astype(np.float64)
    else:
        nib = np.empty((g, 128, n, 4), np.uint8)
        nib[..., 0::2] = words & 0xF
        nib[..., 1::2] = words >> 4
        vals = E2M1[nib]
    vals = vals * np.repeat(np.exp2(scales.astype(np.float64) - 127.0), 8, axis=1)[..., None]
    return vals.transpose(0, 1, 3, 2).reshape(g * 512, n)


def gelu(v):
    return 0.5 * v * (1.0 + np.tanh(np.sqrt(2.0 / np.pi) * (v + 0.044715 * v**3)))


K, T, S, H, N = 1024, 4096, 1024, 1024, 512

def setup_inputs():
    n = np.random.standard_normal
    s = mx_kscale(K)[:, None]
    u = mx_kscale(H)[:, None]
    tab_words, tab_scales = pack_weight(n((K, T)) * s, "e4m3")
    w1_words, w1_scales = pack_weight(n((K, H)) / np.sqrt(K) / s, "e2m1")
    w2 = n((H, N)) / np.sqrt(H) / u
    gain = np.exp(0.3 * n(H)) * u[:, 0]
    offs = striped(np.random.permutation(T)[:S])
    offs2 = striped(np.random.permutation(S))
    return {
        "tab_words": tab_words, "tab_scales": tab_scales, "offs": offs,
        "w1_words": w1_words, "w1_scales": w1_scales,
        "gain": gain.astype(np.float32),
        "w2": w2.astype(np.float32),
        "offs2": offs2,
        "wgo": np.exp(0.3 * n((128, S))).astype(np.float32),
        "x0": n((N, S)).astype(np.float32),
    }

def reference(tab_words, tab_scales, offs, w1_words, w1_scales, gain, w2, offs2, wgo, x0):
    v = unpack_weight(tab_words, tab_scales, "e4m3")[:, unstriped(offs)]
    W1 = unpack_weight(w1_words, w1_scales, "e2m1")
    a = W1.T @ v
    h = (a + np.tanh(a)) * f64(gain)[:, None]
    y = mxq(f64(w2), 0, "e4m3").T @ mxq(h, 0, "e4m3")
    page = np.zeros((N, S))
    page[:, unstriped(offs2)] = np.tile(f64(wgo), (N // 128, 1)) * y
    gate = 1.0 / (1.0 + np.exp(-page))
    return gate * f64(x0)

@@ -1,0 +1,254 @@
+from contextlib import ExitStack
+
+import concourse.mybir as mybir
+
+K, T, S, H, N = 1024, 4096, 1024, 1024, 512
+FLOPS = 2 * K * H * S + 2 * H * N * S
+
+F32 = mybir.dt.float32
+BF16 = mybir.dt.bfloat16
+I32 = mybir.dt.int32
+U32 = mybir.dt.uint32
+U16 = mybir.dt.uint16
+U8 = mybir.dt.uint8
+FP8X4 = mybir.dt.float8_e4m3fn_x4
+FP4X4 = mybir.dt.float4_e2m1fn_x4
+ACT = mybir.ActivationFunctionType
+ALU = mybir.AluOpType
+
+P = 128
+HALF = 512
+SLICES = [(128, 1), (128, 3), (256, 3), (256, 3), (256, 3)]
+
+
+def tile_list_sorted_poem_gates_kernel(
+    tc, tab_words, tab_scales, offs, w1_words, w1_scales, gain, w2, offs2, wgo, x0, out
+):
+    nc = tc.nc
+    with ExitStack() as ctx:
+        keep = ctx.enter_context(tc.tile_pool(name="keep", bufs=1))
+        work = ctx.enter_context(tc.tile_pool(name="work", bufs=2))
+        psum_a = ctx.enter_context(tc.psum_pool(name="psum_a", bufs=5))
+        psum_y = ctx.enter_context(tc.psum_pool(name="psum_y", bufs=3))
+
+        offs_sb = keep.tile([P, S // 16], U16, name="offs_sb")
+        offs2_sb = keep.tile([P, S // 16], U16, name="offs2_sb")
+        tab_sc = keep.tile([P, T], U8, name="tab_sc", tag="slot_c", align_bytes=64)
+        w1_sc_raw = keep.tile([P, 2 * H], U8, name="w1_sc_raw", tag="slot_d", align_bytes=64)
+        v_sc1 = keep.tile([P, S], U8, name="v_sc1", align_bytes=64)
+        nc.vector.memset(tab_sc[:].bitcast(I32), 0)
+        nc.gpsimd.memset(w1_sc_raw[:].bitcast(I32), 0)
+        nc.vector.memset(v_sc1[:].bitcast(I32), 0)
+
+        nc.sync.dma_start(offs_sb[:], offs)
+        nc.sync.dma_start(offs2_sb[:], offs2)
+        w1_raw = keep.tile([P, 2, 2 * H], U8, name="w1_raw", tag="slot_a", align_bytes=64)
+        nc.sync.dma_start(w1_raw[:].bitcast(I32), w1_words.bitcast(I32).rearrange("a p c -> p a c"))
+        tab_w0 = keep.tile([P, T], I32, name="tab_w0", tag="slot_b", align_bytes=64)
+        nc.sync.dma_start(tab_w0[:], tab_words[0].rearrange("p t i -> p (t i)").bitcast(I32))
+        for r in range(4):
+            nc.sync.dma_start(
+                tab_sc[r:128:16, :].bitcast(I32),
+                tab_scales.bitcast(I32)[:, r:16:4, :].rearrange("a q t -> q a t"),
+            )
+        for q in range(4):
+            nc.gpsimd.dma_start(
+                w1_sc_raw[32 * q : 32 * q + 4, :].bitcast(I32).rearrange("p (a c) -> p a c", a=2),
+                w1_scales.bitcast(I32)[:, 4 * q : 4 * q + 4, :].rearrange("a r c -> r a c"),
+            )
+        gain_sb = keep.tile([P, 2, 4], F32, name="gain_sb")
+        nc.gpsimd.dma_start(gain_sb[:], gain.rearrange("(b p t) -> p b t", b=2, t=4))
+
+        w1_w = keep.tile([P, 2, 2 * H], U8, name="w1_w", align_bytes=64)
+        nc.vector.tensor_copy(
+            w1_w[:].rearrange("p a c -> p (a c)").bitcast(U16).rearrange("p (g t h l) -> p g h t l", g=4, t=4, l=8),
+            w1_raw[:].rearrange("p a c -> p (a c)").bitcast(U16).rearrange("p (g h l t) -> p g h t l", g=4, t=4, l=8),
+        )
+        tab_w1 = keep.tile([P, T], I32, name="tab_w1", tag="slot_a", align_bytes=64)
+        nc.sync.dma_start(tab_w1[:], tab_words[1].rearrange("p t i -> p (t i)").bitcast(I32))
+        tab_w = [tab_w0, tab_w1]
+
+        v_w = {}
+
+        def gather_words(a, half, dst):
+            nc.vector.tensor_copy(dst, tab_w[a][:].bitcast(U32).indirect(offs_sb[:, 32 * half : 32 * (half + 1)]))
+            v_w[a, half] = dst
+
+        v0 = keep.tile([P, S], U32, name="v0", align_bytes=64)
+        gather_words(0, 0, v0[:, 0:HALF])
+        v_sc0 = keep.tile([P, S], U8, name="v_sc0", align_bytes=64)
+        nc.vector.tensor_copy(v_sc0[:], tab_sc[:].indirect(offs_sb[:]))
+        nc.sync.dma_start(v_sc1[0:112, :].bitcast(I32), v_sc0[16:128, :].bitcast(I32))
+        v_sc = [v_sc0, v_sc1]
+
+        w1_sc = keep.tile([P, 2 * H], U8, name="w1_sc", align_bytes=64)
+        nc.vector.tensor_copy(
+            w1_sc[:].rearrange("p (g t h l) -> p g h t l", g=4, t=4, l=16),
+            w1_sc_raw[:].rearrange("p (g h l t) -> p g h t l", g=4, t=4, l=16),
+        )
+        v1 = keep.tile([P, S], U32, name="v1", tag="slot_d", align_bytes=64)
+        gather_words(1, 0, v1[:, 0:HALF])
+        gather_words(0, 1, v0[:, HALF:S])
+        gather_words(1, 1, v1[:, HALF:S])
+
+        w2_raw = {}
+
+        def load_w2(pair, flat):
+            for b in range(2):
+                t = flat[:, 1024 * b : 1024 * (b + 1)].rearrange("p (t n) -> p t n", t=4)
+                nc.sync.dma_start(
+                    t, w2[512 * b : 512 * (b + 1), 256 * pair : 256 * (pair + 1)].rearrange("(p t) n -> p t n", t=4)
+                )
+                w2_raw[pair, b] = t
+
+        late_c = keep.tile([P, 3 * 1024], F32, name="late_c", tag="slot_c", align_bytes=64)
+        load_w2(0, late_c)
+        wgo_sb = late_c[:, 2048:3072]
+        nc.sync.dma_start(wgo_sb, wgo)
+        late_b = keep.tile([P, 2 * 1024], F32, name="late_b", tag="slot_b", align_bytes=64)
+        load_w2(1, late_b)
+        late_a = keep.tile([P, 4 * S], F32, name="late_a", tag="slot_a", align_bytes=64)
+        x0_sb = []
+        for n in range(4):
+            nc.sync.dma_start(late_a[:, S * n : S * (n + 1)], x0[P * n : P * (n + 1), :])
+            x0_sb.append(late_a[:, S * n : S * (n + 1)])
+
+        w2_w = {}
+        w2_sc = {}
+
+        def quantise_w2(pair):
+            grouped = keep.tile([P, 2, 256, 4], BF16, name="w2_bf%d" % pair, align_bytes=64)
+            for b in range(2):
+                src = w2_raw[pair, b].rearrange("p t n -> p n t")
+                nc.gpsimd.tensor_scalar(grouped[:, b], src, 1.0, 0.0, ALU.mult, ALU.add)
+            w2_w[pair] = keep.tile([P, 512], U32, name="w2_w%d" % pair, align_bytes=64)
+            w2_sc[pair] = keep.tile([P, 512], U8, name="w2_sc%d" % pair, align_bytes=64)
+            nc.vector.quantize_mx(
+                out=w2_w[pair][:].bitcast(FP8X4),
+                scales=w2_sc[pair][:],
+                in_=grouped[:].rearrange("p b n t -> p (b n t)"),
+            )
+
+        def first_product(bank, col, b, t, j0):
+            half, jj = divmod(j0, HALF)
+            for a in range(2):
+                c0 = 512 * b + 128 * t
+                nc.tensor.matmul_mx(
+                    out=bank[:, col : col + 128],
+                    lhsT=w1_w[:, a, 2 * c0 : 2 * c0 + 256].bitcast(FP4X4),
+                    lhsT_scale=w1_sc[:, H * a + c0 : H * a + c0 + 128],
+                    rhs=v_w[a, half][:, jj : jj + 128].bitcast(FP8X4),
+                    rhs_scale=v_sc[a][:, j0 : j0 + 128],
+                    start=(a == 0),
+                    stop=(a == 1),
+                )
+
+        def h_units(h_bf, j0, w, route):
+            for u in range(w // 128):
+                for b in range(2):
+                    bank = psum_a.tile([P, 512], F32, name="a_bank")
+                    for t in range(4):
+                        first_product(bank, 128 * t, b, t, j0 + 128 * u)
+                    woven = bank[:].rearrange("p (t n) -> p n t", t=4)
+                    th = work.tile([P, 128, 4], F32, name="th", bufs=3)
+                    nc.scalar.activation(th[:], woven, ACT.Tanh)
+                    total = work.tile([P, 128, 4], F32, name="total", bufs=2)
+                    g = gain_sb[:, b, :].unsqueeze(1).to_broadcast([P, 128, 4])
+                    dst = h_bf[:, b, 128 * u : 128 * (u + 1), :]
+                    if route == 1:
+                        nc.vector.tensor_tensor(total[:], woven, th[:], ALU.add)
+                        nc.vector.tensor_tensor(dst, total[:], g, ALU.mult)
+                    elif route == 2:
+                        nc.vector.tensor_tensor(total[:], woven, th[:], ALU.add)
+                        nc.gpsimd.tensor_tensor(dst, total[:], g, ALU.mult)
+                    else:
+                        ac = work.tile([P, 128, 4], F32, name="ac", bufs=2)
+                        nc.scalar.copy(ac[:], woven)
+                        nc.gpsimd.tensor_tensor(total[:], ac[:], th[:], ALU.add)
+                        nc.gpsimd.tensor_tensor(dst, total[:], g, ALU.mult)
+
+        def h_slots(h_bf, j0, w):
+            per_bank = 512 // w
+            for b in range(2):
+                th = work.tile([P, 4, w], F32, name="th3", bufs=3)
+                ga = work.tile([P, 4, w], F32, name="ga3", bufs=3)
+                gt = work.tile([P, 4, w], F32, name="gt3", bufs=3)
+                for t0 in range(0, 4, per_bank):
+                    bank = psum_a.tile([P, 512], F32, name="a_bank")
+                    for t in range(t0, t0 + per_bank):
+                        for u in range(w // 128):
+                            first_product(bank, w * (t - t0) + 128 * u, b, t, j0 + 128 * u)
+                    nc.scalar.activation(
+                        th[:, t0 : t0 + per_bank, :].rearrange("p t n -> p (t n)"), bank[:], ACT.Tanh
+                    )
+                    for t in range(t0, t0 + per_bank):
+                        g = gain_sb[:, b, t : t + 1]
+                        nc.scalar.activation(ga[:, t, :], bank[:, w * (t - t0) : w * (t - t0 + 1)], ACT.Copy, scale=g)
+                        nc.scalar.activation(gt[:, t, :], th[:, t, :], ACT.Copy, scale=g)
+                nc.gpsimd.tensor_tensor(
+                    h_bf[:, b], ga[:].rearrange("p t n -> p n t"), gt[:].rearrange("p t n -> p n t"), ALU.add
+                )
+
+        pages = [keep.tile([P, S], F32, name="page%d" % n) for n in range(4)]
+
+        def second_product(pair, h_w, h_sc, w):
+            bank = psum_y.tile([P, 512], F32, name="y_bank")
+            for m in range(2):
+                for b in range(2):
+                    c0 = 256 * b + 128 * m
+                    nc.tensor.matmul_mx(
+                        out=bank[:, w * m : w * (m + 1)],
+                        lhsT=w2_w[pair][:, c0 : c0 + 128].bitcast(FP8X4),
+                        lhsT_scale=w2_sc[pair][:, c0 : c0 + 128],
+                        rhs=h_w[:, w * b : w * (b + 1)].bitcast(FP8X4),
+                        rhs_scale=h_sc[:, w * b : w * (b + 1)],
+                        start=(b == 0),
+                        stop=(b == 1),
+                    )
+            return bank
+
+        def put_back(pair, bank, j0, w, tag):
+            y_sb = keep.tile([P, 2, w], F32, name="y_sb", tag=tag, align_bytes=64)
+            y_ps = bank[:, 0 : 2 * w].rearrange("p (m j) -> p m j", m=2)
+            nc.vector.tensor_tensor(
+                y_sb[:], y_ps, wgo_sb[:, j0 : j0 + w].unsqueeze(1).to_broadcast([P, 2, w]), ALU.mult
+            )
+            for m in range(2):
+                window = pages[2 * pair + m][:].indirect(offs2_sb[:, j0 // 16 : (j0 + w) // 16])
+                nc.vector.tensor_copy(window, y_sb[:, m, :])
+
+        def finish(n, pieces, engine):
+            width = S // pieces
+            for c0 in range(0, S, width):
+                gate = work.tile([P, width], F32, name="gate", bufs=3)
+                nc.scalar.activation(gate[:], pages[n][:, c0 : c0 + width], ACT.Sigmoid)
+                res = work.tile([P, width], F32, name="res", bufs=3)
+                engine.tensor_tensor(res[:], gate[:], x0_sb[n][:, c0 : c0 + width], ALU.mult)
+                nc.sync.dma_start(out[P * n : P * (n + 1), c0 : c0 + width], res[:])
+
+        quantise_w2(0)
+        waiting = None
+        j0 = 0
+        for i, (w, route) in enumerate(SLICES):
+            h_bf = keep.tile([P, 2, w, 4], BF16, name="h_bf", tag="stage%d" % i, align_bytes=64)
+            if route == 3:
+                h_slots(h_bf, j0, w)
+            else:
+                h_units(h_bf, j0, w, route)
+            h_w = keep.tile([P, 2 * w], U32, name="h_w%d" % i, align_bytes=64)
+            h_sc = keep.tile([P, 2 * w], U8, name="h_sc%d" % i, align_bytes=64)
+            nc.vector.quantize_mx(
+                out=h_w[:].bitcast(FP8X4), scales=h_sc[:], in_=h_bf[:].rearrange("p b n t -> p (b n t)")
+            )
+            if waiting is not None:
+                put_back(1, second_product(1, *waiting[:3]), waiting[3], waiting[2], "stage%d" % i)
+            put_back(0, second_product(0, h_w, h_sc, w), j0, w, "first%d" % i)
+            if i == 0:
+                quantise_w2(1)
+            waiting = (h_w, h_sc, w, j0)
+            j0 = j0 + w
+        finish(0, 1, nc.gpsimd)
+        finish(1, 1, nc.gpsimd)
+        put_back(1, second_product(1, *waiting[:3]), waiting[3], waiting[2], "last")
+        finish(2, 2, nc.vector)
+        finish(3, 2, nc.vector)

@@ -18,7 +18,8 @@ ALU = mybir.AluOpType
 
 P = 128
 HALF = 512
-SLICES = [(128, 1), (128, 3), (256, 3), (256, 3), (256, 3)]
+W2_ON = ["VV", "VV"]
+SLICES = [(256, (1, 8)), (256, (8, 8)), (256, (8, 8)), (256, (8, 8))]
 
 
 def tile_list_sorted_poem_gates_kernel(
@@ -37,28 +38,29 @@ def tile_list_sorted_poem_gates_kernel(
         w1_sc_raw = keep.tile([P, 2 * H], U8, name="w1_sc_raw", tag="slot_d", align_bytes=64)
         v_sc1 = keep.tile([P, S], U8, name="v_sc1", align_bytes=64)
         nc.vector.memset(tab_sc[:].bitcast(I32), 0)
-        nc.gpsimd.memset(w1_sc_raw[:].bitcast(I32), 0)
+        nc.vector.memset(w1_sc_raw[:].bitcast(I32), 0)
         nc.vector.memset(v_sc1[:].bitcast(I32), 0)
 
         nc.sync.dma_start(offs_sb[:], offs)
         nc.sync.dma_start(offs2_sb[:], offs2)
+        gain_sb = keep.tile([P, 2, 4], F32, name="gain_sb")
         w1_raw = keep.tile([P, 2, 2 * H], U8, name="w1_raw", tag="slot_a", align_bytes=64)
         nc.sync.dma_start(w1_raw[:].bitcast(I32), w1_words.bitcast(I32).rearrange("a p c -> p a c"))
         tab_w0 = keep.tile([P, T], I32, name="tab_w0", tag="slot_b", align_bytes=64)
         nc.sync.dma_start(tab_w0[:], tab_words[0].rearrange("p t i -> p (t i)").bitcast(I32))
         for r in range(4):
-            nc.sync.dma_start(
+            nc.scalar.dma_start(
                 tab_sc[r:128:16, :].bitcast(I32),
                 tab_scales.bitcast(I32)[:, r:16:4, :].rearrange("a q t -> q a t"),
             )
         for q in range(4):
-            nc.gpsimd.dma_start(
+            queue = nc.gpsimd if q < 2 else nc.scalar
+            queue.dma_start(
                 w1_sc_raw[32 * q : 32 * q + 4, :].bitcast(I32).rearrange("p (a c) -> p a c", a=2),
                 w1_scales.bitcast(I32)[:, 4 * q : 4 * q + 4, :].rearrange("a r c -> r a c"),
             )
-        gain_sb = keep.tile([P, 2, 4], F32, name="gain_sb")
-        nc.gpsimd.dma_start(gain_sb[:], gain.rearrange("(b p t) -> p b t", b=2, t=4))
 
+        nc.gpsimd.dma_start(gain_sb[:], gain.rearrange("(b p t) -> p b t", b=2, t=4))
         w1_w = keep.tile([P, 2, 2 * H], U8, name="w1_w", align_bytes=64)
         nc.vector.tensor_copy(
             w1_w[:].rearrange("p a c -> p (a c)").bitcast(U16).rearrange("p (g t h l) -> p g h t l", g=4, t=4, l=8),
@@ -75,11 +77,11 @@ def tile_list_sorted_poem_gates_kernel(
             v_w[a, half] = dst
 
         v0 = keep.tile([P, S], U32, name="v0", align_bytes=64)
-        gather_words(0, 0, v0[:, 0:HALF])
         v_sc0 = keep.tile([P, S], U8, name="v_sc0", align_bytes=64)
         nc.vector.tensor_copy(v_sc0[:], tab_sc[:].indirect(offs_sb[:]))
         nc.sync.dma_start(v_sc1[0:112, :].bitcast(I32), v_sc0[16:128, :].bitcast(I32))
         v_sc = [v_sc0, v_sc1]
+        gather_words(0, 0, v0[:, 0:HALF])
 
         w1_sc = keep.tile([P, 2 * H], U8, name="w1_sc", align_bytes=64)
         nc.vector.tensor_copy(
@@ -119,8 +121,12 @@ def tile_list_sorted_poem_gates_kernel(
         def quantise_w2(pair):
             grouped = keep.tile([P, 2, 256, 4], BF16, name="w2_bf%d" % pair, align_bytes=64)
             for b in range(2):
-                src = w2_raw[pair, b].rearrange("p t n -> p n t")
-                nc.gpsimd.tensor_scalar(grouped[:, b], src, 1.0, 0.0, ALU.mult, ALU.add)
+                src = w2_raw[pair, b].rearrange("p t (c i) -> p c t i", i=4)
+                dst = grouped[:, b].rearrange("p (c i) t -> p c t i", i=4)
+                if W2_ON[pair][b] == "S":
+                    nc.scalar.copy(dst, src)
+                else:
+                    nc.vector.tensor_copy(dst, src)
             w2_w[pair] = keep.tile([P, 512], U32, name="w2_w%d" % pair, align_bytes=64)
             w2_sc[pair] = keep.tile([P, 512], U8, name="w2_sc%d" % pair, align_bytes=64)
             nc.vector.quantize_mx(
@@ -143,9 +149,9 @@ def tile_list_sorted_poem_gates_kernel(
                     stop=(a == 1),
                 )
 
-        def h_units(h_bf, j0, w, route):
+        def h_units(h_bf, j0, w, route, bs):
             for u in range(w // 128):
-                for b in range(2):
+                for b in bs:
                     bank = psum_a.tile([P, 512], F32, name="a_bank")
                     for t in range(4):
                         first_product(bank, 128 * t, b, t, j0 + 128 * u)
@@ -162,32 +168,56 @@ def tile_list_sorted_poem_gates_kernel(
                         nc.vector.tensor_tensor(total[:], woven, th[:], ALU.add)
                         nc.gpsimd.tensor_tensor(dst, total[:], g, ALU.mult)
                     else:
-                        ac = work.tile([P, 128, 4], F32, name="ac", bufs=2)
+                        ac = work.tile([P, 128, 4], F32, name="ac", bufs=3)
                         nc.scalar.copy(ac[:], woven)
                         nc.gpsimd.tensor_tensor(total[:], ac[:], th[:], ALU.add)
                         nc.gpsimd.tensor_tensor(dst, total[:], g, ALU.mult)
 
-        def h_slots(h_bf, j0, w):
+        def h_slots(h_bf, j0, w, route, b):
             per_bank = 512 // w
-            for b in range(2):
-                th = work.tile([P, 4, w], F32, name="th3", bufs=3)
-                ga = work.tile([P, 4, w], F32, name="ga3", bufs=3)
-                gt = work.tile([P, 4, w], F32, name="gt3", bufs=3)
-                for t0 in range(0, 4, per_bank):
-                    bank = psum_a.tile([P, 512], F32, name="a_bank")
-                    for t in range(t0, t0 + per_bank):
-                        for u in range(w // 128):
-                            first_product(bank, w * (t - t0) + 128 * u, b, t, j0 + 128 * u)
-                    nc.scalar.activation(
-                        th[:, t0 : t0 + per_bank, :].rearrange("p t n -> p (t n)"), bank[:], ACT.Tanh
-                    )
-                    for t in range(t0, t0 + per_bank):
-                        g = gain_sb[:, b, t : t + 1]
-                        nc.scalar.activation(ga[:, t, :], bank[:, w * (t - t0) : w * (t - t0 + 1)], ACT.Copy, scale=g)
-                        nc.scalar.activation(gt[:, t, :], th[:, t, :], ACT.Copy, scale=g)
-                nc.gpsimd.tensor_tensor(
-                    h_bf[:, b], ga[:].rearrange("p t n -> p n t"), gt[:].rearrange("p t n -> p n t"), ALU.add
+            total = work.tile([P, 4, w], F32, name="total6", bufs=3)
+            hn = work.tile([P, 4, w], BF16, name="hn", bufs=3)
+            for t0 in range(0, 4, per_bank):
+                bank = psum_a.tile([P, 512], F32, name="a_bank")
+                for t in range(t0, t0 + per_bank):
+                    for u in range(w // 128):
+                        first_product(bank, w * (t - t0) + 128 * u, b, t, j0 + 128 * u)
+                th = work.tile([P, 512], F32, name="th6", bufs=4)
+                nc.scalar.activation(th[:], bank[:], ACT.Tanh)
+                nc.vector.tensor_tensor(
+                    total[:, t0 : t0 + per_bank, :].rearrange("p t n -> p (t n)"), bank[:], th[:], ALU.add
                 )
+                for t in range(t0, t0 + per_bank):
+                    nc.scalar.activation(hn[:, t, :], total[:, t, :], ACT.Copy, scale=gain_sb[:, b, t : t + 1])
+            dst = h_bf[:, b].rearrange("p (c i) t -> p c t i", i=4)
+            src = hn[:].rearrange("p t (c i) -> p c t i", i=4)
+            if route == 6:
+                nc.scalar.copy(dst, src)
+            else:
+                nc.vector.tensor_copy(dst, src)
+
+        def h_scaled(h_bf, j0, w, b, i):
+            per_bank = 512 // w
+            ga = keep.tile([P, 4, w], F32, name="ga3", tag="ga%d%d" % (i, b), align_bytes=64)
+            gt = work.tile([P, 4, w], F32, name="gt3", bufs=3)
+            for t0 in range(0, 4, per_bank):
+                bank = psum_a.tile([P, 512], F32, name="a_bank")
+                for t in range(t0, t0 + per_bank):
+                    for u in range(w // 128):
+                        first_product(bank, w * (t - t0) + 128 * u, b, t, j0 + 128 * u)
+                th = work.tile([P, 512], F32, name="th6", bufs=4)
+                nc.scalar.activation(th[:], bank[:], ACT.Tanh)
+                for t in range(t0, t0 + per_bank):
+                    g = gain_sb[:, b, t : t + 1]
+                    cols = slice(w * (t - t0), w * (t - t0 + 1))
+                    nc.scalar.activation(ga[:, t, :], bank[:, cols], ACT.Copy, scale=g)
+                    nc.scalar.activation(gt[:, t, :], th[:, cols], ACT.Copy, scale=g)
+            nc.vector.tensor_tensor(
+                h_bf[:, b].rearrange("p (c i) t -> p c t i", i=4),
+                ga[:].rearrange("p t (c i) -> p c t i", i=4),
+                gt[:].rearrange("p t (c i) -> p c t i", i=4),
+                ALU.add,
+            )
 
         pages = [keep.tile([P, S], F32, name="page%d" % n) for n in range(4)]
 
@@ -210,45 +240,46 @@ def tile_list_sorted_poem_gates_kernel(
         def put_back(pair, bank, j0, w, tag):
             y_sb = keep.tile([P, 2, w], F32, name="y_sb", tag=tag, align_bytes=64)
             y_ps = bank[:, 0 : 2 * w].rearrange("p (m j) -> p m j", m=2)
-            nc.vector.tensor_tensor(
-                y_sb[:], y_ps, wgo_sb[:, j0 : j0 + w].unsqueeze(1).to_broadcast([P, 2, w]), ALU.mult
-            )
+            nc.scalar.copy(y_sb[:], y_ps)
             for m in range(2):
                 window = pages[2 * pair + m][:].indirect(offs2_sb[:, j0 // 16 : (j0 + w) // 16])
-                nc.vector.tensor_copy(window, y_sb[:, m, :])
+                nc.vector.tensor_tensor(window, y_sb[:, m, :], wgo_sb[:, j0 : j0 + w], ALU.mult)
 
         def finish(n, pieces, engine):
             width = S // pieces
             for c0 in range(0, S, width):
-                gate = work.tile([P, width], F32, name="gate", bufs=3)
+                gate = work.tile([P, width], F32, name="gate", bufs=4)
                 nc.scalar.activation(gate[:], pages[n][:, c0 : c0 + width], ACT.Sigmoid)
-                res = work.tile([P, width], F32, name="res", bufs=3)
-                engine.tensor_tensor(res[:], gate[:], x0_sb[n][:, c0 : c0 + width], ALU.mult)
-                nc.sync.dma_start(out[P * n : P * (n + 1), c0 : c0 + width], res[:])
+                res = x0_sb[n][:, c0 : c0 + width]
+                engine.tensor_tensor(res, gate[:], res, ALU.mult)
+                nc.sync.dma_start(out[P * n : P * (n + 1), c0 : c0 + width], res)
 
         quantise_w2(0)
         waiting = None
         j0 = 0
         for i, (w, route) in enumerate(SLICES):
             h_bf = keep.tile([P, 2, w, 4], BF16, name="h_bf", tag="stage%d" % i, align_bytes=64)
-            if route == 3:
-                h_slots(h_bf, j0, w)
-            else:
-                h_units(h_bf, j0, w, route)
+            for b in range(2):
+                if route[b] == 8:
+                    h_scaled(h_bf, j0, w, b, i)
+                elif route[b] >= 6:
+                    h_slots(h_bf, j0, w, route[b], b)
+                else:
+                    h_units(h_bf, j0, w, route[b], [b])
             h_w = keep.tile([P, 2 * w], U32, name="h_w%d" % i, align_bytes=64)
             h_sc = keep.tile([P, 2 * w], U8, name="h_sc%d" % i, align_bytes=64)
             nc.vector.quantize_mx(
                 out=h_w[:].bitcast(FP8X4), scales=h_sc[:], in_=h_bf[:].rearrange("p b n t -> p (b n t)")
             )
             if waiting is not None:
-                put_back(1, second_product(1, *waiting[:3]), waiting[3], waiting[2], "stage%d" % i)
+                put_back(1, second_product(1, *waiting[:3]), waiting[3], waiting[2], "ga%d1" % i)
             put_back(0, second_product(0, h_w, h_sc, w), j0, w, "first%d" % i)
             if i == 0:
                 quantise_w2(1)
             waiting = (h_w, h_sc, w, j0)
             j0 = j0 + w
-        finish(0, 1, nc.gpsimd)
-        finish(1, 1, nc.gpsimd)
+        finish(0, 1, nc.vector)
+        finish(1, 1, nc.vector)
         put_back(1, second_product(1, *waiting[:3]), waiting[3], waiting[2], "last")
         finish(2, 2, nc.vector)
         finish(3, 2, nc.vector)

@@ -43,7 +43,6 @@ def tile_list_sorted_poem_gates_kernel(
 
         nc.sync.dma_start(offs_sb[:], offs)
         nc.sync.dma_start(offs2_sb[:], offs2)
-        gain_sb = keep.tile([P, 2, 4], F32, name="gain_sb")
         w1_raw = keep.tile([P, 2, 2 * H], U8, name="w1_raw", tag="slot_a", align_bytes=64)
         nc.sync.dma_start(w1_raw[:].bitcast(I32), w1_words.bitcast(I32).rearrange("a p c -> p a c"))
         tab_w0 = keep.tile([P, T], I32, name="tab_w0", tag="slot_b", align_bytes=64)
@@ -60,7 +59,6 @@ def tile_list_sorted_poem_gates_kernel(
                 w1_scales.bitcast(I32)[:, 4 * q : 4 * q + 4, :].rearrange("a r c -> r a c"),
             )
 
-        nc.gpsimd.dma_start(gain_sb[:], gain.rearrange("(b p t) -> p b t", b=2, t=4))
         w1_w = keep.tile([P, 2, 2 * H], U8, name="w1_w", align_bytes=64)
         nc.vector.tensor_copy(
             w1_w[:].rearrange("p a c -> p (a c)").bitcast(U16).rearrange("p (g t h l) -> p g h t l", g=4, t=4, l=8),
@@ -103,7 +101,9 @@ def tile_list_sorted_poem_gates_kernel(
                 )
                 w2_raw[pair, b] = t
 
-        late_c = keep.tile([P, 3 * 1024], F32, name="late_c", tag="slot_c", align_bytes=64)
+        late_c = keep.tile([P, 3 * 1024 + 8], F32, name="late_c", tag="slot_c", align_bytes=64)
+        gain_sb = late_c[:, 3072:3080].rearrange("p (b t) -> p b t", b=2)
+        nc.sync.dma_start(gain_sb, gain.rearrange("(b p t) -> p b t", b=2, t=4))
         load_w2(0, late_c)
         wgo_sb = late_c[:, 2048:3072]
         nc.sync.dma_start(wgo_sb, wgo)
@@ -121,8 +121,8 @@ def tile_list_sorted_poem_gates_kernel(
         def quantise_w2(pair):
             grouped = keep.tile([P, 2, 256, 4], BF16, name="w2_bf%d" % pair, align_bytes=64)
             for b in range(2):
-                src = w2_raw[pair, b].rearrange("p t (c i) -> p c t i", i=4)
-                dst = grouped[:, b].rearrange("p (c i) t -> p c t i", i=4)
+                src = w2_raw[pair, b].rearrange("p t (c i) -> p c t i", i=2)
+                dst = grouped[:, b].rearrange("p (c i) t -> p c t i", i=2)
                 if W2_ON[pair][b] == "S":
                     nc.scalar.copy(dst, src)
                 else:
@@ -213,9 +213,9 @@ def tile_list_sorted_poem_gates_kernel(
                     nc.scalar.activation(ga[:, t, :], bank[:, cols], ACT.Copy, scale=g)
                     nc.scalar.activation(gt[:, t, :], th[:, cols], ACT.Copy, scale=g)
             nc.vector.tensor_tensor(
-                h_bf[:, b].rearrange("p (c i) t -> p c t i", i=4),
-                ga[:].rearrange("p t (c i) -> p c t i", i=4),
-                gt[:].rearrange("p t (c i) -> p c t i", i=4),
+                h_bf[:, b].rearrange("p (c i) t -> p c t i", i=2),
+                ga[:].rearrange("p t (c i) -> p c t i", i=2),
+                gt[:].rearrange("p t (c i) -> p c t i", i=2),
                 ALU.add,
             )
 
@@ -248,7 +248,7 @@ def tile_list_sorted_poem_gates_kernel(
         def finish(n, pieces, engine):
             width = S // pieces
             for c0 in range(0, S, width):
-                gate = work.tile([P, width], F32, name="gate", bufs=4)
+                gate = keep.tile([P, width], F32, name="gate", tag="gate%d%d" % (n, c0), align_bytes=64)
                 nc.scalar.activation(gate[:], pages[n][:, c0 : c0 + width], ACT.Sigmoid)
                 res = x0_sb[n][:, c0 : c0 + width]
                 engine.tensor_tensor(res, gate[:], res, ALU.mult)
@@ -278,8 +278,18 @@ def tile_list_sorted_poem_gates_kernel(
                 quantise_w2(1)
             waiting = (h_w, h_sc, w, j0)
             j0 = j0 + w
+        h_w, h_sc, w, j0 = waiting
+        bank = second_product(1, h_w, h_sc, w)
+
+        def put_back_one(m, tag):
+            y_one = keep.tile([P, w], F32, name="y_one", tag=tag, align_bytes=64)
+            nc.scalar.copy(y_one[:], bank[:, w * m : w * (m + 1)])
+            window = pages[2 + m][:].indirect(offs2_sb[:, j0 // 16 : (j0 + w) // 16])
+            nc.vector.tensor_tensor(window, y_one[:], wgo_sb[:, j0 : j0 + w], ALU.mult)
+
+        put_back_one(0, "last")
         finish(0, 1, nc.vector)
         finish(1, 1, nc.vector)
-        put_back(1, second_product(1, *waiting[:3]), waiting[3], waiting[2], "last")
+        put_back_one(1, "gate00")
         finish(2, 2, nc.vector)
         finish(3, 2, nc.vector)

@@ -18,8 +18,8 @@ ALU = mybir.AluOpType
 
 P = 128
 HALF = 512
-W2_ON = ["VV", "VV"]
-SLICES = [(256, (1, 8)), (256, (8, 8)), (256, (8, 8)), (256, (8, 8))]
+W2_ON = "VS"
+SLICES = [(256, (1, 1)), (256, (1, 8)), (256, (8, 8)), (256, (8, 8))]
 
 
 def tile_list_sorted_poem_gates_kernel(
@@ -77,7 +77,7 @@ def tile_list_sorted_poem_gates_kernel(
         v0 = keep.tile([P, S], U32, name="v0", align_bytes=64)
         v_sc0 = keep.tile([P, S], U8, name="v_sc0", align_bytes=64)
         nc.vector.tensor_copy(v_sc0[:], tab_sc[:].indirect(offs_sb[:]))
-        nc.sync.dma_start(v_sc1[0:112, :].bitcast(I32), v_sc0[16:128, :].bitcast(I32))
+        nc.scalar.dma_start(v_sc1[0:112, :].bitcast(I32), v_sc0[16:128, :].bitcast(I32))
         v_sc = [v_sc0, v_sc1]
         gather_words(0, 0, v0[:, 0:HALF])
 
@@ -91,24 +91,16 @@ def tile_list_sorted_poem_gates_kernel(
         gather_words(0, 1, v0[:, HALF:S])
         gather_words(1, 1, v1[:, HALF:S])
 
-        w2_raw = {}
-
-        def load_w2(pair, flat):
-            for b in range(2):
-                t = flat[:, 1024 * b : 1024 * (b + 1)].rearrange("p (t n) -> p t n", t=4)
-                nc.sync.dma_start(
-                    t, w2[512 * b : 512 * (b + 1), 256 * pair : 256 * (pair + 1)].rearrange("(p t) n -> p t n", t=4)
-                )
-                w2_raw[pair, b] = t
-
-        late_c = keep.tile([P, 3 * 1024 + 8], F32, name="late_c", tag="slot_c", align_bytes=64)
-        gain_sb = late_c[:, 3072:3080].rearrange("p (b t) -> p b t", b=2)
+        w2_rows = w2.rearrange("(b p t) n -> b p (t n)", b=2, t=4)
+        late_c = keep.tile([P, 2048 + 8], F32, name="late_c", tag="slot_c", align_bytes=64)
+        gain_sb = late_c[:, 2048:2056].rearrange("p (b t) -> p b t", b=2)
         nc.sync.dma_start(gain_sb, gain.rearrange("(b p t) -> p b t", b=2, t=4))
-        load_w2(0, late_c)
-        wgo_sb = late_c[:, 2048:3072]
+        nc.sync.dma_start(late_c[:, 0:2048], w2_rows[0])
+        late_b = keep.tile([P, 3 * 1024], F32, name="late_b", tag="slot_b", align_bytes=64)
+        nc.sync.dma_start(late_b[:, 0:2048], w2_rows[1])
+        wgo_sb = late_b[:, 2048:3072]
         nc.sync.dma_start(wgo_sb, wgo)
-        late_b = keep.tile([P, 2 * 1024], F32, name="late_b", tag="slot_b", align_bytes=64)
-        load_w2(1, late_b)
+        w2_raw = [late_c[:, 0:2048], late_b[:, 0:2048]]
         late_a = keep.tile([P, 4 * S], F32, name="late_a", tag="slot_a", align_bytes=64)
         x0_sb = []
         for n in range(4):
@@ -118,21 +110,22 @@ def tile_list_sorted_poem_gates_kernel(
         w2_w = {}
         w2_sc = {}
 
-        def quantise_w2(pair):
-            grouped = keep.tile([P, 2, 256, 4], BF16, name="w2_bf%d" % pair, align_bytes=64)
-            for b in range(2):
-                src = w2_raw[pair, b].rearrange("p t (c i) -> p c t i", i=2)
-                dst = grouped[:, b].rearrange("p (c i) t -> p c t i", i=2)
-                if W2_ON[pair][b] == "S":
-                    nc.scalar.copy(dst, src)
-                else:
-                    nc.vector.tensor_copy(dst, src)
-            w2_w[pair] = keep.tile([P, 512], U32, name="w2_w%d" % pair, align_bytes=64)
-            w2_sc[pair] = keep.tile([P, 512], U8, name="w2_sc%d" % pair, align_bytes=64)
+        def quantise_w2(b):
+            grouped = keep.tile([P, N, 4], BF16, name="w2_bf%d" % b, align_bytes=64)
+            src = w2_raw[b].rearrange("p (t c i) -> p c t i", t=4, i=2)
+            dst = grouped[:].rearrange("p (c i) t -> p c t i", i=2)
+            if W2_ON[b] == "S":
+                nc.scalar.copy(dst, src)
+            elif W2_ON[b] == "G":
+                nc.gpsimd.tensor_scalar(dst, src, 1.0, 0.0, ALU.mult, ALU.add)
+            else:
+                nc.vector.tensor_copy(dst, src)
+            w2_w[b] = keep.tile([P, N], U32, name="w2_w%d" % b, align_bytes=64)
+            w2_sc[b] = keep.tile([P, N], U8, name="w2_sc%d" % b, align_bytes=64)
             nc.vector.quantize_mx(
-                out=w2_w[pair][:].bitcast(FP8X4),
-                scales=w2_sc[pair][:],
-                in_=grouped[:].rearrange("p b n t -> p (b n t)"),
+                out=w2_w[b][:].bitcast(FP8X4),
+                scales=w2_sc[b][:],
+                in_=grouped[:].rearrange("p n t -> p (n t)"),
             )
 
         def first_product(bank, col, b, t, j0):
@@ -225,11 +218,11 @@ def tile_list_sorted_poem_gates_kernel(
             bank = psum_y.tile([P, 512], F32, name="y_bank")
             for m in range(2):
                 for b in range(2):
-                    c0 = 256 * b + 128 * m
+                    c0 = 256 * pair + 128 * m
                     nc.tensor.matmul_mx(
                         out=bank[:, w * m : w * (m + 1)],
-                        lhsT=w2_w[pair][:, c0 : c0 + 128].bitcast(FP8X4),
-                        lhsT_scale=w2_sc[pair][:, c0 : c0 + 128],
+                        lhsT=w2_w[b][:, c0 : c0 + 128].bitcast(FP8X4),
+                        lhsT_scale=w2_sc[b][:, c0 : c0 + 128],
                         rhs=h_w[:, w * b : w * (b + 1)].bitcast(FP8X4),
                         rhs_scale=h_sc[:, w * b : w * (b + 1)],
                         start=(b == 0),
@@ -255,6 +248,7 @@ def tile_list_sorted_poem_gates_kernel(
                 nc.sync.dma_start(out[P * n : P * (n + 1), c0 : c0 + width], res)
 
         quantise_w2(0)
+        quantise_w2(1)
         waiting = None
         j0 = 0
         for i, (w, route) in enumerate(SLICES):
@@ -274,8 +268,6 @@ def tile_list_sorted_poem_gates_kernel(
             if waiting is not None:
                 put_back(1, second_product(1, *waiting[:3]), waiting[3], waiting[2], "ga%d1" % i)
             put_back(0, second_product(0, h_w, h_sc, w), j0, w, "first%d" % i)
-            if i == 0:
-                quantise_w2(1)
             waiting = (h_w, h_sc, w, j0)
             j0 = j0 + w
         h_w, h_sc, w, j0 = waiting

@@ -17,9 +17,14 @@ ACT = mybir.ActivationFunctionType
 ALU = mybir.AluOpType
 
 P = 128
-HALF = 512
-W2_ON = "VS"
-SLICES = [(256, (1, 1)), (256, (1, 8)), (256, (8, 8)), (256, (8, 8))]
+PACK = 4
+PASS = P * PACK
+BANK = 512
+PART = 128
+GATHER = 512
+SLICE = 256
+PER_COLUMN = 16
+A_BANKS, Y_BANKS = 5, 3
 
 
 def tile_list_sorted_poem_gates_kernel(
@@ -29,13 +34,13 @@ def tile_list_sorted_poem_gates_kernel(
     with ExitStack() as ctx:
         keep = ctx.enter_context(tc.tile_pool(name="keep", bufs=1))
         work = ctx.enter_context(tc.tile_pool(name="work", bufs=2))
-        psum_a = ctx.enter_context(tc.psum_pool(name="psum_a", bufs=5))
-        psum_y = ctx.enter_context(tc.psum_pool(name="psum_y", bufs=3))
+        psum_a = ctx.enter_context(tc.psum_pool(name="psum_a", bufs=A_BANKS))
+        psum_y = ctx.enter_context(tc.psum_pool(name="psum_y", bufs=Y_BANKS))
 
-        offs_sb = keep.tile([P, S // 16], U16, name="offs_sb")
-        offs2_sb = keep.tile([P, S // 16], U16, name="offs2_sb")
-        tab_sc = keep.tile([P, T], U8, name="tab_sc", tag="slot_c", align_bytes=64)
-        w1_sc_raw = keep.tile([P, 2 * H], U8, name="w1_sc_raw", tag="slot_d", align_bytes=64)
+        offs_sb = keep.tile([P, S // PER_COLUMN], U16, name="offs_sb")
+        offs2_sb = keep.tile([P, S // PER_COLUMN], U16, name="offs2_sb")
+        tab_sc = keep.tile([P, T], U8, name="tab_sc", tag="after_tab_sc", align_bytes=64)
+        w1_sc_raw = keep.tile([P, 2 * H], U8, name="w1_sc_raw", tag="after_w1_sc_raw", align_bytes=64)
         v_sc1 = keep.tile([P, S], U8, name="v_sc1", align_bytes=64)
         nc.vector.memset(tab_sc[:].bitcast(I32), 0)
         nc.vector.memset(w1_sc_raw[:].bitcast(I32), 0)
@@ -43,14 +48,14 @@ def tile_list_sorted_poem_gates_kernel(
 
         nc.sync.dma_start(offs_sb[:], offs)
         nc.sync.dma_start(offs2_sb[:], offs2)
-        w1_raw = keep.tile([P, 2, 2 * H], U8, name="w1_raw", tag="slot_a", align_bytes=64)
+        w1_raw = keep.tile([P, 2, 2 * H], U8, name="w1_raw", tag="after_w1_raw", align_bytes=64)
         nc.sync.dma_start(w1_raw[:].bitcast(I32), w1_words.bitcast(I32).rearrange("a p c -> p a c"))
-        tab_w0 = keep.tile([P, T], I32, name="tab_w0", tag="slot_b", align_bytes=64)
+        tab_w0 = keep.tile([P, T], I32, name="tab_w0", tag="after_tab_w0", align_bytes=64)
         nc.sync.dma_start(tab_w0[:], tab_words[0].rearrange("p t i -> p (t i)").bitcast(I32))
-        for r in range(4):
+        for s in range(4):
             nc.scalar.dma_start(
-                tab_sc[r:128:16, :].bitcast(I32),
-                tab_scales.bitcast(I32)[:, r:16:4, :].rearrange("a q t -> q a t"),
+                tab_sc[s:128:16, :].bitcast(I32),
+                tab_scales.bitcast(I32)[:, s:16:4, :].rearrange("a q t -> q a t"),
             )
         for q in range(4):
             queue = nc.gpsimd if q < 2 else nc.scalar
@@ -64,224 +69,175 @@ def tile_list_sorted_poem_gates_kernel(
             w1_w[:].rearrange("p a c -> p (a c)").bitcast(U16).rearrange("p (g t h l) -> p g h t l", g=4, t=4, l=8),
             w1_raw[:].rearrange("p a c -> p (a c)").bitcast(U16).rearrange("p (g h l t) -> p g h t l", g=4, t=4, l=8),
         )
-        tab_w1 = keep.tile([P, T], I32, name="tab_w1", tag="slot_a", align_bytes=64)
+        tab_w1 = keep.tile([P, T], I32, name="tab_w1", tag="after_w1_raw", align_bytes=64)
         nc.sync.dma_start(tab_w1[:], tab_words[1].rearrange("p t i -> p (t i)").bitcast(I32))
-        tab_w = [tab_w0, tab_w1]
 
-        v_w = {}
+        def gather_words(dst, window, j0):
+            entries = offs_sb[:, j0 // PER_COLUMN : (j0 + GATHER) // PER_COLUMN]
+            nc.vector.tensor_copy(dst[:, j0 : j0 + GATHER], window[:].bitcast(U32).indirect(entries))
 
-        def gather_words(a, half, dst):
-            nc.vector.tensor_copy(dst, tab_w[a][:].bitcast(U32).indirect(offs_sb[:, 32 * half : 32 * (half + 1)]))
-            v_w[a, half] = dst
-
-        v0 = keep.tile([P, S], U32, name="v0", align_bytes=64)
+        v_w0 = keep.tile([P, S], U32, name="v_w0", align_bytes=64)
         v_sc0 = keep.tile([P, S], U8, name="v_sc0", align_bytes=64)
         nc.vector.tensor_copy(v_sc0[:], tab_sc[:].indirect(offs_sb[:]))
         nc.scalar.dma_start(v_sc1[0:112, :].bitcast(I32), v_sc0[16:128, :].bitcast(I32))
-        v_sc = [v_sc0, v_sc1]
-        gather_words(0, 0, v0[:, 0:HALF])
+        gather_words(v_w0, tab_w0, 0)
 
         w1_sc = keep.tile([P, 2 * H], U8, name="w1_sc", align_bytes=64)
         nc.vector.tensor_copy(
             w1_sc[:].rearrange("p (g t h l) -> p g h t l", g=4, t=4, l=16),
             w1_sc_raw[:].rearrange("p (g h l t) -> p g h t l", g=4, t=4, l=16),
         )
-        v1 = keep.tile([P, S], U32, name="v1", tag="slot_d", align_bytes=64)
-        gather_words(1, 0, v1[:, 0:HALF])
-        gather_words(0, 1, v0[:, HALF:S])
-        gather_words(1, 1, v1[:, HALF:S])
+        v_w1 = keep.tile([P, S], U32, name="v_w1", tag="after_w1_sc_raw", align_bytes=64)
+        gather_words(v_w1, tab_w1, 0)
+        gather_words(v_w0, tab_w0, GATHER)
+        gather_words(v_w1, tab_w1, GATHER)
+        v_w = [v_w0, v_w1]
+        v_sc = [v_sc0, v_sc1]
 
-        w2_rows = w2.rearrange("(b p t) n -> b p (t n)", b=2, t=4)
-        late_c = keep.tile([P, 2048 + 8], F32, name="late_c", tag="slot_c", align_bytes=64)
-        gain_sb = late_c[:, 2048:2056].rearrange("p (b t) -> p b t", b=2)
-        nc.sync.dma_start(gain_sb, gain.rearrange("(b p t) -> p b t", b=2, t=4))
-        nc.sync.dma_start(late_c[:, 0:2048], w2_rows[0])
-        late_b = keep.tile([P, 3 * 1024], F32, name="late_b", tag="slot_b", align_bytes=64)
-        nc.sync.dma_start(late_b[:, 0:2048], w2_rows[1])
-        wgo_sb = late_b[:, 2048:3072]
+        w2_rows = w2.rearrange("(b p t) n -> b p (t n)", b=2, t=PACK)
+        w2_width = PACK * N
+        w2_0_and_gain = keep.tile([P, w2_width + 8], F32, name="w2_0_and_gain", tag="after_tab_sc", align_bytes=64)
+        gain_sb = w2_0_and_gain[:, w2_width : w2_width + 8].rearrange("p (b t) -> p b t", b=2)
+        nc.sync.dma_start(gain_sb, gain.rearrange("(b p t) -> p b t", b=2, t=PACK))
+        nc.sync.dma_start(w2_0_and_gain[:, 0:w2_width], w2_rows[0])
+        w2_1_and_wgo = keep.tile([P, w2_width + S], F32, name="w2_1_and_wgo", tag="after_tab_w0", align_bytes=64)
+        nc.sync.dma_start(w2_1_and_wgo[:, 0:w2_width], w2_rows[1])
+        wgo_sb = w2_1_and_wgo[:, w2_width : w2_width + S]
         nc.sync.dma_start(wgo_sb, wgo)
-        w2_raw = [late_c[:, 0:2048], late_b[:, 0:2048]]
-        late_a = keep.tile([P, 4 * S], F32, name="late_a", tag="slot_a", align_bytes=64)
-        x0_sb = []
+        w2_raw = [w2_0_and_gain[:, 0:w2_width], w2_1_and_wgo[:, 0:w2_width]]
+        x0_all = keep.tile([P, 4 * S], F32, name="x0_all", tag="after_w1_raw", align_bytes=64)
+        x0_sb = [x0_all[:, S * n : S * (n + 1)] for n in range(4)]
         for n in range(4):
-            nc.sync.dma_start(late_a[:, S * n : S * (n + 1)], x0[P * n : P * (n + 1), :])
-            x0_sb.append(late_a[:, S * n : S * (n + 1)])
-
-        w2_w = {}
-        w2_sc = {}
+            nc.sync.dma_start(x0_sb[n], x0[P * n : P * (n + 1), :])
 
         def quantise_w2(b):
-            grouped = keep.tile([P, N, 4], BF16, name="w2_bf%d" % b, align_bytes=64)
-            src = w2_raw[b].rearrange("p (t c i) -> p c t i", t=4, i=2)
-            dst = grouped[:].rearrange("p (c i) t -> p c t i", i=2)
-            if W2_ON[b] == "S":
-                nc.scalar.copy(dst, src)
-            elif W2_ON[b] == "G":
-                nc.gpsimd.tensor_scalar(dst, src, 1.0, 0.0, ALU.mult, ALU.add)
-            else:
-                nc.vector.tensor_copy(dst, src)
-            w2_w[b] = keep.tile([P, N], U32, name="w2_w%d" % b, align_bytes=64)
-            w2_sc[b] = keep.tile([P, N], U8, name="w2_sc%d" % b, align_bytes=64)
-            nc.vector.quantize_mx(
-                out=w2_w[b][:].bitcast(FP8X4),
-                scales=w2_sc[b][:],
-                in_=grouped[:].rearrange("p n t -> p (n t)"),
+            woven = keep.tile([P, N, PACK], BF16, name="w2_bf%d" % b, align_bytes=64)
+            nc.vector.tensor_copy(
+                woven[:].rearrange("p (c i) t -> p c t i", i=2),
+                w2_raw[b].rearrange("p (t c i) -> p c t i", t=PACK, i=2),
             )
+            words = keep.tile([P, N], U32, name="w2_w%d" % b, align_bytes=64)
+            scales = keep.tile([P, N], U8, name="w2_sc%d" % b, align_bytes=64)
+            nc.vector.quantize_mx(
+                out=words[:].bitcast(FP8X4), scales=scales[:], in_=woven[:].rearrange("p n t -> p (n t)")
+            )
+            return words, scales
 
-        def first_product(bank, col, b, t, j0):
-            half, jj = divmod(j0, HALF)
+        def first_product(b, parts):
+            bank = psum_a.tile([P, BANK], F32, name="a_bank")
             for a in range(2):
-                c0 = 512 * b + 128 * t
-                nc.tensor.matmul_mx(
-                    out=bank[:, col : col + 128],
-                    lhsT=w1_w[:, a, 2 * c0 : 2 * c0 + 256].bitcast(FP4X4),
-                    lhsT_scale=w1_sc[:, H * a + c0 : H * a + c0 + 128],
-                    rhs=v_w[a, half][:, jj : jj + 128].bitcast(FP8X4),
-                    rhs_scale=v_sc[a][:, j0 : j0 + 128],
-                    start=(a == 0),
-                    stop=(a == 1),
-                )
+                for place, (t, j) in enumerate(parts):
+                    c0 = PASS * b + P * t
+                    nc.tensor.matmul_mx(
+                        out=bank[:, PART * place : PART * (place + 1)],
+                        lhsT=w1_w[:, a, 2 * c0 : 2 * (c0 + P)].bitcast(FP4X4),
+                        lhsT_scale=w1_sc[:, H * a + c0 : H * a + c0 + P],
+                        rhs=v_w[a][:, j : j + PART].bitcast(FP8X4),
+                        rhs_scale=v_sc[a][:, j : j + PART],
+                        start=(a == 0 and place == 0),
+                        stop=(a == 1 and place == len(parts) - 1),
+                    )
+            return bank
 
-        def h_units(h_bf, j0, w, route, bs):
-            for u in range(w // 128):
-                for b in bs:
-                    bank = psum_a.tile([P, 512], F32, name="a_bank")
-                    for t in range(4):
-                        first_product(bank, 128 * t, b, t, j0 + 128 * u)
-                    woven = bank[:].rearrange("p (t n) -> p n t", t=4)
-                    th = work.tile([P, 128, 4], F32, name="th", bufs=3)
-                    nc.scalar.activation(th[:], woven, ACT.Tanh)
-                    total = work.tile([P, 128, 4], F32, name="total", bufs=2)
-                    g = gain_sb[:, b, :].unsqueeze(1).to_broadcast([P, 128, 4])
-                    dst = h_bf[:, b, 128 * u : 128 * (u + 1), :]
-                    if route == 1:
-                        nc.vector.tensor_tensor(total[:], woven, th[:], ALU.add)
-                        nc.vector.tensor_tensor(dst, total[:], g, ALU.mult)
-                    elif route == 2:
-                        nc.vector.tensor_tensor(total[:], woven, th[:], ALU.add)
-                        nc.gpsimd.tensor_tensor(dst, total[:], g, ALU.mult)
-                    else:
-                        ac = work.tile([P, 128, 4], F32, name="ac", bufs=3)
-                        nc.scalar.copy(ac[:], woven)
-                        nc.gpsimd.tensor_tensor(total[:], ac[:], th[:], ALU.add)
-                        nc.gpsimd.tensor_tensor(dst, total[:], g, ALU.mult)
-
-        def h_slots(h_bf, j0, w, route, b):
-            per_bank = 512 // w
-            total = work.tile([P, 4, w], F32, name="total6", bufs=3)
-            hn = work.tile([P, 4, w], BF16, name="hn", bufs=3)
-            for t0 in range(0, 4, per_bank):
-                bank = psum_a.tile([P, 512], F32, name="a_bank")
-                for t in range(t0, t0 + per_bank):
-                    for u in range(w // 128):
-                        first_product(bank, w * (t - t0) + 128 * u, b, t, j0 + 128 * u)
-                th = work.tile([P, 512], F32, name="th6", bufs=4)
-                nc.scalar.activation(th[:], bank[:], ACT.Tanh)
+        def h_mostly_on_vector(h_bf, j0, b):
+            for u in range(SLICE // PART):
+                bank = first_product(b, [(t, j0 + PART * u) for t in range(PACK)])
+                a_woven = bank[:].rearrange("p (t n) -> p n t", t=PACK)
+                tanh_woven = work.tile([P, PART, PACK], F32, name="tanh_woven", bufs=3)
+                nc.scalar.activation(tanh_woven[:], a_woven, ACT.Tanh)
+                total = work.tile([P, PART, PACK], F32, name="total", bufs=2)
+                nc.vector.tensor_tensor(total[:], a_woven, tanh_woven[:], ALU.add)
                 nc.vector.tensor_tensor(
-                    total[:, t0 : t0 + per_bank, :].rearrange("p t n -> p (t n)"), bank[:], th[:], ALU.add
+                    h_bf[:, b, PART * u : PART * (u + 1), :],
+                    total[:],
+                    gain_sb[:, b, :].unsqueeze(1).to_broadcast([P, PART, PACK]),
+                    ALU.mult,
                 )
-                for t in range(t0, t0 + per_bank):
-                    nc.scalar.activation(hn[:, t, :], total[:, t, :], ACT.Copy, scale=gain_sb[:, b, t : t + 1])
-            dst = h_bf[:, b].rearrange("p (c i) t -> p c t i", i=4)
-            src = hn[:].rearrange("p t (c i) -> p c t i", i=4)
-            if route == 6:
-                nc.scalar.copy(dst, src)
-            else:
-                nc.vector.tensor_copy(dst, src)
 
-        def h_scaled(h_bf, j0, w, b, i):
-            per_bank = 512 // w
-            ga = keep.tile([P, 4, w], F32, name="ga3", tag="ga%d%d" % (i, b), align_bytes=64)
-            gt = work.tile([P, 4, w], F32, name="gt3", bufs=3)
-            for t0 in range(0, 4, per_bank):
-                bank = psum_a.tile([P, 512], F32, name="a_bank")
-                for t in range(t0, t0 + per_bank):
-                    for u in range(w // 128):
-                        first_product(bank, w * (t - t0) + 128 * u, b, t, j0 + 128 * u)
-                th = work.tile([P, 512], F32, name="th6", bufs=4)
-                nc.scalar.activation(th[:], bank[:], ACT.Tanh)
-                for t in range(t0, t0 + per_bank):
+        def h_mostly_on_scalar(h_bf, j0, b, tag):
+            gain_a = keep.tile([P, PACK, SLICE], F32, name="gain_a", tag=tag, align_bytes=64)
+            gain_tanh = work.tile([P, PACK, SLICE], F32, name="gain_tanh", bufs=3)
+            per_bank = BANK // SLICE
+            for t0 in range(0, PACK, per_bank):
+                ts = range(t0, t0 + per_bank)
+                bank = first_product(b, [(t, j) for t in ts for j in range(j0, j0 + SLICE, PART)])
+                tanh_a = work.tile([P, BANK], F32, name="tanh_a", bufs=4)
+                nc.scalar.activation(tanh_a[:], bank[:], ACT.Tanh)
+                for t in ts:
                     g = gain_sb[:, b, t : t + 1]
-                    cols = slice(w * (t - t0), w * (t - t0 + 1))
-                    nc.scalar.activation(ga[:, t, :], bank[:, cols], ACT.Copy, scale=g)
-                    nc.scalar.activation(gt[:, t, :], th[:, cols], ACT.Copy, scale=g)
+                    cols = slice(SLICE * (t - t0), SLICE * (t - t0 + 1))
+                    nc.scalar.activation(gain_a[:, t, :], bank[:, cols], ACT.Copy, scale=g)
+                    nc.scalar.activation(gain_tanh[:, t, :], tanh_a[:, cols], ACT.Copy, scale=g)
             nc.vector.tensor_tensor(
                 h_bf[:, b].rearrange("p (c i) t -> p c t i", i=2),
-                ga[:].rearrange("p t (c i) -> p c t i", i=2),
-                gt[:].rearrange("p t (c i) -> p c t i", i=2),
+                gain_a[:].rearrange("p t (c i) -> p c t i", i=2),
+                gain_tanh[:].rearrange("p t (c i) -> p c t i", i=2),
                 ALU.add,
             )
 
         pages = [keep.tile([P, S], F32, name="page%d" % n) for n in range(4)]
 
-        def second_product(pair, h_w, h_sc, w):
-            bank = psum_y.tile([P, 512], F32, name="y_bank")
+        def second_product(pair, h_w, h_sc):
+            bank = psum_y.tile([P, BANK], F32, name="y_bank")
             for m in range(2):
+                c0 = P * (2 * pair + m)
                 for b in range(2):
-                    c0 = 256 * pair + 128 * m
                     nc.tensor.matmul_mx(
-                        out=bank[:, w * m : w * (m + 1)],
-                        lhsT=w2_w[b][:, c0 : c0 + 128].bitcast(FP8X4),
-                        lhsT_scale=w2_sc[b][:, c0 : c0 + 128],
-                        rhs=h_w[:, w * b : w * (b + 1)].bitcast(FP8X4),
-                        rhs_scale=h_sc[:, w * b : w * (b + 1)],
+                        out=bank[:, SLICE * m : SLICE * (m + 1)],
+                        lhsT=w2_q[b][0][:, c0 : c0 + P].bitcast(FP8X4),
+                        lhsT_scale=w2_q[b][1][:, c0 : c0 + P],
+                        rhs=h_w[:, SLICE * b : SLICE * (b + 1)].bitcast(FP8X4),
+                        rhs_scale=h_sc[:, SLICE * b : SLICE * (b + 1)],
                         start=(b == 0),
                         stop=(b == 1),
                     )
             return bank
 
-        def put_back(pair, bank, j0, w, tag):
-            y_sb = keep.tile([P, 2, w], F32, name="y_sb", tag=tag, align_bytes=64)
-            y_ps = bank[:, 0 : 2 * w].rearrange("p (m j) -> p m j", m=2)
-            nc.scalar.copy(y_sb[:], y_ps)
-            for m in range(2):
-                window = pages[2 * pair + m][:].indirect(offs2_sb[:, j0 // 16 : (j0 + w) // 16])
-                nc.vector.tensor_tensor(window, y_sb[:, m, :], wgo_sb[:, j0 : j0 + w], ALU.mult)
+        def put_back(first_page, y_psum, j0, tag):
+            count = y_psum.shape[1] // SLICE
+            y_sb = keep.tile([P, count * SLICE], F32, name="y_sb", tag=tag, align_bytes=64)
+            nc.scalar.copy(y_sb[:], y_psum)
+            entries = offs2_sb[:, j0 // PER_COLUMN : (j0 + SLICE) // PER_COLUMN]
+            for m in range(count):
+                nc.vector.tensor_tensor(
+                    pages[first_page + m][:].indirect(entries),
+                    y_sb[:, SLICE * m : SLICE * (m + 1)],
+                    wgo_sb[:, j0 : j0 + SLICE],
+                    ALU.mult,
+                )
 
-        def finish(n, pieces, engine):
+        def finish(n, pieces):
             width = S // pieces
             for c0 in range(0, S, width):
-                gate = keep.tile([P, width], F32, name="gate", tag="gate%d%d" % (n, c0), align_bytes=64)
+                gate = keep.tile([P, width], F32, name="gate", tag="gate%d_%d" % (n, c0), align_bytes=64)
                 nc.scalar.activation(gate[:], pages[n][:, c0 : c0 + width], ACT.Sigmoid)
-                res = x0_sb[n][:, c0 : c0 + width]
-                engine.tensor_tensor(res, gate[:], res, ALU.mult)
-                nc.sync.dma_start(out[P * n : P * (n + 1), c0 : c0 + width], res)
+                result = x0_sb[n][:, c0 : c0 + width]
+                nc.vector.tensor_tensor(result, gate[:], result, ALU.mult)
+                nc.sync.dma_start(out[P * n : P * (n + 1), c0 : c0 + width], result)
 
-        quantise_w2(0)
-        quantise_w2(1)
-        waiting = None
-        j0 = 0
-        for i, (w, route) in enumerate(SLICES):
-            h_bf = keep.tile([P, 2, w, 4], BF16, name="h_bf", tag="stage%d" % i, align_bytes=64)
+        w2_q = [quantise_w2(b) for b in range(2)]
+        previous = None
+        for j0 in range(0, S, SLICE):
+            h_bf = keep.tile([P, 2, SLICE, PACK], BF16, name="h_bf%d" % j0, align_bytes=64)
             for b in range(2):
-                if route[b] == 8:
-                    h_scaled(h_bf, j0, w, b, i)
-                elif route[b] >= 6:
-                    h_slots(h_bf, j0, w, route[b], b)
+                if j0 == 0 and b == 0:
+                    h_mostly_on_vector(h_bf, j0, b)
                 else:
-                    h_units(h_bf, j0, w, route[b], [b])
-            h_w = keep.tile([P, 2 * w], U32, name="h_w%d" % i, align_bytes=64)
-            h_sc = keep.tile([P, 2 * w], U8, name="h_sc%d" % i, align_bytes=64)
+                    h_mostly_on_scalar(h_bf, j0, b, "gain_a%d_%d" % (j0, b))
+            h_w = keep.tile([P, 2 * SLICE], U32, name="h_w%d" % j0, align_bytes=64)
+            h_sc = keep.tile([P, 2 * SLICE], U8, name="h_sc%d" % j0, align_bytes=64)
             nc.vector.quantize_mx(
                 out=h_w[:].bitcast(FP8X4), scales=h_sc[:], in_=h_bf[:].rearrange("p b n t -> p (b n t)")
             )
-            if waiting is not None:
-                put_back(1, second_product(1, *waiting[:3]), waiting[3], waiting[2], "ga%d1" % i)
-            put_back(0, second_product(0, h_w, h_sc, w), j0, w, "first%d" % i)
-            waiting = (h_w, h_sc, w, j0)
-            j0 = j0 + w
-        h_w, h_sc, w, j0 = waiting
-        bank = second_product(1, h_w, h_sc, w)
+            if previous is not None:
+                put_back(2, second_product(1, *previous)[:], j0 - SLICE, "gain_a%d_1" % j0)
+            put_back(0, second_product(0, h_w, h_sc)[:], j0, "y_first%d" % j0)
+            previous = (h_w, h_sc)
 
-        def put_back_one(m, tag):
-            y_one = keep.tile([P, w], F32, name="y_one", tag=tag, align_bytes=64)
-            nc.scalar.copy(y_one[:], bank[:, w * m : w * (m + 1)])
-            window = pages[2 + m][:].indirect(offs2_sb[:, j0 // 16 : (j0 + w) // 16])
-            nc.vector.tensor_tensor(window, y_one[:], wgo_sb[:, j0 : j0 + w], ALU.mult)
-
-        put_back_one(0, "last")
-        finish(0, 1, nc.vector)
-        finish(1, 1, nc.vector)
-        put_back_one(1, "gate00")
-        finish(2, 2, nc.vector)
-        finish(3, 2, nc.vector)
+        last = second_product(1, *previous)
+        put_back(2, last[:, 0:SLICE], S - SLICE, "y_last")
+        finish(0, 1)
+        finish(1, 1)
+        put_back(3, last[:, SLICE : 2 * SLICE], S - SLICE, "gate0_0")
+        finish(2, 2)
+        finish(3, 2)

@@ -199,12 +199,11 @@ def tile_list_sorted_poem_gates_kernel(
             nc.scalar.copy(y_sb[:], y_psum)
             entries = offs2_sb[:, j0 // PER_COLUMN : (j0 + SLICE) // PER_COLUMN]
             for m in range(count):
-                nc.vector.tensor_tensor(
-                    pages[first_page + m][:].indirect(entries),
-                    y_sb[:, SLICE * m : SLICE * (m + 1)],
-                    wgo_sb[:, j0 : j0 + SLICE],
-                    ALU.mult,
+                weighted = work.tile([P, SLICE], F32, name="weighted", bufs=4)
+                nc.gpsimd.tensor_tensor(
+                    weighted[:], y_sb[:, SLICE * m : SLICE * (m + 1)], wgo_sb[:, j0 : j0 + SLICE], ALU.mult
                 )
+                nc.vector.tensor_copy(pages[first_page + m][:].indirect(entries), weighted[:])
 
         def finish(n, pieces):
             width = S // pieces

@@ -22,7 +22,8 @@ PASS = P * PACK
 BANK = 512
 PART = 128
 GATHER = 512
-SLICE = 256
+SLICES = (128, 128, 256, 256, 256)
+HALF = N // 2
 PER_COLUMN = 16
 A_BANKS, Y_BANKS = 5, 3
 
@@ -94,30 +95,30 @@ def tile_list_sorted_poem_gates_kernel(
         v_w = [v_w0, v_w1]
         v_sc = [v_sc0, v_sc1]
 
-        w2_rows = w2.rearrange("(b p t) n -> b p (t n)", b=2, t=PACK)
-        w2_width = PACK * N
-        w2_0_and_gain = keep.tile([P, w2_width + 8], F32, name="w2_0_and_gain", tag="after_tab_sc", align_bytes=64)
-        gain_sb = w2_0_and_gain[:, w2_width : w2_width + 8].rearrange("p (b t) -> p b t", b=2)
+        w2_rows = w2.rearrange("(b p t) (half n) -> half b p t n", b=2, t=PACK, half=2)
+        w2_width = PACK * HALF
+        early = keep.tile([P, 2 * w2_width + 8], F32, name="early", tag="after_tab_sc", align_bytes=64)
+        late = keep.tile([P, 2 * w2_width + S], F32, name="late", tag="after_tab_w0", align_bytes=64)
+        gain_sb = early[:, 2 * w2_width : 2 * w2_width + 8].rearrange("p (b t) -> p b t", b=2)
         nc.sync.dma_start(gain_sb, gain.rearrange("(b p t) -> p b t", b=2, t=PACK))
-        nc.sync.dma_start(w2_0_and_gain[:, 0:w2_width], w2_rows[0])
-        w2_1_and_wgo = keep.tile([P, w2_width + S], F32, name="w2_1_and_wgo", tag="after_tab_w0", align_bytes=64)
-        nc.sync.dma_start(w2_1_and_wgo[:, 0:w2_width], w2_rows[1])
-        wgo_sb = w2_1_and_wgo[:, w2_width : w2_width + S]
+        w2_raw = [[tile[:, w2_width * b : w2_width * (b + 1)] for b in range(2)] for tile in (early, late)]
+        for half in range(2):
+            for b in range(2):
+                nc.sync.dma_start(w2_raw[half][b].rearrange("p (t n) -> p t n", t=PACK), w2_rows[half, b])
+        wgo_sb = late[:, 2 * w2_width : 2 * w2_width + S]
         nc.sync.dma_start(wgo_sb, wgo)
-        w2_raw = [w2_0_and_gain[:, 0:w2_width], w2_1_and_wgo[:, 0:w2_width]]
         x0_all = keep.tile([P, 4 * S], F32, name="x0_all", tag="after_w1_raw", align_bytes=64)
         x0_sb = [x0_all[:, S * n : S * (n + 1)] for n in range(4)]
         for n in range(4):
             nc.sync.dma_start(x0_sb[n], x0[P * n : P * (n + 1), :])
 
-        def quantise_w2(b):
-            woven = keep.tile([P, N, PACK], BF16, name="w2_bf%d" % b, align_bytes=64)
-            nc.vector.tensor_copy(
-                woven[:].rearrange("p (c i) t -> p c t i", i=2),
-                w2_raw[b].rearrange("p (t c i) -> p c t i", t=PACK, i=2),
-            )
-            words = keep.tile([P, N], U32, name="w2_w%d" % b, align_bytes=64)
-            scales = keep.tile([P, N], U8, name="w2_sc%d" % b, align_bytes=64)
+        def quantise_w2(half, b):
+            woven = keep.tile([P, HALF, PACK], BF16, name="w2_bf%d%d" % (half, b), align_bytes=64)
+            woven_view = woven[:].rearrange("p (c i) t -> p c t i", i=4)
+            raw_view = w2_raw[half][b].rearrange("p (t c i) -> p c t i", t=PACK, i=4)
+            nc.vector.tensor_copy(woven_view, raw_view)
+            words = keep.tile([P, HALF], U32, name="w2_w%d%d" % (half, b), align_bytes=64)
+            scales = keep.tile([P, HALF], U8, name="w2_sc%d%d" % (half, b), align_bytes=64)
             nc.vector.quantize_mx(
                 out=words[:].bitcast(FP8X4), scales=scales[:], in_=woven[:].rearrange("p n t -> p (n t)")
             )
@@ -139,104 +140,110 @@ def tile_list_sorted_poem_gates_kernel(
                     )
             return bank
 
-        def h_mostly_on_vector(h_bf, j0, b):
-            for u in range(SLICE // PART):
-                bank = first_product(b, [(t, j0 + PART * u) for t in range(PACK)])
-                a_woven = bank[:].rearrange("p (t n) -> p n t", t=PACK)
-                tanh_woven = work.tile([P, PART, PACK], F32, name="tanh_woven", bufs=3)
-                nc.scalar.activation(tanh_woven[:], a_woven, ACT.Tanh)
-                total = work.tile([P, PART, PACK], F32, name="total", bufs=2)
-                nc.vector.tensor_tensor(total[:], a_woven, tanh_woven[:], ALU.add)
-                nc.vector.tensor_tensor(
-                    h_bf[:, b, PART * u : PART * (u + 1), :],
-                    total[:],
-                    gain_sb[:, b, :].unsqueeze(1).to_broadcast([P, PART, PACK]),
-                    ALU.mult,
-                )
+        def make_h_on_vector(h_bf, j0, b):
+            bank = first_product(b, [(t, j0) for t in range(PACK)])
+            a_woven = bank[:].rearrange("p (t n) -> p n t", t=PACK)
+            tanh_woven = work.tile([P, PART, PACK], F32, name="tanh_woven", bufs=2)
+            nc.scalar.activation(tanh_woven[:], a_woven, ACT.Tanh)
+            total = work.tile([P, PART, PACK], F32, name="total", bufs=2)
+            nc.vector.tensor_tensor(total[:], a_woven, tanh_woven[:], ALU.add)
+            nc.vector.tensor_tensor(
+                h_bf[:, b], total[:], gain_sb[:, b, :].unsqueeze(1).to_broadcast([P, PART, PACK]), ALU.mult
+            )
 
-        def h_mostly_on_scalar(h_bf, j0, b, tag):
-            gain_a = keep.tile([P, PACK, SLICE], F32, name="gain_a", tag=tag, align_bytes=64)
-            gain_tanh = work.tile([P, PACK, SLICE], F32, name="gain_tanh", bufs=3)
-            per_bank = BANK // SLICE
+        def make_h(h_bf, j0, width, b, adder):
+            gain_a = keep.tile([P, PACK, width], F32, name="gain_a", tag="gain_a%d_%d" % (j0, b))
+            gain_tanh = work.tile([P, PACK, width], F32, name="gain_tanh", bufs=4)
+            per_bank = BANK // width
             for t0 in range(0, PACK, per_bank):
                 ts = range(t0, t0 + per_bank)
-                bank = first_product(b, [(t, j) for t in ts for j in range(j0, j0 + SLICE, PART)])
+                bank = first_product(b, [(t, j) for t in ts for j in range(j0, j0 + width, PART)])
                 tanh_a = work.tile([P, BANK], F32, name="tanh_a", bufs=4)
                 nc.scalar.activation(tanh_a[:], bank[:], ACT.Tanh)
                 for t in ts:
-                    g = gain_sb[:, b, t : t + 1]
-                    cols = slice(SLICE * (t - t0), SLICE * (t - t0 + 1))
-                    nc.scalar.activation(gain_a[:, t, :], bank[:, cols], ACT.Copy, scale=g)
-                    nc.scalar.activation(gain_tanh[:, t, :], tanh_a[:, cols], ACT.Copy, scale=g)
-            nc.vector.tensor_tensor(
-                h_bf[:, b].rearrange("p (c i) t -> p c t i", i=2),
-                gain_a[:].rearrange("p t (c i) -> p c t i", i=2),
-                gain_tanh[:].rearrange("p t (c i) -> p c t i", i=2),
+                    cols = slice(width * (t - t0), width * (t - t0 + 1))
+                    nc.scalar.activation(gain_a[:, t, :], bank[:, cols], ACT.Copy, scale=gain_sb[:, b, t : t + 1])
+                for t in ts:
+                    cols = slice(width * (t - t0), width * (t - t0 + 1))
+                    nc.scalar.activation(gain_tanh[:, t, :], tanh_a[:, cols], ACT.Copy, scale=gain_sb[:, b, t : t + 1])
+            adder.tensor_tensor(
+                h_bf[:, b].rearrange("p (c i) t -> p c t i", i=4),
+                gain_a[:].rearrange("p t (c i) -> p c t i", i=4),
+                gain_tanh[:].rearrange("p t (c i) -> p c t i", i=4),
                 ALU.add,
             )
 
         pages = [keep.tile([P, S], F32, name="page%d" % n) for n in range(4)]
 
-        def second_product(pair, h_w, h_sc):
-            bank = psum_y.tile([P, BANK], F32, name="y_bank")
+        def second_product(pair, width, h_w, h_sc):
+            bank = psum_y.tile([P, 2, width], F32, name="y_bank")
             for m in range(2):
-                c0 = P * (2 * pair + m)
+                c0 = P * m
                 for b in range(2):
                     nc.tensor.matmul_mx(
-                        out=bank[:, SLICE * m : SLICE * (m + 1)],
-                        lhsT=w2_q[b][0][:, c0 : c0 + P].bitcast(FP8X4),
-                        lhsT_scale=w2_q[b][1][:, c0 : c0 + P],
-                        rhs=h_w[:, SLICE * b : SLICE * (b + 1)].bitcast(FP8X4),
-                        rhs_scale=h_sc[:, SLICE * b : SLICE * (b + 1)],
+                        out=bank[:, m, :],
+                        lhsT=w2_q[pair][b][0][:, c0 : c0 + P].bitcast(FP8X4),
+                        lhsT_scale=w2_q[pair][b][1][:, c0 : c0 + P],
+                        rhs=h_w[:, b, :].bitcast(FP8X4),
+                        rhs_scale=h_sc[:, b, :],
                         start=(b == 0),
                         stop=(b == 1),
                     )
             return bank
 
-        def put_back(first_page, y_psum, j0, tag):
-            count = y_psum.shape[1] // SLICE
-            y_sb = keep.tile([P, count * SLICE], F32, name="y_sb", tag=tag, align_bytes=64)
-            nc.scalar.copy(y_sb[:], y_psum)
-            entries = offs2_sb[:, j0 // PER_COLUMN : (j0 + SLICE) // PER_COLUMN]
-            for m in range(count):
-                weighted = work.tile([P, SLICE], F32, name="weighted", bufs=4)
-                nc.gpsimd.tensor_tensor(
-                    weighted[:], y_sb[:, SLICE * m : SLICE * (m + 1)], wgo_sb[:, j0 : j0 + SLICE], ALU.mult
-                )
-                nc.vector.tensor_copy(pages[first_page + m][:].indirect(entries), weighted[:])
+        def weigh(y_psum, j0, width, tag):
+            count = y_psum.shape[1]
+            weighted = keep.tile([P, count, width], F32, name="weighted", tag=tag)
+            nc.vector.tensor_tensor(
+                weighted[:], y_psum, wgo_sb[:, j0 : j0 + width].unsqueeze(1).to_broadcast([P, count, width]), ALU.mult
+            )
+            return weighted
 
-        def finish(n, pieces):
+        def put_back(first_page, weighted, j0, width):
+            entries = offs2_sb[:, j0 // PER_COLUMN : (j0 + width) // PER_COLUMN]
+            for m in range(weighted.shape[1]):
+                nc.vector.tensor_copy(pages[first_page + m][:].indirect(entries), weighted[:, m, :])
+
+        def finish(n, pieces, engine):
             width = S // pieces
             for c0 in range(0, S, width):
                 gate = keep.tile([P, width], F32, name="gate", tag="gate%d_%d" % (n, c0), align_bytes=64)
                 nc.scalar.activation(gate[:], pages[n][:, c0 : c0 + width], ACT.Sigmoid)
                 result = x0_sb[n][:, c0 : c0 + width]
-                nc.vector.tensor_tensor(result, gate[:], result, ALU.mult)
+                engine.tensor_tensor(result, gate[:], result, ALU.mult)
                 nc.sync.dma_start(out[P * n : P * (n + 1), c0 : c0 + width], result)
 
-        w2_q = [quantise_w2(b) for b in range(2)]
-        previous = None
-        for j0 in range(0, S, SLICE):
-            h_bf = keep.tile([P, 2, SLICE, PACK], BF16, name="h_bf%d" % j0, align_bytes=64)
+        w2_q = [[quantise_w2(half, b) for b in range(2)] for half in range(2)]
+        j0 = 0
+        held = None
+        for index, width in enumerate(SLICES):
+            h_bf = keep.tile([P, 2, width, PACK], BF16, name="h_bf", tag="h_bf%d" % min(index, 2), align_bytes=64)
             for b in range(2):
-                if j0 == 0 and b == 0:
-                    h_mostly_on_vector(h_bf, j0, b)
+                if index == 0:
+                    make_h_on_vector(h_bf, j0, b)
                 else:
-                    h_mostly_on_scalar(h_bf, j0, b, "gain_a%d_%d" % (j0, b))
-            h_w = keep.tile([P, 2 * SLICE], U32, name="h_w%d" % j0, align_bytes=64)
-            h_sc = keep.tile([P, 2 * SLICE], U8, name="h_sc%d" % j0, align_bytes=64)
+                    make_h(h_bf, j0, width, b, nc.gpsimd)
+            if held is not None:
+                last_page = weigh(*held, "gain_a%d_1" % j0)
+            h_w = work.tile([P, 2, width], U32, name="h_w", bufs=2, align_bytes=64)
+            h_sc = work.tile([P, 2, width], U8, name="h_sc", bufs=2, align_bytes=64)
             nc.vector.quantize_mx(
-                out=h_w[:].bitcast(FP8X4), scales=h_sc[:], in_=h_bf[:].rearrange("p b n t -> p (b n t)")
+                out=h_w[:].rearrange("p b n -> p (b n)").bitcast(FP8X4),
+                scales=h_sc[:].rearrange("p b n -> p (b n)"),
+                in_=h_bf[:].rearrange("p b n t -> p (b n t)"),
             )
-            if previous is not None:
-                put_back(2, second_product(1, *previous)[:], j0 - SLICE, "gain_a%d_1" % j0)
-            put_back(0, second_product(0, h_w, h_sc)[:], j0, "y_first%d" % j0)
-            previous = (h_w, h_sc)
+            if held is not None:
+                put_back(3, last_page, *held[1:])
+            banks = [second_product(pair, width, h_w, h_sc) for pair in range(2)]
+            first_two = weigh(banks[0][:], j0, width, "first_two")
+            third = weigh(banks[1][:, 0:1, :], j0, width, "third")
+            put_back(0, first_two, j0, width)
+            put_back(2, third, j0, width)
+            held = (banks[1][:, 1:2, :], j0, width)
+            j0 = j0 + width
+        put_back(3, weigh(*held, "last"), *held[1:])
 
-        last = second_product(1, *previous)
-        put_back(2, last[:, 0:SLICE], S - SLICE, "y_last")
-        finish(0, 1)
-        finish(1, 1)
-        put_back(3, last[:, SLICE : 2 * SLICE], S - SLICE, "gate0_0")
-        finish(2, 2)
-        finish(3, 2)
+        finish(0, 1, nc.gpsimd)
+        finish(1, 1, nc.gpsimd)
+        finish(2, 2, nc.vector)
+        finish(3, 2, nc.vector)

@@ -24,6 +24,7 @@ PART = 128
 GATHER = 512
 SLICES = (128, 128, 256, 256, 256)
 HALF = N // 2
+EARLY_BYTES = 4 * (2 * PACK * HALF + 16)
 PER_COLUMN = 16
 A_BANKS, Y_BANKS = 5, 3
 
@@ -34,13 +35,14 @@ def tile_list_sorted_poem_gates_kernel(
     nc = tc.nc
     with ExitStack() as ctx:
         keep = ctx.enter_context(tc.tile_pool(name="keep", bufs=1))
+        reuse = ctx.enter_context(tc.tile_pool(name="reuse", bufs=1))
         work = ctx.enter_context(tc.tile_pool(name="work", bufs=2))
         psum_a = ctx.enter_context(tc.psum_pool(name="psum_a", bufs=A_BANKS))
         psum_y = ctx.enter_context(tc.psum_pool(name="psum_y", bufs=Y_BANKS))
 
         offs_sb = keep.tile([P, S // PER_COLUMN], U16, name="offs_sb")
         offs2_sb = keep.tile([P, S // PER_COLUMN], U16, name="offs2_sb")
-        tab_sc = keep.tile([P, T], U8, name="tab_sc", tag="after_tab_sc", align_bytes=64)
+        tab_sc = reuse.tile([P, T], U8, name="tab_sc", offset=EARLY_BYTES - T // 2, align_bytes=64)
         w1_sc_raw = keep.tile([P, 2 * H], U8, name="w1_sc_raw", tag="after_w1_sc_raw", align_bytes=64)
         v_sc1 = keep.tile([P, S], U8, name="v_sc1", align_bytes=64)
         nc.vector.memset(tab_sc[:].bitcast(I32), 0)
@@ -73,31 +75,29 @@ def tile_list_sorted_poem_gates_kernel(
         tab_w1 = keep.tile([P, T], I32, name="tab_w1", tag="after_w1_raw", align_bytes=64)
         nc.sync.dma_start(tab_w1[:], tab_words[1].rearrange("p t i -> p (t i)").bitcast(I32))
 
-        def gather_words(dst, window, j0):
+        def gather_words(words, window, j0):
             entries = offs_sb[:, j0 // PER_COLUMN : (j0 + GATHER) // PER_COLUMN]
-            nc.vector.tensor_copy(dst[:, j0 : j0 + GATHER], window[:].bitcast(U32).indirect(entries))
+            nc.vector.tensor_copy(words, window[:].bitcast(U32).indirect(entries))
+            return words
 
-        v_w0 = keep.tile([P, S], U32, name="v_w0", align_bytes=64)
         v_sc0 = keep.tile([P, S], U8, name="v_sc0", align_bytes=64)
         nc.vector.tensor_copy(v_sc0[:], tab_sc[:].indirect(offs_sb[:]))
         nc.scalar.dma_start(v_sc1[0:112, :].bitcast(I32), v_sc0[16:128, :].bitcast(I32))
-        gather_words(v_w0, tab_w0, 0)
+        v_w0 = reuse.tile([P, S], U32, name="v_w0", offset=EARLY_BYTES, align_bytes=64)
+        v_w = {(0, j0): gather_words(v_w0[:, j0 : j0 + GATHER], tab_w0, j0) for j0 in range(0, S, GATHER)}
 
         w1_sc = keep.tile([P, 2 * H], U8, name="w1_sc", align_bytes=64)
         nc.vector.tensor_copy(
             w1_sc[:].rearrange("p (g t h l) -> p g h t l", g=4, t=4, l=16),
             w1_sc_raw[:].rearrange("p (g h l t) -> p g h t l", g=4, t=4, l=16),
         )
-        v_w1 = keep.tile([P, S], U32, name="v_w1", tag="after_w1_sc_raw", align_bytes=64)
-        gather_words(v_w1, tab_w1, 0)
-        gather_words(v_w0, tab_w0, GATHER)
-        gather_words(v_w1, tab_w1, GATHER)
-        v_w = [v_w0, v_w1]
+        v_w1_first = keep.tile([P, GATHER], U32, name="v_w1_first", tag="after_w1_sc_raw", align_bytes=64)
+        v_w[1, 0] = gather_words(v_w1_first[:], tab_w1, 0)
         v_sc = [v_sc0, v_sc1]
 
         w2_rows = w2.rearrange("(b p t) (half n) -> half b p t n", b=2, t=PACK, half=2)
         w2_width = PACK * HALF
-        early = keep.tile([P, 2 * w2_width + 8], F32, name="early", tag="after_tab_sc", align_bytes=64)
+        early = reuse.tile([P, 2 * w2_width + 16], F32, name="early", offset=0, align_bytes=64)
         late = keep.tile([P, 2 * w2_width + S], F32, name="late", tag="after_tab_w0", align_bytes=64)
         gain_sb = early[:, 2 * w2_width : 2 * w2_width + 8].rearrange("p (b t) -> p b t", b=2)
         nc.sync.dma_start(gain_sb, gain.rearrange("(b p t) -> p b t", b=2, t=PACK))
@@ -107,10 +107,6 @@ def tile_list_sorted_poem_gates_kernel(
                 nc.sync.dma_start(w2_raw[half][b].rearrange("p (t n) -> p t n", t=PACK), w2_rows[half, b])
         wgo_sb = late[:, 2 * w2_width : 2 * w2_width + S]
         nc.sync.dma_start(wgo_sb, wgo)
-        x0_all = keep.tile([P, 4 * S], F32, name="x0_all", tag="after_w1_raw", align_bytes=64)
-        x0_sb = [x0_all[:, S * n : S * (n + 1)] for n in range(4)]
-        for n in range(4):
-            nc.sync.dma_start(x0_sb[n], x0[P * n : P * (n + 1), :])
 
         def quantise_w2(half, b):
             woven = keep.tile([P, HALF, PACK], BF16, name="w2_bf%d%d" % (half, b), align_bytes=64)
@@ -133,7 +129,7 @@ def tile_list_sorted_poem_gates_kernel(
                         out=bank[:, PART * place : PART * (place + 1)],
                         lhsT=w1_w[:, a, 2 * c0 : 2 * (c0 + P)].bitcast(FP4X4),
                         lhsT_scale=w1_sc[:, H * a + c0 : H * a + c0 + P],
-                        rhs=v_w[a][:, j : j + PART].bitcast(FP8X4),
+                        rhs=v_w[a, j - j % GATHER][:, j % GATHER : j % GATHER + PART].bitcast(FP8X4),
                         rhs_scale=v_sc[a][:, j : j + PART],
                         start=(a == 0 and place == 0),
                         stop=(a == 1 and place == len(parts) - 1),
@@ -145,7 +141,7 @@ def tile_list_sorted_poem_gates_kernel(
             a_woven = bank[:].rearrange("p (t n) -> p n t", t=PACK)
             tanh_woven = work.tile([P, PART, PACK], F32, name="tanh_woven", bufs=2)
             nc.scalar.activation(tanh_woven[:], a_woven, ACT.Tanh)
-            total = work.tile([P, PART, PACK], F32, name="total", bufs=2)
+            total = keep.tile([P, PART, PACK], F32, name="total", tag="total%d" % b, align_bytes=64)
             nc.vector.tensor_tensor(total[:], a_woven, tanh_woven[:], ALU.add)
             nc.vector.tensor_tensor(
                 h_bf[:, b], total[:], gain_sb[:, b, :].unsqueeze(1).to_broadcast([P, PART, PACK]), ALU.mult
@@ -204,27 +200,25 @@ def tile_list_sorted_poem_gates_kernel(
             for m in range(weighted.shape[1]):
                 nc.vector.tensor_copy(pages[first_page + m][:].indirect(entries), weighted[:, m, :])
 
-        def finish(n, pieces, engine):
-            width = S // pieces
-            for c0 in range(0, S, width):
-                gate = keep.tile([P, width], F32, name="gate", tag="gate%d_%d" % (n, c0), align_bytes=64)
-                nc.scalar.activation(gate[:], pages[n][:, c0 : c0 + width], ACT.Sigmoid)
-                result = x0_sb[n][:, c0 : c0 + width]
-                engine.tensor_tensor(result, gate[:], result, ALU.mult)
-                nc.sync.dma_start(out[P * n : P * (n + 1), c0 : c0 + width], result)
+        def finish(n, c0, width, engine, result):
+            gate = keep.tile([P, width], F32, name="gate", tag="gate%d_%d" % (n, c0), align_bytes=64)
+            nc.scalar.activation(gate[:], pages[n][:, c0 : c0 + width], ACT.Sigmoid)
+            engine.tensor_tensor(result, gate[:], x0_sb[n][:, c0 : c0 + width], ALU.mult)
+            nc.sync.dma_start(out[P * n : P * (n + 1), c0 : c0 + width], result)
 
         w2_q = [[quantise_w2(half, b) for b in range(2)] for half in range(2)]
         j0 = 0
-        held = None
+        held, held_pages = None, []
+        last = len(SLICES) - 1
         for index, width in enumerate(SLICES):
-            h_bf = keep.tile([P, 2, width, PACK], BF16, name="h_bf", tag="h_bf%d" % min(index, 2), align_bytes=64)
+            h_bf = keep.tile([P, 2, width, PACK], BF16, name="h_bf", tag="h_bf%d" % (index >= 2), align_bytes=64)
             for b in range(2):
                 if index == 0:
                     make_h_on_vector(h_bf, j0, b)
                 else:
                     make_h(h_bf, j0, width, b, nc.gpsimd)
-            if held is not None:
-                last_page = weigh(*held, "gain_a%d_1" % j0)
+            if held_pages:
+                late_pages = weigh(*held, "gain_a%d_1" % j0)
             h_w = work.tile([P, 2, width], U32, name="h_w", bufs=2, align_bytes=64)
             h_sc = work.tile([P, 2, width], U8, name="h_sc", bufs=2, align_bytes=64)
             nc.vector.quantize_mx(
@@ -232,18 +226,41 @@ def tile_list_sorted_poem_gates_kernel(
                 scales=h_sc[:].rearrange("p b n -> p (b n)"),
                 in_=h_bf[:].rearrange("p b n t -> p (b n t)"),
             )
-            if held is not None:
-                put_back(3, last_page, *held[1:])
+            if index == 0:
+                v_w1_second = keep.tile([P, GATHER], U32, name="v_w1_second", tag="total1", align_bytes=64)
+                v_w[1, GATHER] = gather_words(v_w1_second[:], tab_w1, GATHER)
+                x0_all = keep.tile([P, 4 * S], F32, name="x0_all", tag="after_w1_raw", align_bytes=64)
+                x0_sb = [x0_all[:, S * n : S * (n + 1)] for n in range(4)]
+                for n in range(4):
+                    nc.sync.dma_start(x0_sb[n], x0[P * n : P * (n + 1), :])
+            for page in held_pages:
+                put_back(page, late_pages[:, page - held_pages[0] : page - held_pages[0] + 1, :], *held[1:])
             banks = [second_product(pair, width, h_w, h_sc) for pair in range(2)]
-            first_two = weigh(banks[0][:], j0, width, "first_two")
-            third = weigh(banks[1][:, 0:1, :], j0, width, "third")
-            put_back(0, first_two, j0, width)
-            put_back(2, third, j0, width)
-            held = (banks[1][:, 1:2, :], j0, width)
+            if index == last:
+                break
+            put_back(0, weigh(banks[0][:], j0, width, "first_two"), j0, width)
+            held_pages = [2, 3] if index == last - 1 else [3]
+            if index < last - 1:
+                put_back(2, weigh(banks[1][:, 0:1, :], j0, width, "third"), j0, width)
+            held = (banks[1][:, held_pages[0] - 2 : 2, :], j0, width)
             j0 = j0 + width
-        put_back(3, weigh(*held, "last"), *held[1:])
 
-        finish(0, 1, nc.gpsimd)
-        finish(1, 1, nc.gpsimd)
-        finish(2, 2, nc.vector)
-        finish(3, 2, nc.vector)
+        for pair in range(2):
+            y_sb = keep.tile([P, 2, width], F32, name="y_sb%d" % pair)
+            nc.scalar.copy(y_sb[:], banks[pair][:])
+            for m in range(2):
+                weighted = keep.tile([P, 1, width], F32, name="last_weighted%d%d" % (pair, m))
+                nc.gpsimd.tensor_tensor(weighted[:, 0, :], y_sb[:, m, :], wgo_sb[:, j0 : j0 + width], ALU.mult)
+                put_back(2 * pair + m, weighted, j0, width)
+
+        on_gpsimd = [(0, 0, 1024), (1, 0, 512)]
+        on_vector = [(1, 512, 512), (2, 0, 512), (2, 512, 512), (3, 0, 512), (3, 512, 512)]
+        for n, c0, width in on_gpsimd:
+            finish(n, c0, width, nc.gpsimd, x0_sb[n][:, c0 : c0 + width])
+        results = keep.tile(
+            [P, sum(piece[2] for piece in on_vector)], F32, name="results", tag="gate%d_%d" % on_gpsimd[-1][:2], align_bytes=64
+        )
+        done = 0
+        for n, c0, width in on_vector:
+            finish(n, c0, width, nc.vector, results[:, done : done + width])
+            done = done + width

@@ -22,7 +22,7 @@ PASS = P * PACK
 BANK = 512
 PART = 128
 GATHER = 512
-SLICES = (128, 128, 256, 256, 256)
+SLICES = (256, 256, 256, 256)
 HALF = N // 2
 EARLY_BYTES = 4 * (2 * PACK * HALF + 16)
 PER_COLUMN = 16
@@ -91,8 +91,9 @@ def tile_list_sorted_poem_gates_kernel(
             w1_sc[:].rearrange("p (g t h l) -> p g h t l", g=4, t=4, l=16),
             w1_sc_raw[:].rearrange("p (g h l t) -> p g h t l", g=4, t=4, l=16),
         )
-        v_w1_first = keep.tile([P, GATHER], U32, name="v_w1_first", tag="after_w1_sc_raw", align_bytes=64)
-        v_w[1, 0] = gather_words(v_w1_first[:], tab_w1, 0)
+        v_w1 = keep.tile([P, S], U32, name="v_w1", tag="after_w1_sc_raw", align_bytes=64)
+        for j0 in range(0, S, GATHER):
+            v_w[1, j0] = gather_words(v_w1[:, j0 : j0 + GATHER], tab_w1, j0)
         v_sc = [v_sc0, v_sc1]
 
         w2_rows = w2.rearrange("(b p t) (half n) -> half b p t n", b=2, t=PACK, half=2)
@@ -108,8 +109,8 @@ def tile_list_sorted_poem_gates_kernel(
         wgo_sb = late[:, 2 * w2_width : 2 * w2_width + S]
         nc.sync.dma_start(wgo_sb, wgo)
 
-        def quantise_w2(half, b):
-            woven = keep.tile([P, HALF, PACK], BF16, name="w2_bf%d%d" % (half, b), align_bytes=64)
+        def quantise_w2(half, b, tag):
+            woven = keep.tile([P, HALF, PACK], BF16, name="w2_bf", tag=tag, align_bytes=64)
             woven_view = woven[:].rearrange("p (c i) t -> p c t i", i=4)
             raw_view = w2_raw[half][b].rearrange("p (t c i) -> p c t i", t=PACK, i=4)
             nc.vector.tensor_copy(woven_view, raw_view)
@@ -136,19 +137,19 @@ def tile_list_sorted_poem_gates_kernel(
                     )
             return bank
 
-        def make_h_on_vector(h_bf, j0, b):
+        def make_h_on_vector(h_out, j0, b):
             bank = first_product(b, [(t, j0) for t in range(PACK)])
             a_woven = bank[:].rearrange("p (t n) -> p n t", t=PACK)
             tanh_woven = work.tile([P, PART, PACK], F32, name="tanh_woven", bufs=2)
             nc.scalar.activation(tanh_woven[:], a_woven, ACT.Tanh)
-            total = keep.tile([P, PART, PACK], F32, name="total", tag="total%d" % b, align_bytes=64)
+            total = keep.tile([P, PART, PACK], F32, name="total", tag="total%d_%d" % (j0, b), align_bytes=64)
             nc.vector.tensor_tensor(total[:], a_woven, tanh_woven[:], ALU.add)
             nc.vector.tensor_tensor(
-                h_bf[:, b], total[:], gain_sb[:, b, :].unsqueeze(1).to_broadcast([P, PART, PACK]), ALU.mult
+                h_out, total[:], gain_sb[:, b, :].unsqueeze(1).to_broadcast([P, PART, PACK]), ALU.mult
             )
 
-        def make_h(h_bf, j0, width, b, adder):
-            gain_a = keep.tile([P, PACK, width], F32, name="gain_a", tag="gain_a%d_%d" % (j0, b))
+        def make_h(h_out, j0, width, b, adder):
+            gain_a = keep.tile([P, PACK, width], F32, name="gain_a", tag="gain_a%d_%d" % (j0, b), align_bytes=64)
             gain_tanh = work.tile([P, PACK, width], F32, name="gain_tanh", bufs=4)
             per_bank = BANK // width
             for t0 in range(0, PACK, per_bank):
@@ -163,9 +164,9 @@ def tile_list_sorted_poem_gates_kernel(
                     cols = slice(width * (t - t0), width * (t - t0 + 1))
                     nc.scalar.activation(gain_tanh[:, t, :], tanh_a[:, cols], ACT.Copy, scale=gain_sb[:, b, t : t + 1])
             adder.tensor_tensor(
-                h_bf[:, b].rearrange("p (c i) t -> p c t i", i=4),
-                gain_a[:].rearrange("p t (c i) -> p c t i", i=4),
-                gain_tanh[:].rearrange("p t (c i) -> p c t i", i=4),
+                h_out,
+                gain_a[:].rearrange("p t n -> p n t"),
+                gain_tanh[:].rearrange("p t n -> p n t"),
                 ALU.add,
             )
 
@@ -189,7 +190,7 @@ def tile_list_sorted_poem_gates_kernel(
 
         def weigh(y_psum, j0, width, tag):
             count = y_psum.shape[1]
-            weighted = keep.tile([P, count, width], F32, name="weighted", tag=tag)
+            weighted = keep.tile([P, count, width], F32, name="weighted", tag=tag, align_bytes=64)
             nc.vector.tensor_tensor(
                 weighted[:], y_psum, wgo_sb[:, j0 : j0 + width].unsqueeze(1).to_broadcast([P, count, width]), ALU.mult
             )
@@ -206,19 +207,22 @@ def tile_list_sorted_poem_gates_kernel(
             engine.tensor_tensor(result, gate[:], x0_sb[n][:, c0 : c0 + width], ALU.mult)
             nc.sync.dma_start(out[P * n : P * (n + 1), c0 : c0 + width], result)
 
-        w2_q = [[quantise_w2(half, b) for b in range(2)] for half in range(2)]
+        w2_q = [[quantise_w2(0, b, "w2_bf%d" % b) for b in range(2)]]
         j0 = 0
+        V, G = nc.vector, nc.gpsimd
+        units = [[(0, 128, 0, None), (0, 128, 1, None), (128, 128, 0, V), (128, 128, 1, V)], [(0, 256, 0, G), (0, 128, 1, G), (128, 128, 1, G)], [(0, 256, 0, G), (0, 256, 1, G)], [(0, 256, 0, G), (0, 256, 1, G)]]
         held, held_pages = None, []
         last = len(SLICES) - 1
         for index, width in enumerate(SLICES):
-            h_bf = keep.tile([P, 2, width, PACK], BF16, name="h_bf", tag="h_bf%d" % (index >= 2), align_bytes=64)
-            for b in range(2):
-                if index == 0:
-                    make_h_on_vector(h_bf, j0, b)
+            h_bf = keep.tile([P, 2, width, PACK], BF16, name="h_bf", tag="h_bf0" if index == 0 else "gain_a128_1", align_bytes=64)
+            for n0, count, b, adder in units[index]:
+                if adder is None:
+                    make_h_on_vector(h_bf[:, b, n0 : n0 + count], j0 + n0, b)
                 else:
-                    make_h(h_bf, j0, width, b, nc.gpsimd)
+                    make_h(h_bf[:, b, n0 : n0 + count], j0 + n0, count, b, adder)
+            last_sum = "gain_a%d_1" % (j0 + n0)
             if held_pages:
-                late_pages = weigh(*held, "gain_a%d_1" % j0)
+                late_pages = weigh(*held, last_sum)
             h_w = work.tile([P, 2, width], U32, name="h_w", bufs=2, align_bytes=64)
             h_sc = work.tile([P, 2, width], U8, name="h_sc", bufs=2, align_bytes=64)
             nc.vector.quantize_mx(
@@ -227,8 +231,7 @@ def tile_list_sorted_poem_gates_kernel(
                 in_=h_bf[:].rearrange("p b n t -> p (b n t)"),
             )
             if index == 0:
-                v_w1_second = keep.tile([P, GATHER], U32, name="v_w1_second", tag="total1", align_bytes=64)
-                v_w[1, GATHER] = gather_words(v_w1_second[:], tab_w1, GATHER)
+                w2_q.append([quantise_w2(1, b, ("w2_bf2", "gain_a128_1")[b]) for b in range(2)])
                 x0_all = keep.tile([P, 4 * S], F32, name="x0_all", tag="after_w1_raw", align_bytes=64)
                 x0_sb = [x0_all[:, S * n : S * (n + 1)] for n in range(4)]
                 for n in range(4):
@@ -239,13 +242,14 @@ def tile_list_sorted_poem_gates_kernel(
             if index == last:
                 break
             put_back(0, weigh(banks[0][:], j0, width, "first_two"), j0, width)
-            held_pages = [2, 3] if index == last - 1 else [3]
-            if index < last - 1:
+            held_pages = [3]
+            if index < last:
                 put_back(2, weigh(banks[1][:, 0:1, :], j0, width, "third"), j0, width)
             held = (banks[1][:, held_pages[0] - 2 : 2, :], j0, width)
             j0 = j0 + width
 
-        for pair in range(2):
+        put_back(0, weigh(banks[0][:], j0, width, "first_two"), j0, width)
+        for pair in range(1, 2):
             y_sb = keep.tile([P, 2, width], F32, name="y_sb%d" % pair)
             nc.scalar.copy(y_sb[:], banks[pair][:])
             for m in range(2):
@@ -253,8 +257,8 @@ def tile_list_sorted_poem_gates_kernel(
                 nc.gpsimd.tensor_tensor(weighted[:, 0, :], y_sb[:, m, :], wgo_sb[:, j0 : j0 + width], ALU.mult)
                 put_back(2 * pair + m, weighted, j0, width)
 
-        on_gpsimd = [(0, 0, 1024), (1, 0, 512)]
-        on_vector = [(1, 512, 512), (2, 0, 512), (2, 512, 512), (3, 0, 512), (3, 512, 512)]
+        on_gpsimd = [(0, 0, 512), (0, 512, 512), (1, 0, 512)]
+        on_vector = [(1, 512, 512), (2, 0, 512), (2, 512, 512), (3, 0, 512), (3, 512, 256), (3, 768, 256)]
         for n, c0, width in on_gpsimd:
             finish(n, c0, width, nc.gpsimd, x0_sb[n][:, c0 : c0 + width])
         results = keep.tile(

@@ -164,9 +164,9 @@ def tile_list_sorted_poem_gates_kernel(
                     cols = slice(width * (t - t0), width * (t - t0 + 1))
                     nc.scalar.activation(gain_tanh[:, t, :], tanh_a[:, cols], ACT.Copy, scale=gain_sb[:, b, t : t + 1])
             adder.tensor_tensor(
-                h_out,
-                gain_a[:].rearrange("p t n -> p n t"),
-                gain_tanh[:].rearrange("p t n -> p n t"),
+                h_out.rearrange("p (c i) t -> p c t i", i=2),
+                gain_a[:].rearrange("p t (c i) -> p c t i", i=2),
+                gain_tanh[:].rearrange("p t (c i) -> p c t i", i=2),
                 ALU.add,
             )
 

@@ -25,6 +25,7 @@ GATHER = 512
 SLICES = (256, 256, 256, 256)
 HALF = N // 2
 EARLY_BYTES = 4 * (2 * PACK * HALF + 16)
+RUN = 4
 PER_COLUMN = 16
 A_BANKS, Y_BANKS = 5, 3
 
@@ -149,8 +150,8 @@ def tile_list_sorted_poem_gates_kernel(
             )
 
         def make_h(h_out, j0, width, b, adder):
-            gain_a = keep.tile([P, PACK, width], F32, name="gain_a", tag="gain_a%d_%d" % (j0, b), align_bytes=64)
-            gain_tanh = work.tile([P, PACK, width], F32, name="gain_tanh", bufs=4)
+            gain_a = keep.tile([P, width // RUN, PACK, RUN], F32, name="gain_a", tag="gain_a%d_%d" % (j0, b), align_bytes=64)
+            gain_tanh = work.tile([P, width // RUN, PACK, RUN], F32, name="gain_tanh", bufs=4)
             per_bank = BANK // width
             for t0 in range(0, PACK, per_bank):
                 ts = range(t0, t0 + per_bank)
@@ -159,14 +160,16 @@ def tile_list_sorted_poem_gates_kernel(
                 nc.scalar.activation(tanh_a[:], bank[:], ACT.Tanh)
                 for t in ts:
                     cols = slice(width * (t - t0), width * (t - t0 + 1))
-                    nc.scalar.activation(gain_a[:, t, :], bank[:, cols], ACT.Copy, scale=gain_sb[:, b, t : t + 1])
+                    source = bank[:, cols].rearrange("p (c i) -> p c i", i=RUN)
+                    nc.scalar.activation(gain_a[:, :, t, :], source, ACT.Copy, scale=gain_sb[:, b, t : t + 1])
                 for t in ts:
                     cols = slice(width * (t - t0), width * (t - t0 + 1))
-                    nc.scalar.activation(gain_tanh[:, t, :], tanh_a[:, cols], ACT.Copy, scale=gain_sb[:, b, t : t + 1])
+                    source = tanh_a[:, cols].rearrange("p (c i) -> p c i", i=RUN)
+                    nc.scalar.activation(gain_tanh[:, :, t, :], source, ACT.Copy, scale=gain_sb[:, b, t : t + 1])
             adder.tensor_tensor(
-                h_out.rearrange("p (c i) t -> p c t i", i=2),
-                gain_a[:].rearrange("p t (c i) -> p c t i", i=2),
-                gain_tanh[:].rearrange("p t (c i) -> p c t i", i=2),
+                h_out.rearrange("p (c i) t -> p c t i", i=RUN),
+                gain_a[:],
+                gain_tanh[:],
                 ALU.add,
             )
 

@@ -140,13 +140,20 @@ def tile_list_sorted_poem_gates_kernel(
 
         def make_h_on_vector(h_out, j0, b):
             bank = first_product(b, [(t, j0) for t in range(PACK)])
-            a_woven = bank[:].rearrange("p (t n) -> p n t", t=PACK)
-            tanh_woven = work.tile([P, PART, PACK], F32, name="tanh_woven", bufs=2)
-            nc.scalar.activation(tanh_woven[:], a_woven, ACT.Tanh)
-            total = keep.tile([P, PART, PACK], F32, name="total", tag="total%d_%d" % (j0, b), align_bytes=64)
-            nc.vector.tensor_tensor(total[:], a_woven, tanh_woven[:], ALU.add)
+            tanh_a = work.tile([P, BANK], F32, name="tanh_a", bufs=4)
+            nc.scalar.activation(tanh_a[:], bank[:], ACT.Tanh)
+            total = keep.tile([P, PART // RUN, PACK, RUN], F32, name="total", tag="total%d_%d" % (j0, b), align_bytes=64)
             nc.vector.tensor_tensor(
-                h_out, total[:], gain_sb[:, b, :].unsqueeze(1).to_broadcast([P, PART, PACK]), ALU.mult
+                total[:].rearrange("p c t i -> p t c i"),
+                bank[:].rearrange("p (t c i) -> p t c i", t=PACK, i=RUN),
+                tanh_a[:].rearrange("p (t c i) -> p t c i", t=PACK, i=RUN),
+                ALU.add,
+            )
+            nc.vector.tensor_tensor(
+                h_out.rearrange("p (c i) t -> p c t i", i=RUN),
+                total[:],
+                gain_sb[:, b, :].unsqueeze(1).unsqueeze(3).to_broadcast([P, PART // RUN, PACK, RUN]),
+                ALU.mult,
             )
 
         def make_h(h_out, j0, width, b, adder):
@@ -199,6 +206,24 @@ def tile_list_sorted_poem_gates_kernel(
             )
             return weighted
 
+        def weigh_on_gpsimd(y_psum, j0, width, tag):
+            count = y_psum.shape[1]
+            y_sb = keep.tile([P, count, width], F32, name="y_sb", tag=tag, align_bytes=64)
+            nc.scalar.copy(y_sb[:], y_psum)
+            weighted = keep.tile([P, count, width], F32, name="weighted", tag="from_" + tag, align_bytes=64)
+            for m in range(count):
+                nc.gpsimd.tensor_tensor(weighted[:, m, :], y_sb[:, m, :], wgo_sb[:, j0 : j0 + width], ALU.mult)
+            return weighted
+
+        def copy_out(y_psum, j0, width, tag):
+            y_sb = keep.tile([P, width], F32, name="y_held", tag=tag, align_bytes=64)
+            nc.scalar.copy(y_sb[:], y_psum[:, 0, :])
+            return y_sb
+
+        def weigh_and_put_back(page, y_sb, j0, width):
+            entries = offs2_sb[:, j0 // PER_COLUMN : (j0 + width) // PER_COLUMN]
+            nc.vector.tensor_tensor(pages[page][:].indirect(entries), y_sb[:], wgo_sb[:, j0 : j0 + width], ALU.mult)
+
         def put_back(first_page, weighted, j0, width):
             entries = offs2_sb[:, j0 // PER_COLUMN : (j0 + width) // PER_COLUMN]
             for m in range(weighted.shape[1]):
@@ -225,7 +250,7 @@ def tile_list_sorted_poem_gates_kernel(
                     make_h(h_bf[:, b, n0 : n0 + count], j0 + n0, count, b, adder)
             last_sum = "gain_a%d_1" % (j0 + n0)
             if held_pages:
-                late_pages = weigh(*held, last_sum)
+                late_pages = (copy_out if index > 1 else weigh)(*held, last_sum)
             h_w = work.tile([P, 2, width], U32, name="h_w", bufs=2, align_bytes=64)
             h_sc = work.tile([P, 2, width], U8, name="h_sc", bufs=2, align_bytes=64)
             nc.vector.quantize_mx(
@@ -240,30 +265,24 @@ def tile_list_sorted_poem_gates_kernel(
                 for n in range(4):
                     nc.sync.dma_start(x0_sb[n], x0[P * n : P * (n + 1), :])
             for page in held_pages:
-                put_back(page, late_pages[:, page - held_pages[0] : page - held_pages[0] + 1, :], *held[1:])
+                (weigh_and_put_back if index > 1 else put_back)(page, late_pages, *held[1:])
             banks = [second_product(pair, width, h_w, h_sc) for pair in range(2)]
             if index == last:
                 break
             put_back(0, weigh(banks[0][:], j0, width, "first_two"), j0, width)
-            held_pages = [3]
             if index < last:
                 put_back(2, weigh(banks[1][:, 0:1, :], j0, width, "third"), j0, width)
-            held = (banks[1][:, held_pages[0] - 2 : 2, :], j0, width)
+            held_pages = [3]
+            held = (banks[1][:, 1:2, :], j0, width)
+            postponed = (banks[1][:, 0:1, :], j0, width)
             j0 = j0 + width
 
         put_back(0, weigh(banks[0][:], j0, width, "first_two"), j0, width)
-        for pair in range(1, 2):
-            y_sb = keep.tile([P, 2, width], F32, name="y_sb%d" % pair)
-            nc.scalar.copy(y_sb[:], banks[pair][:])
-            for m in range(2):
-                weighted = keep.tile([P, 1, width], F32, name="last_weighted%d%d" % (pair, m))
-                nc.gpsimd.tensor_tensor(weighted[:, 0, :], y_sb[:, m, :], wgo_sb[:, j0 : j0 + width], ALU.mult)
-                put_back(2 * pair + m, weighted, j0, width)
-
+        put_back(2, weigh_on_gpsimd(banks[1][:], j0, width, "y_last"), j0, width)
         on_gpsimd = [(0, 0, 512), (0, 512, 512), (1, 0, 512)]
         on_vector = [(1, 512, 512), (2, 0, 512), (2, 512, 512), (3, 0, 512), (3, 512, 256), (3, 768, 256)]
-        for n, c0, width in on_gpsimd:
-            finish(n, c0, width, nc.gpsimd, x0_sb[n][:, c0 : c0 + width])
+        for place, (n, c0, count) in enumerate(on_gpsimd):
+            finish(n, c0, count, nc.gpsimd, x0_sb[n][:, c0 : c0 + count])
         results = keep.tile(
             [P, sum(piece[2] for piece in on_vector)], F32, name="results", tag="gate%d_%d" % on_gpsimd[-1][:2], align_bytes=64
         )

@@ -55,7 +55,7 @@ def tile_list_sorted_poem_gates_kernel(
         w1_raw = keep.tile([P, 2, 2 * H], U8, name="w1_raw", tag="after_w1_raw", align_bytes=64)
         nc.sync.dma_start(w1_raw[:].bitcast(I32), w1_words.bitcast(I32).rearrange("a p c -> p a c"))
         tab_w0 = keep.tile([P, T], I32, name="tab_w0", tag="after_tab_w0", align_bytes=64)
-        nc.sync.dma_start(tab_w0[:], tab_words[0].rearrange("p t i -> p (t i)").bitcast(I32))
+        nc.sync.dma_start(tab_w0[:], tab_words[0].rearrange("p t i -> p (t i)").bitcast(I32), max_dma_last_dim=T)
         for s in range(4):
             nc.scalar.dma_start(
                 tab_sc[s:128:16, :].bitcast(I32),

@@ -24,7 +24,7 @@ PART = 128
 GATHER = 512
 SLICES = (256, 256, 256, 256)
 HALF = N // 2
-EARLY_BYTES = 4 * (2 * PACK * HALF + 16)
+PIECE = 4096
 RUN = 4
 PER_COLUMN = 16
 A_BANKS, Y_BANKS = 5, 3
@@ -43,65 +43,64 @@ def tile_list_sorted_poem_gates_kernel(
 
         offs_sb = keep.tile([P, S // PER_COLUMN], U16, name="offs_sb")
         offs2_sb = keep.tile([P, S // PER_COLUMN], U16, name="offs2_sb")
-        tab_sc = reuse.tile([P, T], U8, name="tab_sc", offset=EARLY_BYTES - T // 2, align_bytes=64)
-        w1_sc_raw = keep.tile([P, 2 * H], U8, name="w1_sc_raw", tag="after_w1_sc_raw", align_bytes=64)
-        v_sc1 = keep.tile([P, S], U8, name="v_sc1", align_bytes=64)
-        nc.vector.memset(tab_sc[:].bitcast(I32), 0)
-        nc.vector.memset(w1_sc_raw[:].bitcast(I32), 0)
-        nc.vector.memset(v_sc1[:].bitcast(I32), 0)
+        tab_sc = keep.tile([P, T], U8, name="tab_sc", align_bytes=64)
+        w1_sc_raw = keep.tile([P, H], U8, name="w1_sc_raw", align_bytes=64)
+        planes = keep.tile([P, 2 * (S + H)], U8, name="planes", align_bytes=64)
+        nc.vector.memset(tab_sc[0:96, :].bitcast(I32), 0)
+        nc.vector.memset(w1_sc_raw[0:96, :].bitcast(I32), 0)
+        nc.vector.memset(planes[:].bitcast(I32), 0)
 
+        nc.sync.dma_start(tab_sc[96:128, :].bitcast(I32), tab_scales.bitcast(I32).rearrange("a q t -> (a q) t"))
+        nc.sync.dma_start(w1_sc_raw[96:128, :].bitcast(I32), w1_scales.bitcast(I32).rearrange("a q c -> (a q) c"))
         nc.sync.dma_start(offs_sb[:], offs)
         nc.sync.dma_start(offs2_sb[:], offs2)
         w1_raw = keep.tile([P, 2, 2 * H], U8, name="w1_raw", tag="after_w1_raw", align_bytes=64)
         nc.sync.dma_start(w1_raw[:].bitcast(I32), w1_words.bitcast(I32).rearrange("a p c -> p a c"))
         tab_w0 = keep.tile([P, T], I32, name="tab_w0", tag="after_tab_w0", align_bytes=64)
-        nc.sync.dma_start(tab_w0[:], tab_words[0].rearrange("p t i -> p (t i)").bitcast(I32), max_dma_last_dim=T)
-        for s in range(4):
-            nc.scalar.dma_start(
-                tab_sc[s:128:16, :].bitcast(I32),
-                tab_scales.bitcast(I32)[:, s:16:4, :].rearrange("a q t -> q a t"),
-            )
-        for q in range(4):
-            queue = nc.gpsimd if q < 2 else nc.scalar
-            queue.dma_start(
-                w1_sc_raw[32 * q : 32 * q + 4, :].bitcast(I32).rearrange("p (a c) -> p a c", a=2),
-                w1_scales.bitcast(I32)[:, 4 * q : 4 * q + 4, :].rearrange("a r c -> r a c"),
-            )
+        nc.sync.dma_start(tab_w0[:], tab_words[0].rearrange("p t i -> p (t i)").bitcast(I32), max_dma_last_dim=PIECE)
+        v_sc_rows = reuse.tile([P, S], U8, name="v_sc_rows", offset=4 * T - S // 2, align_bytes=64)
+        nc.vector.tensor_copy(v_sc_rows[:], tab_sc[:].indirect(offs_sb[:]))
+        sc_rows = keep.tile([P, S + H], U8, name="sc_rows", align_bytes=64)
+        nc.vector.tensor_copy(
+            sc_rows[:, S:].rearrange("p (g t h l) -> p g h t l", g=2, t=4, l=16),
+            w1_sc_raw[:].rearrange("p (g h l t) -> p g h t l", g=2, t=4, l=16),
+        )
+        nc.vector.tensor_copy(sc_rows[:, 0:S].bitcast(I32), v_sc_rows[:].bitcast(I32))
 
-        w1_w = keep.tile([P, 2, 2 * H], U8, name="w1_w", align_bytes=64)
+        for a in range(2):
+            for q in range(4):
+                queue = nc.sync if a == 0 else (nc.scalar, nc.gpsimd)[q % 2]
+                row = 96 + 16 * a + 4 * q
+                queue.dma_start(
+                    planes[32 * q : 32 * q + 4, (S + H) * a : (S + H) * (a + 1)].bitcast(I32),
+                    sc_rows[row : row + 4, :].bitcast(I32),
+                )
+
+        w1_w = reuse.tile([P, 2, 2 * H], U8, name="w1_w", offset=4 * T, align_bytes=64)
         nc.vector.tensor_copy(
             w1_w[:].rearrange("p a c -> p (a c)").bitcast(U16).rearrange("p (g t h l) -> p g h t l", g=4, t=4, l=8),
             w1_raw[:].rearrange("p a c -> p (a c)").bitcast(U16).rearrange("p (g h l t) -> p g h t l", g=4, t=4, l=8),
         )
-        tab_w1 = keep.tile([P, T], I32, name="tab_w1", tag="after_w1_raw", align_bytes=64)
-        nc.sync.dma_start(tab_w1[:], tab_words[1].rearrange("p t i -> p (t i)").bitcast(I32))
+        tab_w1 = reuse.tile([P, T], I32, name="tab_w1", offset=0, align_bytes=64)
+        nc.sync.dma_start(tab_w1[:], tab_words[1].rearrange("p t i -> p (t i)").bitcast(I32), max_dma_last_dim=PIECE)
 
         def gather_words(words, window, j0):
             entries = offs_sb[:, j0 // PER_COLUMN : (j0 + GATHER) // PER_COLUMN]
             nc.vector.tensor_copy(words, window[:].bitcast(U32).indirect(entries))
             return words
 
-        v_sc0 = keep.tile([P, S], U8, name="v_sc0", align_bytes=64)
-        nc.vector.tensor_copy(v_sc0[:], tab_sc[:].indirect(offs_sb[:]))
-        nc.scalar.dma_start(v_sc1[0:112, :].bitcast(I32), v_sc0[16:128, :].bitcast(I32))
-        v_w0 = reuse.tile([P, S], U32, name="v_w0", offset=EARLY_BYTES, align_bytes=64)
-        v_w = {(0, j0): gather_words(v_w0[:, j0 : j0 + GATHER], tab_w0, j0) for j0 in range(0, S, GATHER)}
+        v_w0 = keep.tile([P, S], U32, name="v_w0", align_bytes=64)
+        v_w = {(0, j0): gather_words(v_w0[:, j0 : j0 + GATHER], tab_w0, j0) for j0 in range(S - GATHER, -1, -GATHER)}
 
-        w1_sc = keep.tile([P, 2 * H], U8, name="w1_sc", align_bytes=64)
-        nc.vector.tensor_copy(
-            w1_sc[:].rearrange("p (g t h l) -> p g h t l", g=4, t=4, l=16),
-            w1_sc_raw[:].rearrange("p (g h l t) -> p g h t l", g=4, t=4, l=16),
-        )
-        v_w1 = keep.tile([P, S], U32, name="v_w1", tag="after_w1_sc_raw", align_bytes=64)
+        v_w1 = keep.tile([P, S], U32, name="v_w1", align_bytes=64)
         for j0 in range(0, S, GATHER):
             v_w[1, j0] = gather_words(v_w1[:, j0 : j0 + GATHER], tab_w1, j0)
-        v_sc = [v_sc0, v_sc1]
 
         w2_rows = w2.rearrange("(b p t) (half n) -> half b p t n", b=2, t=PACK, half=2)
         w2_width = PACK * HALF
-        early = reuse.tile([P, 2 * w2_width + 16], F32, name="early", offset=0, align_bytes=64)
+        early = keep.tile([P, 2 * w2_width + 8], F32, name="early", tag="after_w1_raw", align_bytes=64)
         late = keep.tile([P, 2 * w2_width + S], F32, name="late", tag="after_tab_w0", align_bytes=64)
-        gain_sb = early[:, 2 * w2_width : 2 * w2_width + 8].rearrange("p (b t) -> p b t", b=2)
+        gain_sb = early[:, 2 * w2_width :].rearrange("p (b t) -> p b t", b=2)
         nc.sync.dma_start(gain_sb, gain.rearrange("(b p t) -> p b t", b=2, t=PACK))
         w2_raw = [[tile[:, w2_width * b : w2_width * (b + 1)] for b in range(2)] for tile in (early, late)]
         for half in range(2):
@@ -130,9 +129,9 @@ def tile_list_sorted_poem_gates_kernel(
                     nc.tensor.matmul_mx(
                         out=bank[:, PART * place : PART * (place + 1)],
                         lhsT=w1_w[:, a, 2 * c0 : 2 * (c0 + P)].bitcast(FP4X4),
-                        lhsT_scale=w1_sc[:, H * a + c0 : H * a + c0 + P],
+                        lhsT_scale=planes[:, (S + H) * a + S + c0 : (S + H) * a + S + c0 + P],
                         rhs=v_w[a, j - j % GATHER][:, j % GATHER : j % GATHER + PART].bitcast(FP8X4),
-                        rhs_scale=v_sc[a][:, j : j + PART],
+                        rhs_scale=planes[:, (S + H) * a + j : (S + H) * a + j + PART],
                         start=(a == 0 and place == 0),
                         stop=(a == 1 and place == len(parts) - 1),
                     )
@@ -260,7 +259,7 @@ def tile_list_sorted_poem_gates_kernel(
             )
             if index == 0:
                 w2_q.append([quantise_w2(1, b, ("w2_bf2", "gain_a128_1")[b]) for b in range(2)])
-                x0_all = keep.tile([P, 4 * S], F32, name="x0_all", tag="after_w1_raw", align_bytes=64)
+                x0_all = reuse.tile([P, 4 * S], F32, name="x0_all", offset=0, align_bytes=64)
                 x0_sb = [x0_all[:, S * n : S * (n + 1)] for n in range(4)]
                 for n in range(4):
                     nc.sync.dma_start(x0_sb[n], x0[P * n : P * (n + 1), :])

@@ -24,7 +24,6 @@ PART = 128
 GATHER = 512
 SLICES = (256, 256, 256, 256)
 HALF = N // 2
-PIECE = 4096
 RUN = 4
 PER_COLUMN = 16
 A_BANKS, Y_BANKS = 5, 3
@@ -50,14 +49,14 @@ def tile_list_sorted_poem_gates_kernel(
         nc.vector.memset(w1_sc_raw[0:96, :].bitcast(I32), 0)
         nc.vector.memset(planes[:].bitcast(I32), 0)
 
+        nc.sync.dma_start(offs_sb[:], offs)
         nc.sync.dma_start(tab_sc[96:128, :].bitcast(I32), tab_scales.bitcast(I32).rearrange("a q t -> (a q) t"))
         nc.sync.dma_start(w1_sc_raw[96:128, :].bitcast(I32), w1_scales.bitcast(I32).rearrange("a q c -> (a q) c"))
-        nc.sync.dma_start(offs_sb[:], offs)
         nc.sync.dma_start(offs2_sb[:], offs2)
         w1_raw = keep.tile([P, 2, 2 * H], U8, name="w1_raw", tag="after_w1_raw", align_bytes=64)
         nc.sync.dma_start(w1_raw[:].bitcast(I32), w1_words.bitcast(I32).rearrange("a p c -> p a c"))
         tab_w0 = keep.tile([P, T], I32, name="tab_w0", tag="after_tab_w0", align_bytes=64)
-        nc.sync.dma_start(tab_w0[:], tab_words[0].rearrange("p t i -> p (t i)").bitcast(I32), max_dma_last_dim=PIECE)
+        nc.sync.dma_start(tab_w0[:], tab_words[0].rearrange("p t i -> p (t i)").bitcast(I32))
         v_sc_rows = reuse.tile([P, S], U8, name="v_sc_rows", offset=4 * T - S // 2, align_bytes=64)
         nc.vector.tensor_copy(v_sc_rows[:], tab_sc[:].indirect(offs_sb[:]))
         sc_rows = keep.tile([P, S + H], U8, name="sc_rows", align_bytes=64)
@@ -67,14 +66,15 @@ def tile_list_sorted_poem_gates_kernel(
         )
         nc.vector.tensor_copy(sc_rows[:, 0:S].bitcast(I32), v_sc_rows[:].bitcast(I32))
 
-        for a in range(2):
+        def move_rows(a):
             for q in range(4):
-                queue = nc.sync if a == 0 else (nc.scalar, nc.gpsimd)[q % 2]
                 row = 96 + 16 * a + 4 * q
-                queue.dma_start(
+                nc.sync.dma_start(
                     planes[32 * q : 32 * q + 4, (S + H) * a : (S + H) * (a + 1)].bitcast(I32),
                     sc_rows[row : row + 4, :].bitcast(I32),
                 )
+
+        move_rows(0)
 
         w1_w = reuse.tile([P, 2, 2 * H], U8, name="w1_w", offset=4 * T, align_bytes=64)
         nc.vector.tensor_copy(
@@ -82,7 +82,8 @@ def tile_list_sorted_poem_gates_kernel(
             w1_raw[:].rearrange("p a c -> p (a c)").bitcast(U16).rearrange("p (g h l t) -> p g h t l", g=4, t=4, l=8),
         )
         tab_w1 = reuse.tile([P, T], I32, name="tab_w1", offset=0, align_bytes=64)
-        nc.sync.dma_start(tab_w1[:], tab_words[1].rearrange("p t i -> p (t i)").bitcast(I32), max_dma_last_dim=PIECE)
+        nc.sync.dma_start(tab_w1[:], tab_words[1].rearrange("p t i -> p (t i)").bitcast(I32))
+        move_rows(1)
 
         def gather_words(words, window, j0):
             entries = offs_sb[:, j0 // PER_COLUMN : (j0 + GATHER) // PER_COLUMN]
@@ -157,7 +158,7 @@ def tile_list_sorted_poem_gates_kernel(
 
         def make_h(h_out, j0, width, b, adder):
             gain_a = keep.tile([P, width // RUN, PACK, RUN], F32, name="gain_a", tag="gain_a%d_%d" % (j0, b), align_bytes=64)
-            gain_tanh = work.tile([P, width // RUN, PACK, RUN], F32, name="gain_tanh", bufs=4)
+            gain_tanh = work.tile([P, width // RUN, PACK, RUN], F32, name="gain_tanh", bufs=6)
             per_bank = BANK // width
             for t0 in range(0, PACK, per_bank):
                 ts = range(t0, t0 + per_bank)
@@ -180,108 +181,126 @@ def tile_list_sorted_poem_gates_kernel(
             )
 
         pages = [keep.tile([P, S], F32, name="page%d" % n) for n in range(4)]
+        h_q = []
+        starts = [sum(SLICES[:k]) for k in range(len(SLICES))]
 
-        def second_product(pair, width, h_w, h_sc):
-            bank = psum_y.tile([P, 2, width], F32, name="y_bank")
-            for m in range(2):
-                c0 = P * m
+        def second_product(parts):
+            bank = psum_y.tile([P, sum(SLICES[k] for n, k in parts)], F32, name="y_bank")
+            at = 0
+            for n, k in parts:
+                c0 = P * (n % 2)
                 for b in range(2):
                     nc.tensor.matmul_mx(
-                        out=bank[:, m, :],
-                        lhsT=w2_q[pair][b][0][:, c0 : c0 + P].bitcast(FP8X4),
-                        lhsT_scale=w2_q[pair][b][1][:, c0 : c0 + P],
-                        rhs=h_w[:, b, :].bitcast(FP8X4),
-                        rhs_scale=h_sc[:, b, :],
+                        out=bank[:, at : at + SLICES[k]],
+                        lhsT=w2_q[n // 2][b][0][:, c0 : c0 + P].bitcast(FP8X4),
+                        lhsT_scale=w2_q[n // 2][b][1][:, c0 : c0 + P],
+                        rhs=h_q[k][0][:, b, :].bitcast(FP8X4),
+                        rhs_scale=h_q[k][1][:, b, :],
                         start=(b == 0),
                         stop=(b == 1),
                     )
+                at = at + SLICES[k]
             return bank
 
-        def weigh(y_psum, j0, width, tag):
-            count = y_psum.shape[1]
-            weighted = keep.tile([P, count, width], F32, name="weighted", tag=tag, align_bytes=64)
-            nc.vector.tensor_tensor(
-                weighted[:], y_psum, wgo_sb[:, j0 : j0 + width].unsqueeze(1).to_broadcast([P, count, width]), ALU.mult
-            )
-            return weighted
+        def places(j0, width):
+            return offs2_sb[:, j0 // PER_COLUMN : (j0 + width) // PER_COLUMN]
 
-        def weigh_on_gpsimd(y_psum, j0, width, tag):
-            count = y_psum.shape[1]
+        def weigh(how, y_psum, count, j0, width, tag):
+            factor = wgo_sb[:, j0 : j0 + width]
+            if how == "V":
+                weighted = keep.tile([P, count, width], F32, name="weighted", tag=tag, align_bytes=64)
+                nc.vector.tensor_tensor(
+                    weighted[:], y_psum.rearrange("p (m j) -> p m j", m=count), factor.unsqueeze(1).to_broadcast([P, count, width]), ALU.mult
+                )
+                return weighted
+            if how == "H":
+                weighted = keep.tile([P, count, width], F32, name="weighted", tag=tag, align_bytes=64)
+                for m in range(count):
+                    nc.gpsimd.tensor_tensor(weighted[:, m, :], y_psum[:, m, :], factor, ALU.mult)
+                return weighted
             y_sb = keep.tile([P, count, width], F32, name="y_sb", tag=tag, align_bytes=64)
-            nc.scalar.copy(y_sb[:], y_psum)
+            nc.scalar.copy(y_sb[:].rearrange("p m j -> p (m j)"), y_psum)
+            if how == "F":
+                return y_sb
             weighted = keep.tile([P, count, width], F32, name="weighted", tag="from_" + tag, align_bytes=64)
             for m in range(count):
-                nc.gpsimd.tensor_tensor(weighted[:, m, :], y_sb[:, m, :], wgo_sb[:, j0 : j0 + width], ALU.mult)
+                nc.gpsimd.tensor_tensor(weighted[:, m, :], y_sb[:, m, :], factor, ALU.mult)
             return weighted
 
-        def copy_out(y_psum, j0, width, tag):
-            y_sb = keep.tile([P, width], F32, name="y_held", tag=tag, align_bytes=64)
-            nc.scalar.copy(y_sb[:], y_psum[:, 0, :])
-            return y_sb
+        def put_back(how, values, page_list, j0, width):
+            for m, n in enumerate(page_list):
+                window = pages[n][:].indirect(places(j0, width))
+                if how == "F":
+                    nc.vector.tensor_tensor(window, values[:, m, :], wgo_sb[:, j0 : j0 + width], ALU.mult)
+                else:
+                    nc.vector.tensor_copy(window, values[:, m, :])
 
-        def weigh_and_put_back(page, y_sb, j0, width):
-            entries = offs2_sb[:, j0 // PER_COLUMN : (j0 + width) // PER_COLUMN]
-            nc.vector.tensor_tensor(pages[page][:].indirect(entries), y_sb[:], wgo_sb[:, j0 : j0 + width], ALU.mult)
-
-        def put_back(first_page, weighted, j0, width):
-            entries = offs2_sb[:, j0 // PER_COLUMN : (j0 + width) // PER_COLUMN]
-            for m in range(weighted.shape[1]):
-                nc.vector.tensor_copy(pages[first_page + m][:].indirect(entries), weighted[:, m, :])
-
-        def finish(n, c0, width, engine, result):
+        def finish(n, c0, width, engine, tag):
             gate = keep.tile([P, width], F32, name="gate", tag="gate%d_%d" % (n, c0), align_bytes=64)
             nc.scalar.activation(gate[:], pages[n][:, c0 : c0 + width], ACT.Sigmoid)
+            if tag is None:
+                result = x0_sb[n][:, c0 : c0 + width]
+            else:
+                result = tag
             engine.tensor_tensor(result, gate[:], x0_sb[n][:, c0 : c0 + width], ALU.mult)
             nc.sync.dma_start(out[P * n : P * (n + 1), c0 : c0 + width], result)
 
-        w2_q = [[quantise_w2(0, b, "w2_bf%d" % b) for b in range(2)]]
-        j0 = 0
         V, G = nc.vector, nc.gpsimd
         units = [[(0, 128, 0, None), (0, 128, 1, None), (128, 128, 0, V), (128, 128, 1, V)], [(0, 256, 0, G), (0, 128, 1, G), (128, 128, 1, G)], [(0, 256, 0, G), (0, 256, 1, G)], [(0, 256, 0, G), (0, 256, 1, G)]]
-        held, held_pages = None, []
-        last = len(SLICES) - 1
+        plan = [
+ [[("V", [0, 1], [0], False)], [("V", [2], [0], False), ("V", [3], [0], True)]],
+ [[("V", [0, 1], [1], False)], [("V", [2], [1], False), ("F", [3], [1], True)]],
+ [[("V", [0, 1], [2], False)], [("V", [2], [2], False), ("F", [3], [2], True)]],
+ [[("V", [0, 1], [3], False)], [("G", [2, 3], [3], False)]],
+]
+        w2_q = [[quantise_w2(0, b, "w2_bf%d" % b) for b in range(2)]]
+        held = []
+        gate_tag = "gain_a128_1"
         for index, width in enumerate(SLICES):
-            h_bf = keep.tile([P, 2, width, PACK], BF16, name="h_bf", tag="h_bf0" if index == 0 else "gain_a128_1", align_bytes=64)
+            j0 = starts[index]
+            h_bf = keep.tile([P, 2, width, PACK], BF16, name="h_bf", tag="h_bf0" if index == 0 else gate_tag, align_bytes=64)
             for n0, count, b, adder in units[index]:
                 if adder is None:
                     make_h_on_vector(h_bf[:, b, n0 : n0 + count], j0 + n0, b)
                 else:
                     make_h(h_bf[:, b, n0 : n0 + count], j0 + n0, count, b, adder)
             last_sum = "gain_a%d_1" % (j0 + n0)
-            if held_pages:
-                late_pages = (copy_out if index > 1 else weigh)(*held, last_sum)
-            h_w = work.tile([P, 2, width], U32, name="h_w", bufs=2, align_bytes=64)
-            h_sc = work.tile([P, 2, width], U8, name="h_sc", bufs=2, align_bytes=64)
+            late_values = [weigh(how, y, len(ps), i0, w, last_sum) for how, y, ps, i0, w in held]
+            h_w = keep.tile([P, 2, width], U32, name="h_w%d" % index, align_bytes=64)
+            h_sc = keep.tile([P, 2, width], U8, name="h_sc%d" % index, align_bytes=64)
             nc.vector.quantize_mx(
                 out=h_w[:].rearrange("p b n -> p (b n)").bitcast(FP8X4),
                 scales=h_sc[:].rearrange("p b n -> p (b n)"),
                 in_=h_bf[:].rearrange("p b n t -> p (b n t)"),
             )
+            h_q.append((h_w, h_sc))
             if index == 0:
                 w2_q.append([quantise_w2(1, b, ("w2_bf2", "gain_a128_1")[b]) for b in range(2)])
                 x0_all = reuse.tile([P, 4 * S], F32, name="x0_all", offset=0, align_bytes=64)
                 x0_sb = [x0_all[:, S * n : S * (n + 1)] for n in range(4)]
                 for n in range(4):
                     nc.sync.dma_start(x0_sb[n], x0[P * n : P * (n + 1), :])
-            for page in held_pages:
-                (weigh_and_put_back if index > 1 else put_back)(page, late_pages, *held[1:])
-            banks = [second_product(pair, width, h_w, h_sc) for pair in range(2)]
-            if index == last:
-                break
-            put_back(0, weigh(banks[0][:], j0, width, "first_two"), j0, width)
-            if index < last:
-                put_back(2, weigh(banks[1][:, 0:1, :], j0, width, "third"), j0, width)
-            held_pages = [3]
-            held = (banks[1][:, 1:2, :], j0, width)
-            postponed = (banks[1][:, 0:1, :], j0, width)
-            j0 = j0 + width
+            for (how, y, ps, i0, w), values in zip(held, late_values):
+                put_back(how, values, ps, i0, w)
+            held = []
+            for number, groups in enumerate(plan[index]):
+                bank = second_product([(n, k) for how, ps, ks, hold in groups for n in ps for k in ks])
+                at = 0
+                for place, (how, ps, ks, hold) in enumerate(groups):
+                    w = sum(SLICES[k] for k in ks)
+                    y = bank[:, at : at + w * len(ps)]
+                    at = at + w * len(ps)
+                    if how == "H":
+                        y = weigh("F", y, len(ps), starts[ks[0]], w, "y_kept%d" % index)
+                    if hold:
+                        held.append((how, y, ps, starts[ks[0]], w))
+                    else:
+                        put_back(how, weigh(how, y, len(ps), starts[ks[0]], w, "w%d_%d_%d" % (index, number, place)), ps, starts[ks[0]], w)
 
-        put_back(0, weigh(banks[0][:], j0, width, "first_two"), j0, width)
-        put_back(2, weigh_on_gpsimd(banks[1][:], j0, width, "y_last"), j0, width)
         on_gpsimd = [(0, 0, 512), (0, 512, 512), (1, 0, 512)]
         on_vector = [(1, 512, 512), (2, 0, 512), (2, 512, 512), (3, 0, 512), (3, 512, 256), (3, 768, 256)]
-        for place, (n, c0, count) in enumerate(on_gpsimd):
-            finish(n, c0, count, nc.gpsimd, x0_sb[n][:, c0 : c0 + count])
+        for n, c0, count in on_gpsimd:
+            finish(n, c0, count, nc.gpsimd, None)
         results = keep.tile(
             [P, sum(piece[2] for piece in on_vector)], F32, name="results", tag="gate%d_%d" % on_gpsimd[-1][:2], align_bytes=64
         )

@@ -97,6 +97,11 @@ def tile_list_sorted_poem_gates_kernel(
         for j0 in range(0, S, GATHER):
             v_w[1, j0] = gather_words(v_w1[:, j0 : j0 + GATHER], tab_w1, j0)
 
+        warm_in = keep.tile([P, 1], F32, name="warm_in")
+        warm_out = keep.tile([P, 1], F32, name="warm_out")
+        nc.gpsimd.memset(warm_in[:], 0.0)
+        nc.scalar.activation(warm_out[:], warm_in[:], ACT.Sigmoid)
+
         w2_rows = w2.rearrange("(b p t) (half n) -> half b p t n", b=2, t=PACK, half=2)
         w2_width = PACK * HALF
         early = keep.tile([P, 2 * w2_width + 8], F32, name="early", tag="after_w1_raw", align_bytes=64)

@@ -22,7 +22,7 @@ PASS = P * PACK
 BANK = 512
 PART = 128
 GATHER = 512
-SLICES = (256, 256, 256, 256)
+SLICES = (128, 128, 256, 256, 256)
 HALF = N // 2
 RUN = 4
 PER_COLUMN = 16
@@ -115,11 +115,14 @@ def tile_list_sorted_poem_gates_kernel(
         wgo_sb = late[:, 2 * w2_width : 2 * w2_width + S]
         nc.sync.dma_start(wgo_sb, wgo)
 
-        def quantise_w2(half, b, tag):
+        def quantise_w2(half, b, tag, on_scalar=False):
             woven = keep.tile([P, HALF, PACK], BF16, name="w2_bf", tag=tag, align_bytes=64)
             woven_view = woven[:].rearrange("p (c i) t -> p c t i", i=4)
             raw_view = w2_raw[half][b].rearrange("p (t c i) -> p c t i", t=PACK, i=4)
-            nc.vector.tensor_copy(woven_view, raw_view)
+            if on_scalar:
+                nc.scalar.copy(woven_view, raw_view)
+            else:
+                nc.vector.tensor_copy(woven_view, raw_view)
             words = keep.tile([P, HALF], U32, name="w2_w%d%d" % (half, b), align_bytes=64)
             scales = keep.tile([P, HALF], U8, name="w2_sc%d%d" % (half, b), align_bytes=64)
             nc.vector.quantize_mx(
@@ -143,23 +146,14 @@ def tile_list_sorted_poem_gates_kernel(
                     )
             return bank
 
-        def make_h_on_vector(h_out, j0, b):
+        def make_h_on_vector(h_out, j0, b, engine):
             bank = first_product(b, [(t, j0) for t in range(PACK)])
-            tanh_a = work.tile([P, BANK], F32, name="tanh_a", bufs=4)
-            nc.scalar.activation(tanh_a[:], bank[:], ACT.Tanh)
-            total = keep.tile([P, PART // RUN, PACK, RUN], F32, name="total", tag="total%d_%d" % (j0, b), align_bytes=64)
-            nc.vector.tensor_tensor(
-                total[:].rearrange("p c t i -> p t c i"),
-                bank[:].rearrange("p (t c i) -> p t c i", t=PACK, i=RUN),
-                tanh_a[:].rearrange("p (t c i) -> p t c i", t=PACK, i=RUN),
-                ALU.add,
-            )
-            nc.vector.tensor_tensor(
-                h_out.rearrange("p (c i) t -> p c t i", i=RUN),
-                total[:],
-                gain_sb[:, b, :].unsqueeze(1).unsqueeze(3).to_broadcast([P, PART // RUN, PACK, RUN]),
-                ALU.mult,
-            )
+            woven_a = bank[:].rearrange("p (t j) -> p j t", t=PACK)
+            tanh_a = work.tile([P, PART, PACK], F32, name="tanh_a", bufs=4)
+            nc.scalar.activation(tanh_a[:], woven_a, ACT.Tanh)
+            total = keep.tile([P, PART, PACK], F32, name="total", tag="total%d_%d" % (j0, b), align_bytes=64)
+            nc.vector.tensor_tensor(total[:], woven_a, tanh_a[:], ALU.add)
+            engine.tensor_tensor(h_out, total[:], gain_sb[:, b, :].unsqueeze(1).to_broadcast([P, PART, PACK]), ALU.mult)
 
         def make_h(h_out, j0, width, b, adder):
             gain_a = keep.tile([P, width // RUN, PACK, RUN], F32, name="gain_a", tag="gain_a%d_%d" % (j0, b), align_bytes=64)
@@ -251,36 +245,49 @@ def tile_list_sorted_poem_gates_kernel(
             nc.sync.dma_start(out[P * n : P * (n + 1), c0 : c0 + width], result)
 
         V, G = nc.vector, nc.gpsimd
-        units = [[(0, 128, 0, None), (0, 128, 1, None), (128, 128, 0, V), (128, 128, 1, V)], [(0, 256, 0, G), (0, 128, 1, G), (128, 128, 1, G)], [(0, 256, 0, G), (0, 256, 1, G)], [(0, 256, 0, G), (0, 256, 1, G)]]
+        units = [[(0, 128, 0, "BV"), (0, 128, 1, "BV")], [(0, 128, 0, "BG"), (0, 128, 1, "BG")], [(0, 128, 0, "BG"), (128, 128, 0, "BG"), (0, 256, 1, G)], [(0, 256, 0, G), (0, 256, 1, G)], [(0, 256, 0, G), (0, 128, 1, G), (128, 128, 1, G)]]
         plan = [
- [[("V", [0, 1], [0], False)], [("V", [2], [0], False), ("V", [3], [0], True)]],
- [[("V", [0, 1], [1], False)], [("V", [2], [1], False), ("F", [3], [1], True)]],
- [[("V", [0, 1], [2], False)], [("V", [2], [2], False), ("F", [3], [2], True)]],
- [[("V", [0, 1], [3], False)], [("G", [2, 3], [3], False)]],
+ [[("V", [0], [0], False), ("V", [1], [0], True)]],
+ [[("V", [0, 1], [1], False)], [("V", [3], [0, 1], False)], [("V", [2], [0, 1], True)]],
+ [[("V", [0, 1], [2], False)], [("V", [3], [2], False), ("V", [2], [2], True)]],
+ [[("V", [0, 1], [3], False)], [("F", [2], [3], True)]],
+ [[("V", [0, 1], [4], False)], [("G", [2], [4], False)], [("G", [3], [3, 4], False)]],
 ]
-        w2_q = [[quantise_w2(0, b, "w2_bf%d" % b) for b in range(2)]]
+        w2_q = [[None, None], [None, None]]
+        pieces = {(0, 0): [(0, 0, False, "a")], (0, 9): [(0, 1, True, "b")]}
+        joined = {0: (1, 0), 1: (1, 1)}
         held = []
-        gate_tag = "gain_a128_1"
+        gate_tag = "h_bf0"
         for index, width in enumerate(SLICES):
             j0 = starts[index]
-            h_bf = keep.tile([P, 2, width, PACK], BF16, name="h_bf", tag="h_bf0" if index == 0 else gate_tag, align_bytes=64)
-            for n0, count, b, adder in units[index]:
-                if adder is None:
-                    make_h_on_vector(h_bf[:, b, n0 : n0 + count], j0 + n0, b)
+            extra = HALF if index in joined else 0
+            both = keep.tile([P, 2 * width + extra, PACK], BF16, name="h_bf", tag="h_bf0" if index == 0 else gate_tag, align_bytes=64)
+            h_bf = both[:, 0 : 2 * width, :].rearrange("p (b n) t -> p b n t", b=2)
+            for u, (n0, count, b, adder) in enumerate(units[index]):
+                for half, pb, on_scalar, tag in pieces.get((index, u), []):
+                    w2_q[half][pb] = quantise_w2(half, pb, tag, on_scalar)
+                if adder in ("BV", "BG"):
+                    make_h_on_vector(h_bf[:, b, n0 : n0 + count], j0 + n0, b, V if adder == "BV" else G)
+                    last_sum = "total%d_%d" % (j0 + n0, b)
                 else:
+                    last_sum = "gain_a%d_%d" % (j0 + n0, b)
                     make_h(h_bf[:, b, n0 : n0 + count], j0 + n0, count, b, adder)
-            last_sum = "gain_a%d_1" % (j0 + n0)
+            if extra:
+                half, pb = joined[index]
+                nc.scalar.copy(
+                    both[:, 2 * width :, :].rearrange("p (c i) t -> p c t i", i=4),
+                    w2_raw[half][pb].rearrange("p (t c i) -> p c t i", t=PACK, i=4),
+                )
             late_values = [weigh(how, y, len(ps), i0, w, last_sum) for how, y, ps, i0, w in held]
-            h_w = keep.tile([P, 2, width], U32, name="h_w%d" % index, align_bytes=64)
-            h_sc = keep.tile([P, 2, width], U8, name="h_sc%d" % index, align_bytes=64)
-            nc.vector.quantize_mx(
-                out=h_w[:].rearrange("p b n -> p (b n)").bitcast(FP8X4),
-                scales=h_sc[:].rearrange("p b n -> p (b n)"),
-                in_=h_bf[:].rearrange("p b n t -> p (b n t)"),
-            )
-            h_q.append((h_w, h_sc))
+            h_w = keep.tile([P, 2 * width + extra], U32, name="h_w%d" % index, align_bytes=64)
+            h_sc = keep.tile([P, 2 * width + extra], U8, name="h_sc%d" % index, align_bytes=64)
+            nc.vector.quantize_mx(out=h_w[:].bitcast(FP8X4), scales=h_sc[:], in_=both[:].rearrange("p n t -> p (n t)"))
+            h_q.append([tile[:, 0 : 2 * width].rearrange("p (b n) -> p b n", b=2) for tile in (h_w, h_sc)])
+            if extra:
+                w2_q[half][pb] = (h_w[:, 2 * width :], h_sc[:, 2 * width :])
+            for half, pb, on_scalar, tag in pieces.get((index, 9), []):
+                w2_q[half][pb] = quantise_w2(half, pb, tag, on_scalar)
             if index == 0:
-                w2_q.append([quantise_w2(1, b, ("w2_bf2", "gain_a128_1")[b]) for b in range(2)])
                 x0_all = reuse.tile([P, 4 * S], F32, name="x0_all", offset=0, align_bytes=64)
                 x0_sb = [x0_all[:, S * n : S * (n + 1)] for n in range(4)]
                 for n in range(4):
@@ -302,8 +309,8 @@ def tile_list_sorted_poem_gates_kernel(
                     else:
                         put_back(how, weigh(how, y, len(ps), starts[ks[0]], w, "w%d_%d_%d" % (index, number, place)), ps, starts[ks[0]], w)
 
-        on_gpsimd = [(0, 0, 512), (0, 512, 512), (1, 0, 512)]
-        on_vector = [(1, 512, 512), (2, 0, 512), (2, 512, 512), (3, 0, 512), (3, 512, 256), (3, 768, 256)]
+        on_gpsimd = [(0, 0, 512), (0, 512, 512), (1, 0, 512), (1, 512, 512)]
+        on_vector = [(2, 0, 512), (2, 512, 512), (3, 0, 512), (3, 512, 256), (3, 768, 256)]
         for n, c0, count in on_gpsimd:
             finish(n, c0, count, nc.gpsimd, None)
         results = keep.tile(

@@ -24,9 +24,11 @@ PART = 128
 GATHER = 512
 SLICES = (128, 128, 256, 256, 256)
 HALF = N // 2
+SHARED = 4 * T + 4 * H
 RUN = 4
 PER_COLUMN = 16
-A_BANKS, Y_BANKS = 5, 3
+A_BANKS = (0, 1, 2, 3, 4, 0, 1, 2, 3, 4, 0, 2, 3, 4, 6, 7)
+Y_BANKS = (5, 6, 7, 1, 5, 1, 0, 2, 3, 4, 6)
 
 
 def tile_list_sorted_poem_gates_kernel(
@@ -37,8 +39,8 @@ def tile_list_sorted_poem_gates_kernel(
         keep = ctx.enter_context(tc.tile_pool(name="keep", bufs=1))
         reuse = ctx.enter_context(tc.tile_pool(name="reuse", bufs=1))
         work = ctx.enter_context(tc.tile_pool(name="work", bufs=2))
-        psum_a = ctx.enter_context(tc.psum_pool(name="psum_a", bufs=A_BANKS))
-        psum_y = ctx.enter_context(tc.psum_pool(name="psum_y", bufs=Y_BANKS))
+        psum = ctx.enter_context(tc.psum_pool(name="psum", bufs=1))
+        a_made, y_made = [], []
 
         offs_sb = keep.tile([P, S // PER_COLUMN], U16, name="offs_sb")
         offs2_sb = keep.tile([P, S // PER_COLUMN], U16, name="offs2_sb")
@@ -115,23 +117,21 @@ def tile_list_sorted_poem_gates_kernel(
         wgo_sb = late[:, 2 * w2_width : 2 * w2_width + S]
         nc.sync.dma_start(wgo_sb, wgo)
 
-        def quantise_w2(half, b, tag, on_scalar=False):
-            woven = keep.tile([P, HALF, PACK], BF16, name="w2_bf", tag=tag, align_bytes=64)
-            woven_view = woven[:].rearrange("p (c i) t -> p c t i", i=4)
-            raw_view = w2_raw[half][b].rearrange("p (t c i) -> p c t i", t=PACK, i=4)
-            if on_scalar:
-                nc.scalar.copy(woven_view, raw_view)
-            else:
-                nc.vector.tensor_copy(woven_view, raw_view)
-            words = keep.tile([P, HALF], U32, name="w2_w%d%d" % (half, b), align_bytes=64)
-            scales = keep.tile([P, HALF], U8, name="w2_sc%d%d" % (half, b), align_bytes=64)
-            nc.vector.quantize_mx(
-                out=words[:].bitcast(FP8X4), scales=scales[:], in_=woven[:].rearrange("p n t -> p (n t)")
-            )
+        def weave_w2(copy, woven, half, b, c0, count):
+            raw = w2_raw[half][b].rearrange("p (t n) -> p t n", t=PACK)[:, :, c0 : c0 + count]
+            copy(woven.rearrange("p (c i) t -> p c t i", i=RUN), raw.rearrange("p t (c i) -> p c t i", i=RUN))
+
+        def quantise(words, scales, woven):
+            nc.vector.quantize_mx(out=words.bitcast(FP8X4), scales=scales, in_=woven.rearrange("p n t -> p (n t)"))
+
+        def quantised_tiles(name, count):
+            words = keep.tile([P, count], U32, name=name + "_w", align_bytes=64)
+            scales = keep.tile([P, count], U8, name=name + "_sc", align_bytes=64)
             return words, scales
 
         def first_product(b, parts):
-            bank = psum_a.tile([P, BANK], F32, name="a_bank")
+            bank = psum.tile([P, BANK], F32, name="a_bank", tag="bank%d" % A_BANKS[len(a_made)])
+            a_made.append(bank)
             for a in range(2):
                 for place, (t, j) in enumerate(parts):
                     c0 = PASS * b + P * t
@@ -146,14 +146,21 @@ def tile_list_sorted_poem_gates_kernel(
                     )
             return bank
 
-        def make_h_on_vector(h_out, j0, b, engine):
-            bank = first_product(b, [(t, j0) for t in range(PACK)])
-            woven_a = bank[:].rearrange("p (t j) -> p j t", t=PACK)
-            tanh_a = work.tile([P, PART, PACK], F32, name="tanh_a", bufs=4)
-            nc.scalar.activation(tanh_a[:], woven_a, ACT.Tanh)
-            total = keep.tile([P, PART, PACK], F32, name="total", tag="total%d_%d" % (j0, b), align_bytes=64)
-            nc.vector.tensor_tensor(total[:], woven_a, tanh_a[:], ALU.add)
-            engine.tensor_tensor(h_out, total[:], gain_sb[:, b, :].unsqueeze(1).to_broadcast([P, PART, PACK]), ALU.mult)
+        def sum_on_vector(j0, bs, width, total=None):
+            if total is None:
+                total = keep.tile([P, len(bs), width, PACK], F32, name="total%d_%d" % (j0, bs[-1]), align_bytes=64)
+            for b in bs:
+                for n0 in range(0, width, PART):
+                    bank = first_product(b, [(t, j0 + n0) for t in range(PACK)])
+                    woven_a = bank[:].rearrange("p (t j) -> p j t", t=PACK)
+                    tanh_a = work.tile([P, PART, PACK], F32, name="tanh_a", bufs=4)
+                    nc.scalar.activation(tanh_a[:], woven_a, ACT.Tanh)
+                    nc.vector.tensor_tensor(total[:, b - bs[0], n0 : n0 + PART, :], woven_a, tanh_a[:], ALU.add)
+            return total
+
+        def times_gain(engine, h_out, total, b0):
+            factor = gain_sb[:, b0 : b0 + total.shape[1], :].unsqueeze(2).to_broadcast(total.shape)
+            engine.tensor_tensor(h_out, total[:], factor, ALU.mult)
 
         def make_h(h_out, j0, width, b, adder):
             gain_a = keep.tile([P, width // RUN, PACK, RUN], F32, name="gain_a", tag="gain_a%d_%d" % (j0, b), align_bytes=64)
@@ -180,19 +187,20 @@ def tile_list_sorted_poem_gates_kernel(
             )
 
         pages = [keep.tile([P, S], F32, name="page%d" % n) for n in range(4)]
-        h_q = []
         starts = [sum(SLICES[:k]) for k in range(len(SLICES))]
+        h_q = []
+        w2_q = {}
 
         def second_product(parts):
-            bank = psum_y.tile([P, sum(SLICES[k] for n, k in parts)], F32, name="y_bank")
+            bank = psum.tile([P, sum(SLICES[k] for n, k in parts)], F32, name="y_bank", tag="bank%d" % Y_BANKS[len(y_made)])
+            y_made.append(bank)
             at = 0
             for n, k in parts:
-                c0 = P * (n % 2)
                 for b in range(2):
                     nc.tensor.matmul_mx(
                         out=bank[:, at : at + SLICES[k]],
-                        lhsT=w2_q[n // 2][b][0][:, c0 : c0 + P].bitcast(FP8X4),
-                        lhsT_scale=w2_q[n // 2][b][1][:, c0 : c0 + P],
+                        lhsT=w2_q[n, b][0].bitcast(FP8X4),
+                        lhsT_scale=w2_q[n, b][1],
                         rhs=h_q[k][0][:, b, :].bitcast(FP8X4),
                         rhs_scale=h_q[k][1][:, b, :],
                         start=(b == 0),
@@ -204,119 +212,127 @@ def tile_list_sorted_poem_gates_kernel(
         def places(j0, width):
             return offs2_sb[:, j0 // PER_COLUMN : (j0 + width) // PER_COLUMN]
 
-        def weigh(how, y_psum, count, j0, width, tag):
-            factor = wgo_sb[:, j0 : j0 + width]
-            if how == "V":
-                weighted = keep.tile([P, count, width], F32, name="weighted", tag=tag, align_bytes=64)
-                nc.vector.tensor_tensor(
-                    weighted[:], y_psum.rearrange("p (m j) -> p m j", m=count), factor.unsqueeze(1).to_broadcast([P, count, width]), ALU.mult
-                )
-                return weighted
-            if how == "H":
-                weighted = keep.tile([P, count, width], F32, name="weighted", tag=tag, align_bytes=64)
-                for m in range(count):
-                    nc.gpsimd.tensor_tensor(weighted[:, m, :], y_psum[:, m, :], factor, ALU.mult)
-                return weighted
-            y_sb = keep.tile([P, count, width], F32, name="y_sb", tag=tag, align_bytes=64)
-            nc.scalar.copy(y_sb[:].rearrange("p m j -> p (m j)"), y_psum)
-            if how == "F":
-                return y_sb
-            weighted = keep.tile([P, count, width], F32, name="weighted", tag="from_" + tag, align_bytes=64)
-            for m in range(count):
-                nc.gpsimd.tensor_tensor(weighted[:, m, :], y_sb[:, m, :], factor, ALU.mult)
+        def weigh(y_psum, j0, width, tag):
+            count = y_psum.shape[1] // width
+            weighted = keep.tile([P, count, width], F32, name="weighted", tag=tag, align_bytes=64)
+            factor = wgo_sb[:, j0 : j0 + width].unsqueeze(1).to_broadcast([P, count, width])
+            nc.vector.tensor_tensor(weighted[:], y_psum.rearrange("p (m j) -> p m j", m=count), factor, ALU.mult)
             return weighted
 
-        def put_back(how, values, page_list, j0, width):
-            for m, n in enumerate(page_list):
-                window = pages[n][:].indirect(places(j0, width))
-                if how == "F":
-                    nc.vector.tensor_tensor(window, values[:, m, :], wgo_sb[:, j0 : j0 + width], ALU.mult)
-                else:
-                    nc.vector.tensor_copy(window, values[:, m, :])
+        def copy_out(y_psum, tag):
+            y_sb = keep.tile([P, y_psum.shape[1]], F32, name="y_sb", tag=tag, align_bytes=64)
+            nc.scalar.copy(y_sb[:], y_psum)
+            return y_sb
 
-        def finish(n, c0, width, engine, tag):
+        def weigh_on_gpsimd(y_psum, j0, tag):
+            width = y_psum.shape[1]
+            y_sb = copy_out(y_psum, tag)
+            weighted = keep.tile([P, 1, width], F32, name="weighted", tag="from_" + tag, align_bytes=64)
+            nc.gpsimd.tensor_tensor(weighted[:, 0, :], y_sb[:], wgo_sb[:, j0 : j0 + width], ALU.mult)
+            return weighted
+
+        def put_back(first_page, weighted, j0):
+            for m in range(weighted.shape[1]):
+                window = pages[first_page + m][:].indirect(places(j0, weighted.shape[2]))
+                nc.vector.tensor_copy(window, weighted[:, m, :])
+
+        def finish(n, c0, width, engine, result):
             gate = keep.tile([P, width], F32, name="gate", tag="gate%d_%d" % (n, c0), align_bytes=64)
             nc.scalar.activation(gate[:], pages[n][:, c0 : c0 + width], ACT.Sigmoid)
-            if tag is None:
-                result = x0_sb[n][:, c0 : c0 + width]
-            else:
-                result = tag
             engine.tensor_tensor(result, gate[:], x0_sb[n][:, c0 : c0 + width], ALU.mult)
             nc.sync.dma_start(out[P * n : P * (n + 1), c0 : c0 + width], result)
 
-        V, G = nc.vector, nc.gpsimd
-        units = [[(0, 128, 0, "BV"), (0, 128, 1, "BV")], [(0, 128, 0, "BG"), (0, 128, 1, "BG")], [(0, 128, 0, "BG"), (128, 128, 0, "BG"), (0, 256, 1, G)], [(0, 256, 0, G), (0, 256, 1, G)], [(0, 256, 0, G), (0, 128, 1, G), (128, 128, 1, G)]]
-        plan = [
- [[("V", [0], [0], False), ("V", [1], [0], True)]],
- [[("V", [0, 1], [1], False)], [("V", [3], [0, 1], False)], [("V", [2], [0, 1], True)]],
- [[("V", [0, 1], [2], False)], [("V", [3], [2], False), ("V", [2], [2], True)]],
- [[("V", [0, 1], [3], False)], [("F", [2], [3], True)]],
- [[("V", [0, 1], [4], False)], [("G", [2], [4], False)], [("G", [3], [3, 4], False)]],
-]
-        w2_q = [[None, None], [None, None]]
-        pieces = {(0, 0): [(0, 0, False, "a")], (0, 9): [(0, 1, True, "b")]}
-        joined = {0: (1, 0), 1: (1, 1)}
-        held = []
-        gate_tag = "h_bf0"
-        for index, width in enumerate(SLICES):
-            j0 = starts[index]
-            extra = HALF if index in joined else 0
-            both = keep.tile([P, 2 * width + extra, PACK], BF16, name="h_bf", tag="h_bf0" if index == 0 else gate_tag, align_bytes=64)
-            h_bf = both[:, 0 : 2 * width, :].rearrange("p (b n) t -> p b n t", b=2)
-            for u, (n0, count, b, adder) in enumerate(units[index]):
-                for half, pb, on_scalar, tag in pieces.get((index, u), []):
-                    w2_q[half][pb] = quantise_w2(half, pb, tag, on_scalar)
-                if adder in ("BV", "BG"):
-                    make_h_on_vector(h_bf[:, b, n0 : n0 + count], j0 + n0, b, V if adder == "BV" else G)
-                    last_sum = "total%d_%d" % (j0 + n0, b)
-                else:
-                    last_sum = "gain_a%d_%d" % (j0 + n0, b)
-                    make_h(h_bf[:, b, n0 : n0 + count], j0 + n0, count, b, adder)
-            if extra:
-                half, pb = joined[index]
-                nc.scalar.copy(
-                    both[:, 2 * width :, :].rearrange("p (c i) t -> p c t i", i=4),
-                    w2_raw[half][pb].rearrange("p (t c i) -> p c t i", t=PACK, i=4),
-                )
-            late_values = [weigh(how, y, len(ps), i0, w, last_sum) for how, y, ps, i0, w in held]
-            h_w = keep.tile([P, 2 * width + extra], U32, name="h_w%d" % index, align_bytes=64)
-            h_sc = keep.tile([P, 2 * width + extra], U8, name="h_sc%d" % index, align_bytes=64)
-            nc.vector.quantize_mx(out=h_w[:].bitcast(FP8X4), scales=h_sc[:], in_=both[:].rearrange("p n t -> p (n t)"))
-            h_q.append([tile[:, 0 : 2 * width].rearrange("p (b n) -> p b n", b=2) for tile in (h_w, h_sc)])
-            if extra:
-                w2_q[half][pb] = (h_w[:, 2 * width :], h_sc[:, 2 * width :])
-            for half, pb, on_scalar, tag in pieces.get((index, 9), []):
-                w2_q[half][pb] = quantise_w2(half, pb, tag, on_scalar)
-            if index == 0:
-                x0_all = reuse.tile([P, 4 * S], F32, name="x0_all", offset=0, align_bytes=64)
-                x0_sb = [x0_all[:, S * n : S * (n + 1)] for n in range(4)]
-                for n in range(4):
-                    nc.sync.dma_start(x0_sb[n], x0[P * n : P * (n + 1), :])
-            for (how, y, ps, i0, w), values in zip(held, late_values):
-                put_back(how, values, ps, i0, w)
-            held = []
-            for number, groups in enumerate(plan[index]):
-                bank = second_product([(n, k) for how, ps, ks, hold in groups for n in ps for k in ks])
-                at = 0
-                for place, (how, ps, ks, hold) in enumerate(groups):
-                    w = sum(SLICES[k] for k in ks)
-                    y = bank[:, at : at + w * len(ps)]
-                    at = at + w * len(ps)
-                    if how == "H":
-                        y = weigh("F", y, len(ps), starts[ks[0]], w, "y_kept%d" % index)
-                    if hold:
-                        held.append((how, y, ps, starts[ks[0]], w))
-                    else:
-                        put_back(how, weigh(how, y, len(ps), starts[ks[0]], w, "w%d_%d_%d" % (index, number, place)), ps, starts[ks[0]], w)
+        def by_pass(tile, c0, width):
+            return tile[:, c0 : c0 + 2 * width].rearrange("p (b n) -> p b n", b=2)
 
+        woven = keep.tile([P, HALF, PACK], BF16, name="w2_first", align_bytes=64)
+        weave_w2(nc.vector.tensor_copy, woven[:], 0, 0, 0, HALF)
+        words, scales = quantised_tiles("w2_first", HALF)
+        quantise(words[:], scales[:], woven[:])
+        for n in range(2):
+            w2_q[n, 0] = (words[:, P * n : P * (n + 1)], scales[:, P * n : P * (n + 1)])
+        woven = keep.tile([P, 4 * P, PACK], BF16, name="woven", tag="woven", align_bytes=64)
+        for b in range(2):
+            times_gain(nc.vector, woven[:, P * b : P * (b + 1), :].unsqueeze(1), sum_on_vector(0, [b], P), b)
+        total = reuse.tile([P, 2, P, PACK], F32, name="total_second", offset=SHARED, align_bytes=64)
+        sum_on_vector(P, [0, 1], P, total)
+        weave_w2(nc.scalar.copy, woven[:, 2 * P :, :], 0, 1, 0, HALF)
+        words, scales = quantised_tiles("first", 4 * P)
+        quantise(words[:], scales[:], woven[:])
+        h_q.append([by_pass(tile, 0, P) for tile in (words, scales)])
+        for n in range(2):
+            w2_q[n, 1] = (words[:, P * (2 + n) : P * (3 + n)], scales[:, P * (2 + n) : P * (3 + n)])
+        x0_all = reuse.tile([P, 4 * S], F32, name="x0_all", offset=0, align_bytes=64)
+        x0_sb = [x0_all[:, S * n : S * (n + 1)] for n in range(4)]
+        for n in range(4):
+            nc.sync.dma_start(x0_sb[n], x0[P * n : P * (n + 1), :])
+
+        woven = keep.tile([P, 2, P, PACK], BF16, name="woven", tag="woven", align_bytes=64)
+        times_gain(nc.gpsimd, woven[:], total, 0)
+        bank = second_product([(0, 0), (1, 0)])
+        put_back(0, weigh(bank[:, 0:P], 0, P, "page0_first"), 0)
+        total = sum_on_vector(2 * P, [0], 2 * P)
+        w2_rest = keep.tile([P, 2, HALF, PACK], BF16, name="w2_rest", align_bytes=64)
+        for b in range(2):
+            weave_w2(nc.scalar.copy, w2_rest[:, b], 1, b, 0, HALF)
+        held = reuse.tile([P, 1, P], F32, name="held_first", offset=SHARED + 4 * N, align_bytes=64)
+        nc.vector.tensor_tensor(held[:, 0, :], bank[:, P:], wgo_sb[:, 0:P], ALU.mult)
+        words = reuse.tile([P, N], U32, name="w2_rest_w", offset=SHARED, align_bytes=64)
+        scales = keep.tile([P, N], U8, name="w2_rest_sc", align_bytes=64)
+        quantise(words[:], scales[:], w2_rest[:].rearrange("p b n t -> p (b n) t"))
+        for n in range(2, 4):
+            for b in range(2):
+                cols = slice(HALF * b + P * (n - 2), HALF * b + P * (n - 1))
+                w2_q[n, b] = (words[:, cols], scales[:, cols])
+        words, scales = quantised_tiles("second", 2 * P)
+        quantise(words[:], scales[:], woven[:].rearrange("p b n t -> p (b n) t"))
+        h_q.append([by_pass(tile, 0, P) for tile in (words, scales)])
+        woven = keep.tile([P, 2, 2 * P, PACK], BF16, name="woven", tag="woven", align_bytes=64)
+        times_gain(nc.gpsimd, woven[:, 0:1], total, 0)
+        make_h(woven[:, 1], 2 * P, 2 * P, 1, nc.gpsimd)
+        put_back(1, held, 0)
+        put_back(0, weigh(second_product([(0, 1), (1, 1)])[:], P, P, "first_two"), P)
+        put_back(3, weigh(second_product([(3, 0), (3, 1)])[:], 0, 2 * P, "fourth"), 0)
+        held_y = second_product([(2, 0), (2, 1)])[:]
+
+        last = len(SLICES) - 1
+        for index in range(2, last + 1):
+            j0, width = starts[index], SLICES[index]
+            n0 = 0
+            if index > 2:
+                woven = keep.tile([P, 2, width, PACK], BF16, name="woven", tag="woven", align_bytes=64)
+                make_h(woven[:, 0], j0, width, 0, nc.gpsimd)
+                step = width
+                for n0 in range(0, width, step):
+                    make_h(woven[:, 1, n0 : n0 + step], j0 + n0, step, 1, nc.gpsimd)
+            last_sum = "gain_a%d_1" % (j0 + n0)
+            held = copy_out(held_y, last_sum) if index == last else weigh(held_y, j0 - width, width, last_sum)
+            words, scales = quantised_tiles("h%d" % index, 2 * width)
+            quantise(words[:], scales[:], woven[:].rearrange("p b n t -> p (b n) t"))
+            h_q.append([by_pass(tile, 0, width) for tile in (words, scales)])
+            if index == last:
+                window = pages[2][:].indirect(places(j0 - width, width))
+                nc.vector.tensor_tensor(window, held[:], wgo_sb[:, j0 - width : j0], ALU.mult)
+            else:
+                put_back(2, held, j0 - width)
+            put_back(0, weigh(second_product([(0, index), (1, index)])[:], j0, width, "first_two"), j0)
+            if index == 2:
+                bank = second_product([(3, index), (2, index)])
+                put_back(3, weigh(bank[:, 0:width], j0, width, "fourth"), j0)
+                held_y = bank[:, width:]
+            elif index < last:
+                held_y = second_product([(2, index)])[:]
+
+        put_back(2, weigh_on_gpsimd(second_product([(2, last)])[:], j0, "y_third"), j0)
+        put_back(3, weigh_on_gpsimd(second_product([(3, last - 1), (3, last)])[:], j0 - width, "y_fourth"), j0 - width)
         on_gpsimd = [(0, 0, 512), (0, 512, 512), (1, 0, 512), (1, 512, 512)]
         on_vector = [(2, 0, 512), (2, 512, 512), (3, 0, 512), (3, 512, 256), (3, 768, 256)]
         for n, c0, count in on_gpsimd:
-            finish(n, c0, count, nc.gpsimd, None)
+            finish(n, c0, count, nc.gpsimd, x0_sb[n][:, c0 : c0 + count])
         results = keep.tile(
             [P, sum(piece[2] for piece in on_vector)], F32, name="results", tag="gate%d_%d" % on_gpsimd[-1][:2], align_bytes=64
         )
         done = 0
-        for n, c0, width in on_vector:
-            finish(n, c0, width, nc.vector, results[:, done : done + width])
-            done = done + width
+        for n, c0, count in on_vector:
+            finish(n, c0, count, nc.vector, results[:, done : done + count])
+            done = done + count

@@ -24,7 +24,7 @@ PART = 128
 GATHER = 512
 SLICES = (128, 128, 256, 256, 256)
 HALF = N // 2
-SHARED = 4 * T + 4 * H
+SHARED = 4 * T + 64 + 4 * H
 RUN = 4
 PER_COLUMN = 16
 A_BANKS = (0, 1, 2, 3, 4, 0, 1, 2, 3, 4, 0, 2, 3, 4, 6, 7)
@@ -78,13 +78,15 @@ def tile_list_sorted_poem_gates_kernel(
 
         move_rows(0)
 
-        w1_w = reuse.tile([P, 2, 2 * H], U8, name="w1_w", offset=4 * T, align_bytes=64)
+        w1_w = reuse.tile([P, 2, 2 * H], U8, name="w1_w", offset=4 * T + 64, align_bytes=64)
         nc.vector.tensor_copy(
             w1_w[:].rearrange("p a c -> p (a c)").bitcast(U16).rearrange("p (g t h l) -> p g h t l", g=4, t=4, l=8),
             w1_raw[:].rearrange("p a c -> p (a c)").bitcast(U16).rearrange("p (g h l t) -> p g h t l", g=4, t=4, l=8),
         )
         tab_w1 = reuse.tile([P, T], I32, name="tab_w1", offset=0, align_bytes=64)
         nc.sync.dma_start(tab_w1[:], tab_words[1].rearrange("p t i -> p (t i)").bitcast(I32))
+        gain_sb = reuse.tile([P, 2, PACK], F32, name="gain_sb", offset=4 * T, align_bytes=64)
+        nc.sync.dma_start(gain_sb[:], gain.rearrange("(b p t) -> p b t", b=2, t=PACK))
         move_rows(1)
 
         def gather_words(words, window, j0):
@@ -106,10 +108,10 @@ def tile_list_sorted_poem_gates_kernel(
 
         w2_rows = w2.rearrange("(b p t) (half n) -> half b p t n", b=2, t=PACK, half=2)
         w2_width = PACK * HALF
-        early = keep.tile([P, 2 * w2_width + 8], F32, name="early", tag="after_w1_raw", align_bytes=64)
+        early = keep.tile([P, 2 * w2_width], F32, name="early", tag="after_w1_raw", align_bytes=64)
         late = keep.tile([P, 2 * w2_width + S], F32, name="late", tag="after_tab_w0", align_bytes=64)
-        gain_sb = early[:, 2 * w2_width :].rearrange("p (b t) -> p b t", b=2)
-        nc.sync.dma_start(gain_sb, gain.rearrange("(b p t) -> p b t", b=2, t=PACK))
+        gain_woven = keep.tile([P, 2, PART, PACK], F32, name="gain_woven", align_bytes=64)
+        nc.scalar.copy(gain_woven[:], gain_sb[:].unsqueeze(2).to_broadcast([P, 2, PART, PACK]))
         w2_raw = [[tile[:, w2_width * b : w2_width * (b + 1)] for b in range(2)] for tile in (early, late)]
         for half in range(2):
             for b in range(2):
@@ -159,8 +161,14 @@ def tile_list_sorted_poem_gates_kernel(
             return total
 
         def times_gain(engine, h_out, total, b0):
-            factor = gain_sb[:, b0 : b0 + total.shape[1], :].unsqueeze(2).to_broadcast(total.shape)
-            engine.tensor_tensor(h_out, total[:], factor, ALU.mult)
+            passes, parts = total.shape[1], total.shape[2] // PART
+            factor = gain_woven[:, b0 : b0 + passes].rearrange("p b n t -> p b (n t)").unsqueeze(2)
+            engine.tensor_tensor(
+                h_out.rearrange("p b (m n) t -> p b m (n t)", m=parts),
+                total[:].rearrange("p b (m n) t -> p b m (n t)", m=parts),
+                factor.to_broadcast([P, passes, parts, PART * PACK]),
+                ALU.mult,
+            )
 
         def make_h(h_out, j0, width, b, adder):
             gain_a = keep.tile([P, width // RUN, PACK, RUN], F32, name="gain_a", tag="gain_a%d_%d" % (j0, b), align_bytes=64)

@@ -323,10 +323,13 @@ def tile_list_sorted_poem_gates_kernel(
                 nc.vector.tensor_tensor(window, held[:], wgo_sb[:, j0 - width : j0], ALU.mult)
             else:
                 put_back(2, held, j0 - width)
-            put_back(0, weigh(second_product([(0, index), (1, index)])[:], j0, width, "first_two"), j0)
+            bank = second_product([(0, index), (1, index)])
+            first_two = [weigh(bank[:, width * n : width * (n + 1)], j0, width, "page%d_next" % n) for n in range(2)]
+            for n in range(2):
+                put_back(n, first_two[n], j0)
             if index == 2:
                 bank = second_product([(3, index), (2, index)])
-                put_back(3, weigh(bank[:, 0:width], j0, width, "fourth"), j0)
+                put_back(3, weigh_on_gpsimd(bank[:, 0:width], j0, "y_mid"), j0)
                 held_y = bank[:, width:]
             elif index < last:
                 held_y = second_product([(2, index)])[:]

@@ -329,7 +329,7 @@ def tile_list_sorted_poem_gates_kernel(
                 put_back(n, first_two[n], j0)
             if index == 2:
                 bank = second_product([(3, index), (2, index)])
-                put_back(3, weigh_on_gpsimd(bank[:, 0:width], j0, "y_mid"), j0)
+                put_back(3, weigh(bank[:, 0:width], j0, width, "fourth"), j0)
                 held_y = bank[:, width:]
             elif index < last:
                 held_y = second_product([(2, index)])[:]

@@ -24,11 +24,15 @@ PART = 128
 GATHER = 512
 SLICES = (128, 128, 256, 256, 256)
 HALF = N // 2
-SHARED = 4 * T + 64 + 4 * H
+SCALE_ROWS = 96
+PLANE = S + H
+GAIN_AT = 4 * T
+W1_AT = GAIN_AT + 64
+SUMS_AT = W1_AT + 4 * H
+TANH_BUFFERS, TERM_BUFFERS = 4, 6
 RUN = 4
 PER_COLUMN = 16
-A_BANKS = (0, 1, 2, 3, 4, 0, 1, 2, 3, 4, 0, 2, 3, 4, 6, 7)
-Y_BANKS = (5, 6, 7, 1, 5, 1, 0, 2, 3, 4, 6)
+A_BANKS, Y_BANKS = 5, 3
 
 
 def tile_list_sorted_poem_gates_kernel(
@@ -39,29 +43,29 @@ def tile_list_sorted_poem_gates_kernel(
         keep = ctx.enter_context(tc.tile_pool(name="keep", bufs=1))
         reuse = ctx.enter_context(tc.tile_pool(name="reuse", bufs=1))
         work = ctx.enter_context(tc.tile_pool(name="work", bufs=2))
-        psum = ctx.enter_context(tc.psum_pool(name="psum", bufs=1))
-        a_made, y_made = [], []
+        psum_a = ctx.enter_context(tc.psum_pool(name="psum_a", bufs=A_BANKS))
+        psum_y = ctx.enter_context(tc.psum_pool(name="psum_y", bufs=Y_BANKS))
 
         offs_sb = keep.tile([P, S // PER_COLUMN], U16, name="offs_sb")
         offs2_sb = keep.tile([P, S // PER_COLUMN], U16, name="offs2_sb")
         tab_sc = keep.tile([P, T], U8, name="tab_sc", align_bytes=64)
         w1_sc_raw = keep.tile([P, H], U8, name="w1_sc_raw", align_bytes=64)
-        planes = keep.tile([P, 2 * (S + H)], U8, name="planes", align_bytes=64)
-        nc.vector.memset(tab_sc[0:96, :].bitcast(I32), 0)
-        nc.vector.memset(w1_sc_raw[0:96, :].bitcast(I32), 0)
+        planes = keep.tile([P, 2 * PLANE], U8, name="planes", align_bytes=64)
+        nc.vector.memset(tab_sc[0:SCALE_ROWS, :].bitcast(I32), 0)
+        nc.vector.memset(w1_sc_raw[0:SCALE_ROWS, :].bitcast(I32), 0)
         nc.vector.memset(planes[:].bitcast(I32), 0)
 
         nc.sync.dma_start(offs_sb[:], offs)
-        nc.sync.dma_start(tab_sc[96:128, :].bitcast(I32), tab_scales.bitcast(I32).rearrange("a q t -> (a q) t"))
-        nc.sync.dma_start(w1_sc_raw[96:128, :].bitcast(I32), w1_scales.bitcast(I32).rearrange("a q c -> (a q) c"))
+        nc.sync.dma_start(tab_sc[SCALE_ROWS:P, :].bitcast(I32), tab_scales.bitcast(I32).rearrange("a q t -> (a q) t"))
+        nc.sync.dma_start(w1_sc_raw[SCALE_ROWS:P, :].bitcast(I32), w1_scales.bitcast(I32).rearrange("a q c -> (a q) c"))
         nc.sync.dma_start(offs2_sb[:], offs2)
         w1_raw = keep.tile([P, 2, 2 * H], U8, name="w1_raw", tag="after_w1_raw", align_bytes=64)
         nc.sync.dma_start(w1_raw[:].bitcast(I32), w1_words.bitcast(I32).rearrange("a p c -> p a c"))
         tab_w0 = keep.tile([P, T], I32, name="tab_w0", tag="after_tab_w0", align_bytes=64)
         nc.sync.dma_start(tab_w0[:], tab_words[0].rearrange("p t i -> p (t i)").bitcast(I32))
-        v_sc_rows = reuse.tile([P, S], U8, name="v_sc_rows", offset=4 * T - S // 2, align_bytes=64)
+        v_sc_rows = reuse.tile([P, S], U8, name="v_sc_rows", offset=GAIN_AT - S // 2, align_bytes=64)
         nc.vector.tensor_copy(v_sc_rows[:], tab_sc[:].indirect(offs_sb[:]))
-        sc_rows = keep.tile([P, S + H], U8, name="sc_rows", align_bytes=64)
+        sc_rows = keep.tile([P, PLANE], U8, name="sc_rows", align_bytes=64)
         nc.vector.tensor_copy(
             sc_rows[:, S:].rearrange("p (g t h l) -> p g h t l", g=2, t=4, l=16),
             w1_sc_raw[:].rearrange("p (g h l t) -> p g h t l", g=2, t=4, l=16),
@@ -69,23 +73,23 @@ def tile_list_sorted_poem_gates_kernel(
         nc.vector.tensor_copy(sc_rows[:, 0:S].bitcast(I32), v_sc_rows[:].bitcast(I32))
 
         def move_rows(a):
-            for q in range(4):
-                row = 96 + 16 * a + 4 * q
+            for quadrant in range(4):
+                row = SCALE_ROWS + 16 * a + 4 * quadrant
                 nc.sync.dma_start(
-                    planes[32 * q : 32 * q + 4, (S + H) * a : (S + H) * (a + 1)].bitcast(I32),
+                    planes[32 * quadrant : 32 * quadrant + 4, PLANE * a : PLANE * (a + 1)].bitcast(I32),
                     sc_rows[row : row + 4, :].bitcast(I32),
                 )
 
         move_rows(0)
 
-        w1_w = reuse.tile([P, 2, 2 * H], U8, name="w1_w", offset=4 * T + 64, align_bytes=64)
+        w1_w = reuse.tile([P, 2, 2 * H], U8, name="w1_w", offset=W1_AT, align_bytes=64)
         nc.vector.tensor_copy(
             w1_w[:].rearrange("p a c -> p (a c)").bitcast(U16).rearrange("p (g t h l) -> p g h t l", g=4, t=4, l=8),
             w1_raw[:].rearrange("p a c -> p (a c)").bitcast(U16).rearrange("p (g h l t) -> p g h t l", g=4, t=4, l=8),
         )
         tab_w1 = reuse.tile([P, T], I32, name="tab_w1", offset=0, align_bytes=64)
         nc.sync.dma_start(tab_w1[:], tab_words[1].rearrange("p t i -> p (t i)").bitcast(I32))
-        gain_sb = reuse.tile([P, 2, PACK], F32, name="gain_sb", offset=4 * T, align_bytes=64)
+        gain_sb = reuse.tile([P, 2, PACK], F32, name="gain_sb", offset=GAIN_AT, align_bytes=64)
         nc.sync.dma_start(gain_sb[:], gain.rearrange("(b p t) -> p b t", b=2, t=PACK))
         move_rows(1)
 
@@ -119,9 +123,9 @@ def tile_list_sorted_poem_gates_kernel(
         wgo_sb = late[:, 2 * w2_width : 2 * w2_width + S]
         nc.sync.dma_start(wgo_sb, wgo)
 
-        def weave_w2(copy, woven, half, b, c0, count):
-            raw = w2_raw[half][b].rearrange("p (t n) -> p t n", t=PACK)[:, :, c0 : c0 + count]
-            copy(woven.rearrange("p (c i) t -> p c t i", i=RUN), raw.rearrange("p t (c i) -> p c t i", i=RUN))
+        def weave_w2(copy, woven, half, b):
+            raw = w2_raw[half][b].rearrange("p (t c i) -> p c t i", t=PACK, i=RUN)
+            copy(woven.rearrange("p (c i) t -> p c t i", i=RUN), raw)
 
         def quantise(words, scales, woven):
             nc.vector.quantize_mx(out=words.bitcast(FP8X4), scales=scales, in_=woven.rearrange("p n t -> p (n t)"))
@@ -132,33 +136,30 @@ def tile_list_sorted_poem_gates_kernel(
             return words, scales
 
         def first_product(b, parts):
-            bank = psum.tile([P, BANK], F32, name="a_bank", tag="bank%d" % A_BANKS[len(a_made)])
-            a_made.append(bank)
+            bank = psum_a.tile([P, BANK], F32, name="a_bank")
             for a in range(2):
                 for place, (t, j) in enumerate(parts):
                     c0 = PASS * b + P * t
                     nc.tensor.matmul_mx(
                         out=bank[:, PART * place : PART * (place + 1)],
                         lhsT=w1_w[:, a, 2 * c0 : 2 * (c0 + P)].bitcast(FP4X4),
-                        lhsT_scale=planes[:, (S + H) * a + S + c0 : (S + H) * a + S + c0 + P],
+                        lhsT_scale=planes[:, PLANE * a + S + c0 : PLANE * a + S + c0 + P],
                         rhs=v_w[a, j - j % GATHER][:, j % GATHER : j % GATHER + PART].bitcast(FP8X4),
-                        rhs_scale=planes[:, (S + H) * a + j : (S + H) * a + j + PART],
+                        rhs_scale=planes[:, PLANE * a + j : PLANE * a + j + PART],
                         start=(a == 0 and place == 0),
                         stop=(a == 1 and place == len(parts) - 1),
                     )
             return bank
 
-        def sum_on_vector(j0, bs, width, total=None):
-            if total is None:
-                total = keep.tile([P, len(bs), width, PACK], F32, name="total%d_%d" % (j0, bs[-1]), align_bytes=64)
+        def sum_on_vector(total, j0, bs):
+            width = total.shape[2]
             for b in bs:
                 for n0 in range(0, width, PART):
                     bank = first_product(b, [(t, j0 + n0) for t in range(PACK)])
                     woven_a = bank[:].rearrange("p (t j) -> p j t", t=PACK)
-                    tanh_a = work.tile([P, PART, PACK], F32, name="tanh_a", bufs=4)
+                    tanh_a = work.tile([P, PART, PACK], F32, name="tanh_a", bufs=TANH_BUFFERS)
                     nc.scalar.activation(tanh_a[:], woven_a, ACT.Tanh)
                     nc.vector.tensor_tensor(total[:, b - bs[0], n0 : n0 + PART, :], woven_a, tanh_a[:], ALU.add)
-            return total
 
         def times_gain(engine, h_out, total, b0):
             passes, parts = total.shape[1], total.shape[2] // PART
@@ -170,14 +171,14 @@ def tile_list_sorted_poem_gates_kernel(
                 ALU.mult,
             )
 
-        def make_h(h_out, j0, width, b, adder):
+        def make_h(h_out, j0, width, b):
             gain_a = keep.tile([P, width // RUN, PACK, RUN], F32, name="gain_a", tag="gain_a%d_%d" % (j0, b), align_bytes=64)
-            gain_tanh = work.tile([P, width // RUN, PACK, RUN], F32, name="gain_tanh", bufs=6)
+            gain_tanh = work.tile([P, width // RUN, PACK, RUN], F32, name="gain_tanh", bufs=TERM_BUFFERS)
             per_bank = BANK // width
             for t0 in range(0, PACK, per_bank):
                 ts = range(t0, t0 + per_bank)
                 bank = first_product(b, [(t, j) for t in ts for j in range(j0, j0 + width, PART)])
-                tanh_a = work.tile([P, BANK], F32, name="tanh_a", bufs=4)
+                tanh_a = work.tile([P, BANK], F32, name="tanh_a", bufs=TANH_BUFFERS)
                 nc.scalar.activation(tanh_a[:], bank[:], ACT.Tanh)
                 for t in ts:
                     cols = slice(width * (t - t0), width * (t - t0 + 1))
@@ -187,12 +188,7 @@ def tile_list_sorted_poem_gates_kernel(
                     cols = slice(width * (t - t0), width * (t - t0 + 1))
                     source = tanh_a[:, cols].rearrange("p (c i) -> p c i", i=RUN)
                     nc.scalar.activation(gain_tanh[:, :, t, :], source, ACT.Copy, scale=gain_sb[:, b, t : t + 1])
-            adder.tensor_tensor(
-                h_out.rearrange("p (c i) t -> p c t i", i=RUN),
-                gain_a[:],
-                gain_tanh[:],
-                ALU.add,
-            )
+            nc.gpsimd.tensor_tensor(h_out.rearrange("p (c i) t -> p c t i", i=RUN), gain_a[:], gain_tanh[:], ALU.add)
 
         pages = [keep.tile([P, S], F32, name="page%d" % n) for n in range(4)]
         starts = [sum(SLICES[:k]) for k in range(len(SLICES))]
@@ -200,8 +196,7 @@ def tile_list_sorted_poem_gates_kernel(
         w2_q = {}
 
         def second_product(parts):
-            bank = psum.tile([P, sum(SLICES[k] for n, k in parts)], F32, name="y_bank", tag="bank%d" % Y_BANKS[len(y_made)])
-            y_made.append(bank)
+            bank = psum_y.tile([P, sum(SLICES[k] for n, k in parts)], F32, name="y_bank")
             at = 0
             for n, k in parts:
                 for b in range(2):
@@ -220,11 +215,10 @@ def tile_list_sorted_poem_gates_kernel(
         def places(j0, width):
             return offs2_sb[:, j0 // PER_COLUMN : (j0 + width) // PER_COLUMN]
 
-        def weigh(y_psum, j0, width, tag):
-            count = y_psum.shape[1] // width
-            weighted = keep.tile([P, count, width], F32, name="weighted", tag=tag, align_bytes=64)
-            factor = wgo_sb[:, j0 : j0 + width].unsqueeze(1).to_broadcast([P, count, width])
-            nc.vector.tensor_tensor(weighted[:], y_psum.rearrange("p (m j) -> p m j", m=count), factor, ALU.mult)
+        def weigh(y_psum, j0, tag):
+            width = y_psum.shape[1]
+            weighted = keep.tile([P, width], F32, name="weighted", tag=tag, align_bytes=64)
+            nc.vector.tensor_tensor(weighted[:], y_psum, wgo_sb[:, j0 : j0 + width], ALU.mult)
             return weighted
 
         def copy_out(y_psum, tag):
@@ -235,14 +229,19 @@ def tile_list_sorted_poem_gates_kernel(
         def weigh_on_gpsimd(y_psum, j0, tag):
             width = y_psum.shape[1]
             y_sb = copy_out(y_psum, tag)
-            weighted = keep.tile([P, 1, width], F32, name="weighted", tag="from_" + tag, align_bytes=64)
-            nc.gpsimd.tensor_tensor(weighted[:, 0, :], y_sb[:], wgo_sb[:, j0 : j0 + width], ALU.mult)
+            weighted = keep.tile([P, width], F32, name="weighted", tag="from_" + tag, align_bytes=64)
+            nc.gpsimd.tensor_tensor(weighted[:], y_sb[:], wgo_sb[:, j0 : j0 + width], ALU.mult)
             return weighted
 
-        def put_back(first_page, weighted, j0):
-            for m in range(weighted.shape[1]):
-                window = pages[first_page + m][:].indirect(places(j0, weighted.shape[2]))
-                nc.vector.tensor_copy(window, weighted[:, m, :])
+        def put_back(page, weighted, j0):
+            nc.vector.tensor_copy(pages[page][:].indirect(places(j0, weighted.shape[1])), weighted[:])
+
+        def put_back_pair(bank, j0, width):
+            weighted = keep.tile([P, 2, width], F32, name="weighted", tag="first_two", align_bytes=64)
+            factor = wgo_sb[:, j0 : j0 + width].unsqueeze(1).to_broadcast([P, 2, width])
+            nc.vector.tensor_tensor(weighted[:], bank[:].rearrange("p (m j) -> p m j", m=2), factor, ALU.mult)
+            for n in range(2):
+                put_back(n, weighted[:, n, :], j0)
 
         def finish(n, c0, width, engine, result):
             gate = keep.tile([P, width], F32, name="gate", tag="gate%d_%d" % (n, c0), align_bytes=64)
@@ -250,24 +249,26 @@ def tile_list_sorted_poem_gates_kernel(
             engine.tensor_tensor(result, gate[:], x0_sb[n][:, c0 : c0 + width], ALU.mult)
             nc.sync.dma_start(out[P * n : P * (n + 1), c0 : c0 + width], result)
 
-        def by_pass(tile, c0, width):
-            return tile[:, c0 : c0 + 2 * width].rearrange("p (b n) -> p b n", b=2)
+        def by_pass(columns):
+            return columns.rearrange("p (b n) -> p b n", b=2)
 
-        woven = keep.tile([P, HALF, PACK], BF16, name="w2_first", align_bytes=64)
-        weave_w2(nc.vector.tensor_copy, woven[:], 0, 0, 0, HALF)
+        w2_first = keep.tile([P, HALF, PACK], BF16, name="w2_first", align_bytes=64)
+        weave_w2(nc.vector.tensor_copy, w2_first[:], 0, 0)
         words, scales = quantised_tiles("w2_first", HALF)
-        quantise(words[:], scales[:], woven[:])
+        quantise(words[:], scales[:], w2_first[:])
         for n in range(2):
             w2_q[n, 0] = (words[:, P * n : P * (n + 1)], scales[:, P * n : P * (n + 1)])
         woven = keep.tile([P, 4 * P, PACK], BF16, name="woven", tag="woven", align_bytes=64)
         for b in range(2):
-            times_gain(nc.vector, woven[:, P * b : P * (b + 1), :].unsqueeze(1), sum_on_vector(0, [b], P), b)
-        total = reuse.tile([P, 2, P, PACK], F32, name="total_second", offset=SHARED, align_bytes=64)
-        sum_on_vector(P, [0, 1], P, total)
-        weave_w2(nc.scalar.copy, woven[:, 2 * P :, :], 0, 1, 0, HALF)
+            total = keep.tile([P, 1, P, PACK], F32, name="total0_%d" % b, align_bytes=64)
+            sum_on_vector(total, 0, [b])
+            times_gain(nc.vector, woven[:, P * b : P * (b + 1), :].unsqueeze(1), total, b)
+        total = reuse.tile([P, 2, P, PACK], F32, name="total_second", offset=SUMS_AT, align_bytes=64)
+        sum_on_vector(total, P, [0, 1])
+        weave_w2(nc.scalar.copy, woven[:, 2 * P :, :], 0, 1)
         words, scales = quantised_tiles("first", 4 * P)
         quantise(words[:], scales[:], woven[:])
-        h_q.append([by_pass(tile, 0, P) for tile in (words, scales)])
+        h_q.append([by_pass(tile) for tile in (words[:, 0 : 2 * P], scales[:, 0 : 2 * P])])
         for n in range(2):
             w2_q[n, 1] = (words[:, P * (2 + n) : P * (3 + n)], scales[:, P * (2 + n) : P * (3 + n)])
         x0_all = reuse.tile([P, 4 * S], F32, name="x0_all", offset=0, align_bytes=64)
@@ -278,14 +279,15 @@ def tile_list_sorted_poem_gates_kernel(
         woven = keep.tile([P, 2, P, PACK], BF16, name="woven", tag="woven", align_bytes=64)
         times_gain(nc.gpsimd, woven[:], total, 0)
         bank = second_product([(0, 0), (1, 0)])
-        put_back(0, weigh(bank[:, 0:P], 0, P, "page0_first"), 0)
-        total = sum_on_vector(2 * P, [0], 2 * P)
+        put_back(0, weigh(bank[:, 0:P], 0, "page0_first"), 0)
+        total = keep.tile([P, 1, SLICES[2], PACK], F32, name="total256_0", align_bytes=64)
+        sum_on_vector(total, starts[2], [0])
         w2_rest = keep.tile([P, 2, HALF, PACK], BF16, name="w2_rest", align_bytes=64)
         for b in range(2):
-            weave_w2(nc.scalar.copy, w2_rest[:, b], 1, b, 0, HALF)
-        held = reuse.tile([P, 1, P], F32, name="held_first", offset=SHARED + 4 * N, align_bytes=64)
-        nc.vector.tensor_tensor(held[:, 0, :], bank[:, P:], wgo_sb[:, 0:P], ALU.mult)
-        words = reuse.tile([P, N], U32, name="w2_rest_w", offset=SHARED, align_bytes=64)
+            weave_w2(nc.scalar.copy, w2_rest[:, b], 1, b)
+        held = reuse.tile([P, P], F32, name="held_first", offset=SUMS_AT + 4 * N, align_bytes=64)
+        nc.vector.tensor_tensor(held[:], bank[:, P:], wgo_sb[:, 0:P], ALU.mult)
+        words = reuse.tile([P, N], U32, name="w2_rest_w", offset=SUMS_AT, align_bytes=64)
         scales = keep.tile([P, N], U8, name="w2_rest_sc", align_bytes=64)
         quantise(words[:], scales[:], w2_rest[:].rearrange("p b n t -> p (b n) t"))
         for n in range(2, 4):
@@ -294,56 +296,50 @@ def tile_list_sorted_poem_gates_kernel(
                 w2_q[n, b] = (words[:, cols], scales[:, cols])
         words, scales = quantised_tiles("second", 2 * P)
         quantise(words[:], scales[:], woven[:].rearrange("p b n t -> p (b n) t"))
-        h_q.append([by_pass(tile, 0, P) for tile in (words, scales)])
-        woven = keep.tile([P, 2, 2 * P, PACK], BF16, name="woven", tag="woven", align_bytes=64)
+        h_q.append([by_pass(tile[:]) for tile in (words, scales)])
+        woven = keep.tile([P, 2, SLICES[2], PACK], BF16, name="woven", tag="woven", align_bytes=64)
         times_gain(nc.gpsimd, woven[:, 0:1], total, 0)
-        make_h(woven[:, 1], 2 * P, 2 * P, 1, nc.gpsimd)
+        make_h(woven[:, 1], starts[2], SLICES[2], 1)
         put_back(1, held, 0)
-        put_back(0, weigh(second_product([(0, 1), (1, 1)])[:], P, P, "first_two"), P)
-        put_back(3, weigh(second_product([(3, 0), (3, 1)])[:], 0, 2 * P, "fourth"), 0)
+        put_back_pair(second_product([(0, 1), (1, 1)]), P, P)
+        put_back(3, weigh(second_product([(3, 0), (3, 1)])[:], 0, "fourth"), 0)
         held_y = second_product([(2, 0), (2, 1)])[:]
 
         last = len(SLICES) - 1
         for index in range(2, last + 1):
             j0, width = starts[index], SLICES[index]
-            n0 = 0
             if index > 2:
                 woven = keep.tile([P, 2, width, PACK], BF16, name="woven", tag="woven", align_bytes=64)
-                make_h(woven[:, 0], j0, width, 0, nc.gpsimd)
-                step = width
-                for n0 in range(0, width, step):
-                    make_h(woven[:, 1, n0 : n0 + step], j0 + n0, step, 1, nc.gpsimd)
-            last_sum = "gain_a%d_1" % (j0 + n0)
-            held = copy_out(held_y, last_sum) if index == last else weigh(held_y, j0 - width, width, last_sum)
+                for b in range(2):
+                    make_h(woven[:, b], j0, width, b)
+            last_sum = "gain_a%d_1" % j0
+            held = copy_out(held_y, last_sum) if index == last else weigh(held_y, j0 - width, last_sum)
             words, scales = quantised_tiles("h%d" % index, 2 * width)
             quantise(words[:], scales[:], woven[:].rearrange("p b n t -> p (b n) t"))
-            h_q.append([by_pass(tile, 0, width) for tile in (words, scales)])
+            h_q.append([by_pass(tile[:]) for tile in (words, scales)])
             if index == last:
                 window = pages[2][:].indirect(places(j0 - width, width))
                 nc.vector.tensor_tensor(window, held[:], wgo_sb[:, j0 - width : j0], ALU.mult)
             else:
                 put_back(2, held, j0 - width)
             bank = second_product([(0, index), (1, index)])
-            first_two = [weigh(bank[:, width * n : width * (n + 1)], j0, width, "page%d_next" % n) for n in range(2)]
+            first_two = [weigh(bank[:, width * n : width * (n + 1)], j0, "page%d_next" % n) for n in range(2)]
             for n in range(2):
                 put_back(n, first_two[n], j0)
             if index == 2:
                 bank = second_product([(3, index), (2, index)])
-                put_back(3, weigh(bank[:, 0:width], j0, width, "fourth"), j0)
+                put_back(3, weigh(bank[:, 0:width], j0, "fourth"), j0)
                 held_y = bank[:, width:]
             elif index < last:
                 held_y = second_product([(2, index)])[:]
 
         put_back(2, weigh_on_gpsimd(second_product([(2, last)])[:], j0, "y_third"), j0)
         put_back(3, weigh_on_gpsimd(second_product([(3, last - 1), (3, last)])[:], j0 - width, "y_fourth"), j0 - width)
-        on_gpsimd = [(0, 0, 512), (0, 512, 512), (1, 0, 512), (1, 512, 512)]
+        on_gpsimd = [(n, c0, S // 2) for n in range(2) for c0 in (0, S // 2)]
         on_vector = [(2, 0, 512), (2, 512, 512), (3, 0, 512), (3, 512, 256), (3, 768, 256)]
         for n, c0, count in on_gpsimd:
             finish(n, c0, count, nc.gpsimd, x0_sb[n][:, c0 : c0 + count])
-        results = keep.tile(
-            [P, sum(piece[2] for piece in on_vector)], F32, name="results", tag="gate%d_%d" % on_gpsimd[-1][:2], align_bytes=64
-        )
-        done = 0
+        results = keep.tile([P, 2 * S], F32, name="results", tag="gate%d_%d" % on_gpsimd[-1][:2], align_bytes=64)
         for n, c0, count in on_vector:
-            finish(n, c0, count, nc.vector, results[:, done : done + count])
-            done = done + count
+            at = S * (n - 2) + c0
+            finish(n, c0, count, nc.vector, results[:, at : at + count])

@@ -1,6 +1,7 @@
 from contextlib import ExitStack
 
 import concourse.mybir as mybir
+from concourse.masks import make_identity
 
 K, T, S, H, N = 1024, 4096, 1024, 1024, 512
 FLOPS = 2 * K * H * S + 2 * H * N * S
@@ -21,14 +22,12 @@ PACK = 4
 PASS = P * PACK
 BANK = 512
 PART = 128
-GATHER = 512
-SLICES = (128, 128, 256, 256, 256)
+WIDTH = 256
+SLICES = S // WIDTH
 HALF = N // 2
 SCALE_ROWS = 96
 PLANE = S + H
-GAIN_AT = 4 * T
-W1_AT = GAIN_AT + 64
-SUMS_AT = W1_AT + 4 * H
+W1_AT = 4 * T
 TANH_BUFFERS, TERM_BUFFERS = 4, 6
 RUN = 4
 PER_COLUMN = 16
@@ -59,11 +58,13 @@ def tile_list_sorted_poem_gates_kernel(
         nc.sync.dma_start(tab_sc[SCALE_ROWS:P, :].bitcast(I32), tab_scales.bitcast(I32).rearrange("a q t -> (a q) t"))
         nc.sync.dma_start(w1_sc_raw[SCALE_ROWS:P, :].bitcast(I32), w1_scales.bitcast(I32).rearrange("a q c -> (a q) c"))
         nc.sync.dma_start(offs2_sb[:], offs2)
+        gain_sb = keep.tile([P, 2, PACK], F32, name="gain_sb", align_bytes=64)
+        nc.sync.dma_start(gain_sb[:], gain.rearrange("(b p t) -> p b t", b=2, t=PACK))
         w1_raw = keep.tile([P, 2, 2 * H], U8, name="w1_raw", tag="after_w1_raw", align_bytes=64)
         nc.sync.dma_start(w1_raw[:].bitcast(I32), w1_words.bitcast(I32).rearrange("a p c -> p a c"))
         tab_w0 = keep.tile([P, T], I32, name="tab_w0", tag="after_tab_w0", align_bytes=64)
         nc.sync.dma_start(tab_w0[:], tab_words[0].rearrange("p t i -> p (t i)").bitcast(I32))
-        v_sc_rows = reuse.tile([P, S], U8, name="v_sc_rows", offset=GAIN_AT - S // 2, align_bytes=64)
+        v_sc_rows = reuse.tile([P, S], U8, name="v_sc_rows", offset=W1_AT - S // 2, align_bytes=64)
         nc.vector.tensor_copy(v_sc_rows[:], tab_sc[:].indirect(offs_sb[:]))
         sc_rows = keep.tile([P, PLANE], U8, name="sc_rows", align_bytes=64)
         nc.vector.tensor_copy(
@@ -89,51 +90,70 @@ def tile_list_sorted_poem_gates_kernel(
         )
         tab_w1 = reuse.tile([P, T], I32, name="tab_w1", offset=0, align_bytes=64)
         nc.sync.dma_start(tab_w1[:], tab_words[1].rearrange("p t i -> p (t i)").bitcast(I32))
-        gain_sb = reuse.tile([P, 2, PACK], F32, name="gain_sb", offset=GAIN_AT, align_bytes=64)
-        nc.sync.dma_start(gain_sb[:], gain.rearrange("(b p t) -> p b t", b=2, t=PACK))
         move_rows(1)
 
-        def gather_words(words, window, j0):
-            entries = offs_sb[:, j0 // PER_COLUMN : (j0 + GATHER) // PER_COLUMN]
-            nc.vector.tensor_copy(words, window[:].bitcast(U32).indirect(entries))
-            return words
+        def gather_words(words, window, j0, j1):
+            entries = offs_sb[:, j0 // PER_COLUMN : j1 // PER_COLUMN]
+            nc.vector.tensor_copy(words[:, j0:j1], window[:].bitcast(U32).indirect(entries))
 
-        v_w0 = keep.tile([P, S], U32, name="v_w0", align_bytes=64)
-        v_w = {(0, j0): gather_words(v_w0[:, j0 : j0 + GATHER], tab_w0, j0) for j0 in range(S - GATHER, -1, -GATHER)}
-
-        v_w1 = keep.tile([P, S], U32, name="v_w1", align_bytes=64)
-        for j0 in range(0, S, GATHER):
-            v_w[1, j0] = gather_words(v_w1[:, j0 : j0 + GATHER], tab_w1, j0)
+        v_w = [keep.tile([P, S], U32, name="v_w%d" % a, align_bytes=64) for a in range(2)]
+        gather_words(v_w[0], tab_w0, S // 2, S)
+        gather_words(v_w[0], tab_w0, 0, S // 2)
+        gather_words(v_w[1], tab_w1, 0, WIDTH)
+        gather_words(v_w[1], tab_w1, WIDTH, S)
 
         warm_in = keep.tile([P, 1], F32, name="warm_in")
         warm_out = keep.tile([P, 1], F32, name="warm_out")
         nc.gpsimd.memset(warm_in[:], 0.0)
         nc.scalar.activation(warm_out[:], warm_in[:], ACT.Sigmoid)
 
+        identity = keep.tile([P, P], F32, name="identity", align_bytes=64)
+        make_identity(nc, identity[:])
+
+        def into_psum(values, pool, name):
+            width = values.shape[1]
+            turned = pool.tile([P, width], F32, name=name)
+            for c0 in range(0, width, P):
+                nc.tensor.transpose(turned[:, c0 : c0 + P], values[:, c0 : c0 + P], identity[:])
+            turned_sb = work.tile([P, width], F32, name="turned_sb")
+            nc.scalar.copy(turned_sb[:], turned[:])
+            upright = pool.tile([P, width], F32, name=name)
+            for c0 in range(0, width, P):
+                nc.tensor.transpose(upright[:, c0 : c0 + P], turned_sb[:, c0 : c0 + P], identity[:])
+            return upright
+
+        gain_woven = keep.tile([P, 2, P // PACK, PACK], F32, name="gain_woven", align_bytes=64)
+        nc.scalar.copy(gain_woven[:], gain_sb[:].unsqueeze(2).to_broadcast([P, 2, P // PACK, PACK]))
+        gain_psum = into_psum(gain_woven[:].rearrange("p b n t -> p (b n t)"), psum_y, "y_bank")
+
         w2_rows = w2.rearrange("(b p t) (half n) -> half b p t n", b=2, t=PACK, half=2)
         w2_width = PACK * HALF
         early = keep.tile([P, 2 * w2_width], F32, name="early", tag="after_w1_raw", align_bytes=64)
         late = keep.tile([P, 2 * w2_width + S], F32, name="late", tag="after_tab_w0", align_bytes=64)
-        gain_woven = keep.tile([P, 2, PART, PACK], F32, name="gain_woven", align_bytes=64)
-        nc.scalar.copy(gain_woven[:], gain_sb[:].unsqueeze(2).to_broadcast([P, 2, PART, PACK]))
         w2_raw = [[tile[:, w2_width * b : w2_width * (b + 1)] for b in range(2)] for tile in (early, late)]
         for half in range(2):
             for b in range(2):
                 nc.sync.dma_start(w2_raw[half][b].rearrange("p (t n) -> p t n", t=PACK), w2_rows[half, b])
         wgo_sb = late[:, 2 * w2_width : 2 * w2_width + S]
         nc.sync.dma_start(wgo_sb, wgo)
+        x0_all = reuse.tile([P, 4 * S], F32, name="x0_all", offset=0, align_bytes=64)
+        x0_sb = [x0_all[:, S * n : S * (n + 1)] for n in range(4)]
+        for n in range(4):
+            nc.sync.dma_start(x0_sb[n], x0[P * n : P * (n + 1), :])
 
-        def weave_w2(copy, woven, half, b):
-            raw = w2_raw[half][b].rearrange("p (t c i) -> p c t i", t=PACK, i=RUN)
-            copy(woven.rearrange("p (c i) t -> p c t i", i=RUN), raw)
+        def weave_on_gpsimd(woven, half, b):
+            raw = w2_raw[half][b].rearrange("p (t n) -> p n t", t=PACK)
+            nc.gpsimd.tensor_scalar(woven, raw, 1.0, 0.0, ALU.mult, ALU.add)
 
-        def quantise(words, scales, woven):
-            nc.vector.quantize_mx(out=words.bitcast(FP8X4), scales=scales, in_=woven.rearrange("p n t -> p (n t)"))
-
-        def quantised_tiles(name, count):
-            words = keep.tile([P, count], U32, name=name + "_w", align_bytes=64)
+        def quantise(woven, name, tag=None):
+            passes = woven.shape[1]
+            count = passes * woven.shape[2]
+            words = keep.tile([P, count], U32, name=name + "_w", tag=tag or name + "_w", align_bytes=64)
             scales = keep.tile([P, count], U8, name=name + "_sc", align_bytes=64)
-            return words, scales
+            nc.vector.quantize_mx(
+                out=words[:].bitcast(FP8X4), scales=scales[:], in_=woven[:].rearrange("p b n t -> p (b n t)")
+            )
+            return [tile[:].rearrange("p (b n) -> p b n", b=passes) for tile in (words, scales)]
 
         def first_product(b, parts):
             bank = psum_a.tile([P, BANK], F32, name="a_bank")
@@ -144,41 +164,26 @@ def tile_list_sorted_poem_gates_kernel(
                         out=bank[:, PART * place : PART * (place + 1)],
                         lhsT=w1_w[:, a, 2 * c0 : 2 * (c0 + P)].bitcast(FP4X4),
                         lhsT_scale=planes[:, PLANE * a + S + c0 : PLANE * a + S + c0 + P],
-                        rhs=v_w[a, j - j % GATHER][:, j % GATHER : j % GATHER + PART].bitcast(FP8X4),
+                        rhs=v_w[a][:, j : j + PART].bitcast(FP8X4),
                         rhs_scale=planes[:, PLANE * a + j : PLANE * a + j + PART],
                         start=(a == 0 and place == 0),
                         stop=(a == 1 and place == len(parts) - 1),
                     )
             return bank
 
-        def sum_on_vector(total, j0, bs):
-            width = total.shape[2]
-            for b in bs:
-                for n0 in range(0, width, PART):
-                    bank = first_product(b, [(t, j0 + n0) for t in range(PACK)])
-                    woven_a = bank[:].rearrange("p (t j) -> p j t", t=PACK)
-                    tanh_a = work.tile([P, PART, PACK], F32, name="tanh_a", bufs=TANH_BUFFERS)
-                    nc.scalar.activation(tanh_a[:], woven_a, ACT.Tanh)
-                    nc.vector.tensor_tensor(total[:, b - bs[0], n0 : n0 + PART, :], woven_a, tanh_a[:], ALU.add)
-
-        def times_gain(engine, h_out, total, b0):
-            passes, parts = total.shape[1], total.shape[2] // PART
-            factor = gain_woven[:, b0 : b0 + passes].rearrange("p b n t -> p b (n t)").unsqueeze(2)
-            engine.tensor_tensor(
-                h_out.rearrange("p b (m n) t -> p b m (n t)", m=parts),
-                total[:].rearrange("p b (m n) t -> p b m (n t)", m=parts),
-                factor.to_broadcast([P, passes, parts, PART * PACK]),
-                ALU.mult,
-            )
-
-        def make_h(h_out, j0, width, b):
+        def make_h(h_out, j0, b, between=None):
+            width = h_out.shape[1]
             gain_a = keep.tile([P, width // RUN, PACK, RUN], F32, name="gain_a", tag="gain_a%d_%d" % (j0, b), align_bytes=64)
             gain_tanh = work.tile([P, width // RUN, PACK, RUN], F32, name="gain_tanh", bufs=TERM_BUFFERS)
             per_bank = BANK // width
             for t0 in range(0, PACK, per_bank):
                 ts = range(t0, t0 + per_bank)
                 bank = first_product(b, [(t, j) for t in ts for j in range(j0, j0 + width, PART)])
-                tanh_a = work.tile([P, BANK], F32, name="tanh_a", bufs=TANH_BUFFERS)
+                marked = between is not None and t0 == 0
+                if marked:
+                    tanh_a = keep.tile([P, BANK], F32, name="tanh_mark", tag="tanh_mark%d" % j0, align_bytes=64)
+                else:
+                    tanh_a = work.tile([P, BANK], F32, name="tanh_a", bufs=TANH_BUFFERS)
                 nc.scalar.activation(tanh_a[:], bank[:], ACT.Tanh)
                 for t in ts:
                     cols = slice(width * (t - t0), width * (t - t0 + 1))
@@ -188,158 +193,141 @@ def tile_list_sorted_poem_gates_kernel(
                     cols = slice(width * (t - t0), width * (t - t0 + 1))
                     source = tanh_a[:, cols].rearrange("p (c i) -> p c i", i=RUN)
                     nc.scalar.activation(gain_tanh[:, :, t, :], source, ACT.Copy, scale=gain_sb[:, b, t : t + 1])
+                if marked:
+                    between("tanh_mark%d" % j0)
             nc.gpsimd.tensor_tensor(h_out.rearrange("p (c i) t -> p c t i", i=RUN), gain_a[:], gain_tanh[:], ALU.add)
 
         pages = [keep.tile([P, S], F32, name="page%d" % n) for n in range(4)]
-        starts = [sum(SLICES[:k]) for k in range(len(SLICES))]
         h_q = []
         w2_q = {}
 
-        def second_product(parts):
-            bank = psum_y.tile([P, sum(SLICES[k] for n, k in parts)], F32, name="y_bank")
-            at = 0
-            for n, k in parts:
+        def second_product(chosen):
+            bank = psum_y.tile([P, WIDTH * len(chosen)], F32, name="y_bank")
+            for place, (n, k) in enumerate(chosen):
+                cols = slice(P * (n % 2), P * (n % 2 + 1))
                 for b in range(2):
                     nc.tensor.matmul_mx(
-                        out=bank[:, at : at + SLICES[k]],
-                        lhsT=w2_q[n, b][0].bitcast(FP8X4),
-                        lhsT_scale=w2_q[n, b][1],
+                        out=bank[:, WIDTH * place : WIDTH * (place + 1)],
+                        lhsT=w2_q[n // 2, b][0][:, cols].bitcast(FP8X4),
+                        lhsT_scale=w2_q[n // 2, b][1][:, cols],
                         rhs=h_q[k][0][:, b, :].bitcast(FP8X4),
                         rhs_scale=h_q[k][1][:, b, :],
                         start=(b == 0),
                         stop=(b == 1),
                     )
-                at = at + SLICES[k]
             return bank
 
-        def places(j0, width):
-            return offs2_sb[:, j0 // PER_COLUMN : (j0 + width) // PER_COLUMN]
+        def weighted_tile(tag, width=WIDTH):
+            return keep.tile([P, width], F32, name="weighted", tag=tag, align_bytes=64)
 
-        def weigh(y_psum, j0, tag):
-            width = y_psum.shape[1]
-            weighted = keep.tile([P, width], F32, name="weighted", tag=tag, align_bytes=64)
-            nc.vector.tensor_tensor(weighted[:], y_psum, wgo_sb[:, j0 : j0 + width], ALU.mult)
-            return weighted
+        def weigh(engine, weighted, y, j0):
+            engine.tensor_tensor(weighted, y, wgo_sb[:, j0 : j0 + y.shape[1]], ALU.mult)
 
         def copy_out(y_psum, tag):
             y_sb = keep.tile([P, y_psum.shape[1]], F32, name="y_sb", tag=tag, align_bytes=64)
             nc.scalar.copy(y_sb[:], y_psum)
             return y_sb
 
-        def weigh_on_gpsimd(y_psum, j0, tag):
-            width = y_psum.shape[1]
-            y_sb = copy_out(y_psum, tag)
-            weighted = keep.tile([P, width], F32, name="weighted", tag="from_" + tag, align_bytes=64)
-            nc.gpsimd.tensor_tensor(weighted[:], y_sb[:], wgo_sb[:, j0 : j0 + width], ALU.mult)
-            return weighted
-
         def put_back(page, weighted, j0):
-            nc.vector.tensor_copy(pages[page][:].indirect(places(j0, weighted.shape[1])), weighted[:])
+            places = offs2_sb[:, j0 // PER_COLUMN : (j0 + weighted.shape[1]) // PER_COLUMN]
+            nc.vector.tensor_copy(pages[page][:].indirect(places), weighted[:])
 
-        def put_back_pair(bank, j0, width):
-            weighted = keep.tile([P, 2, width], F32, name="weighted", tag="first_two", align_bytes=64)
-            factor = wgo_sb[:, j0 : j0 + width].unsqueeze(1).to_broadcast([P, 2, width])
-            nc.vector.tensor_tensor(weighted[:], bank[:].rearrange("p (m j) -> p m j", m=2), factor, ALU.mult)
+        w2_first = keep.tile([P, 2, HALF, PACK], BF16, name="w2_first", align_bytes=64)
+        w2_third = keep.tile([P, 1, HALF, PACK], BF16, name="w2_third", align_bytes=64)
+        for b in range(2):
+            weave_on_gpsimd(w2_first[:, b], 0, b)
+        weave_on_gpsimd(w2_third[:, 0], 1, 0)
+        banks = [(b, n0) for b in range(2) for n0 in range(0, WIDTH, PART)]
+        sum_tags = ["total0", "total1", "total2", "woven"]
+        sums = []
+        for (b, n0), tag in zip(banks, sum_tags):
+            woven_a = first_product(b, [(t, n0) for t in range(PACK)])[:].rearrange("p (t j) -> p j t", t=PACK)
+            tanh_a = work.tile([P, PART, PACK], F32, name="tanh_a", bufs=TANH_BUFFERS)
+            nc.scalar.activation(tanh_a[:], woven_a, ACT.Tanh)
+            total = keep.tile([P, PART, PACK], F32, name="total", tag=tag, align_bytes=64)
+            nc.vector.tensor_tensor(total[:], woven_a, tanh_a[:], ALU.add)
+            sums.append(total)
+        woven = keep.tile([P, 2, WIDTH, PACK], BF16, name="woven_first", align_bytes=64)
+        for (b, n0), total in zip(banks, sums):
+            nc.vector.tensor_tensor(
+                woven[:, b, n0 : n0 + PART, :].rearrange("p (m n) t -> p m (n t)", m=PACK),
+                total[:].rearrange("p (m n) t -> p m (n t)", m=PACK),
+                gain_psum[:, P * b : P * (b + 1)].unsqueeze(1).to_broadcast([P, PACK, P]),
+                ALU.mult,
+            )
+        words, scales = quantise(w2_first, "w2_first", "total2")
+        for b in range(2):
+            w2_q[0, b] = (words[:, b], scales[:, b])
+        h_q.append(quantise(woven, "h0"))
+        w2_fourth = keep.tile([P, 1, HALF, PACK], BF16, name="w2_fourth", tag="woven", align_bytes=64)
+        nc.vector.tensor_copy(
+            w2_fourth[:, 0].rearrange("p (c i) t -> p c t i", i=RUN),
+            w2_raw[1][1].rearrange("p (t c i) -> p c t i", t=PACK, i=RUN),
+        )
+        for b, (piece, tag) in enumerate([(w2_third, "total1"), (w2_fourth, None)]):
+            words, scales = quantise(piece, "w2_rest%d" % b, tag)
+            w2_q[1, b] = (words[:, 0], scales[:, 0])
+
+        last = SLICES - 1
+
+        def first_two(k):
+            bank = second_product([(0, k), (1, k)])
+            ready = [weighted_tile("page%d_next" % n) for n in range(2)]
             for n in range(2):
-                put_back(n, weighted[:, n, :], j0)
+                weigh(nc.vector, ready[n][:], bank[:, WIDTH * n : WIDTH * (n + 1)], WIDTH * k)
+            return ready
 
-        def finish(n, c0, width, engine, result):
-            gate = keep.tile([P, width], F32, name="gate", tag="gate%d_%d" % (n, c0), align_bytes=64)
-            nc.scalar.activation(gate[:], pages[n][:, c0 : c0 + width], ACT.Sigmoid)
-            engine.tensor_tensor(result, gate[:], x0_sb[n][:, c0 : c0 + width], ALU.mult)
+        def by_gpsimd(page, y_psum, j0, tag):
+            weighted = weighted_tile("by_gpsimd%d" % page, y_psum.shape[1])
+            weigh(nc.gpsimd, weighted[:], copy_out(y_psum, tag)[:], j0)
+            put_back(page, weighted, j0)
+
+        for k in range(last):
+            j0, j1 = WIDTH * k, WIDTH * (k + 1)
+            ready = first_two(k)
+            held_page = 2 if k == last - 1 else 3
+            other = second_product([(n, k) for n in range(2, held_page + 1)])
+            put_back(0, ready[0], j0)
+            if k == 0:
+                third = weighted_tile("page2_next")
+                weigh(nc.vector, third[:], other[:, 0:WIDTH], j0)
+            put_back(1, ready[1], j0)
+            if k == 0:
+                put_back(2, third, j0)
+            woven = keep.tile([P, 2, WIDTH, PACK], BF16, name="woven", tag="woven", align_bytes=64)
+            make_h(woven[:, 0], j1, 0)
+            if k == last - 1:
+                for n0 in range(0, WIDTH, PART):
+                    make_h(woven[:, 1, n0 : n0 + PART], j1 + n0, 1)
+                last_term = "gain_a%d_1" % (j1 + PART)
+            else:
+                between = (lambda tag: by_gpsimd(2, other[:, 0:WIDTH], j0, tag)) if k > 0 else None
+                make_h(woven[:, 1], j1, 1, between)
+                last_term = "gain_a%d_1" % j1
+            held = weighted_tile(last_term)
+            weigh(nc.vector, held[:], other[:, WIDTH * (held_page - 2) : WIDTH * (held_page - 1)], j0)
+            h_q.append(quantise(woven, "h%d" % (k + 1)))
+            put_back(held_page, held, j0)
+
+        ready = first_two(last)
+        for n in range(2):
+            put_back(n, ready[n], WIDTH * last)
+        by_gpsimd(2, second_product([(2, last)])[:], WIDTH * last, "y_last2")
+        by_gpsimd(3, second_product([(3, last - 1), (3, last)])[:], WIDTH * (last - 1), "y_last3")
+
+        def finish(n, c0, engine, gate, result):
+            width = result.shape[1]
+            nc.scalar.activation(gate, pages[n][:, c0 : c0 + width], ACT.Sigmoid)
+            engine.tensor_tensor(result, gate, x0_sb[n][:, c0 : c0 + width], ALU.mult)
             nc.sync.dma_start(out[P * n : P * (n + 1), c0 : c0 + width], result)
 
-        def by_pass(columns):
-            return columns.rearrange("p (b n) -> p b n", b=2)
-
-        w2_first = keep.tile([P, HALF, PACK], BF16, name="w2_first", align_bytes=64)
-        weave_w2(nc.vector.tensor_copy, w2_first[:], 0, 0)
-        words, scales = quantised_tiles("w2_first", HALF)
-        quantise(words[:], scales[:], w2_first[:])
-        for n in range(2):
-            w2_q[n, 0] = (words[:, P * n : P * (n + 1)], scales[:, P * n : P * (n + 1)])
-        woven = keep.tile([P, 4 * P, PACK], BF16, name="woven", tag="woven", align_bytes=64)
-        for b in range(2):
-            total = keep.tile([P, 1, P, PACK], F32, name="total0_%d" % b, align_bytes=64)
-            sum_on_vector(total, 0, [b])
-            times_gain(nc.vector, woven[:, P * b : P * (b + 1), :].unsqueeze(1), total, b)
-        total = reuse.tile([P, 2, P, PACK], F32, name="total_second", offset=SUMS_AT, align_bytes=64)
-        sum_on_vector(total, P, [0, 1])
-        weave_w2(nc.scalar.copy, woven[:, 2 * P :, :], 0, 1)
-        words, scales = quantised_tiles("first", 4 * P)
-        quantise(words[:], scales[:], woven[:])
-        h_q.append([by_pass(tile) for tile in (words[:, 0 : 2 * P], scales[:, 0 : 2 * P])])
-        for n in range(2):
-            w2_q[n, 1] = (words[:, P * (2 + n) : P * (3 + n)], scales[:, P * (2 + n) : P * (3 + n)])
-        x0_all = reuse.tile([P, 4 * S], F32, name="x0_all", offset=0, align_bytes=64)
-        x0_sb = [x0_all[:, S * n : S * (n + 1)] for n in range(4)]
-        for n in range(4):
-            nc.sync.dma_start(x0_sb[n], x0[P * n : P * (n + 1), :])
-
-        woven = keep.tile([P, 2, P, PACK], BF16, name="woven", tag="woven", align_bytes=64)
-        times_gain(nc.gpsimd, woven[:], total, 0)
-        bank = second_product([(0, 0), (1, 0)])
-        put_back(0, weigh(bank[:, 0:P], 0, "page0_first"), 0)
-        total = keep.tile([P, 1, SLICES[2], PACK], F32, name="total256_0", align_bytes=64)
-        sum_on_vector(total, starts[2], [0])
-        w2_rest = keep.tile([P, 2, HALF, PACK], BF16, name="w2_rest", align_bytes=64)
-        for b in range(2):
-            weave_w2(nc.scalar.copy, w2_rest[:, b], 1, b)
-        held = reuse.tile([P, P], F32, name="held_first", offset=SUMS_AT + 4 * N, align_bytes=64)
-        nc.vector.tensor_tensor(held[:], bank[:, P:], wgo_sb[:, 0:P], ALU.mult)
-        words = reuse.tile([P, N], U32, name="w2_rest_w", offset=SUMS_AT, align_bytes=64)
-        scales = keep.tile([P, N], U8, name="w2_rest_sc", align_bytes=64)
-        quantise(words[:], scales[:], w2_rest[:].rearrange("p b n t -> p (b n) t"))
-        for n in range(2, 4):
-            for b in range(2):
-                cols = slice(HALF * b + P * (n - 2), HALF * b + P * (n - 1))
-                w2_q[n, b] = (words[:, cols], scales[:, cols])
-        words, scales = quantised_tiles("second", 2 * P)
-        quantise(words[:], scales[:], woven[:].rearrange("p b n t -> p (b n) t"))
-        h_q.append([by_pass(tile[:]) for tile in (words, scales)])
-        woven = keep.tile([P, 2, SLICES[2], PACK], BF16, name="woven", tag="woven", align_bytes=64)
-        times_gain(nc.gpsimd, woven[:, 0:1], total, 0)
-        make_h(woven[:, 1], starts[2], SLICES[2], 1)
-        put_back(1, held, 0)
-        put_back_pair(second_product([(0, 1), (1, 1)]), P, P)
-        put_back(3, weigh(second_product([(3, 0), (3, 1)])[:], 0, "fourth"), 0)
-        held_y = second_product([(2, 0), (2, 1)])[:]
-
-        last = len(SLICES) - 1
-        for index in range(2, last + 1):
-            j0, width = starts[index], SLICES[index]
-            if index > 2:
-                woven = keep.tile([P, 2, width, PACK], BF16, name="woven", tag="woven", align_bytes=64)
-                for b in range(2):
-                    make_h(woven[:, b], j0, width, b)
-            last_sum = "gain_a%d_1" % j0
-            held = copy_out(held_y, last_sum) if index == last else weigh(held_y, j0 - width, last_sum)
-            words, scales = quantised_tiles("h%d" % index, 2 * width)
-            quantise(words[:], scales[:], woven[:].rearrange("p b n t -> p (b n) t"))
-            h_q.append([by_pass(tile[:]) for tile in (words, scales)])
-            if index == last:
-                window = pages[2][:].indirect(places(j0 - width, width))
-                nc.vector.tensor_tensor(window, held[:], wgo_sb[:, j0 - width : j0], ALU.mult)
-            else:
-                put_back(2, held, j0 - width)
-            bank = second_product([(0, index), (1, index)])
-            first_two = [weigh(bank[:, width * n : width * (n + 1)], j0, "page%d_next" % n) for n in range(2)]
-            for n in range(2):
-                put_back(n, first_two[n], j0)
-            if index == 2:
-                bank = second_product([(3, index), (2, index)])
-                put_back(3, weigh(bank[:, 0:width], j0, "fourth"), j0)
-                held_y = bank[:, width:]
-            elif index < last:
-                held_y = second_product([(2, index)])[:]
-
-        put_back(2, weigh_on_gpsimd(second_product([(2, last)])[:], j0, "y_third"), j0)
-        put_back(3, weigh_on_gpsimd(second_product([(3, last - 1), (3, last)])[:], j0 - width, "y_fourth"), j0 - width)
-        on_gpsimd = [(n, c0, S // 2) for n in range(2) for c0 in (0, S // 2)]
-        on_vector = [(2, 0, 512), (2, 512, 512), (3, 0, 512), (3, 512, 256), (3, 768, 256)]
-        for n, c0, count in on_gpsimd:
-            finish(n, c0, count, nc.gpsimd, x0_sb[n][:, c0 : c0 + count])
-        results = keep.tile([P, 2 * S], F32, name="results", tag="gate%d_%d" % on_gpsimd[-1][:2], align_bytes=64)
-        for n, c0, count in on_vector:
-            at = S * (n - 2) + c0
-            finish(n, c0, count, nc.vector, results[:, at : at + count])
+        gates = keep.tile([P, 4, S], F32, name="gates", tag="y_last2", align_bytes=64)
+        on_gpsimd = [(0, 0, WIDTH), (0, WIDTH, WIDTH), (0, BANK, BANK), (1, 0, BANK), (1, BANK, BANK), (2, 0, WIDTH)]
+        on_vector = [(2, WIDTH, WIDTH), (2, BANK, BANK), (3, 0, BANK), (3, BANK, WIDTH), (3, BANK + WIDTH, WIDTH)]
+        last_gate = keep.tile([P, on_gpsimd[-1][2]], F32, name="last_gate", tag="y_last3", align_bytes=64)
+        for n, c0, width in on_gpsimd:
+            gate = last_gate[:] if (n, c0, width) == on_gpsimd[-1] else gates[:, n, c0 : c0 + width]
+            finish(n, c0, nc.gpsimd, gate, x0_sb[n][:, c0 : c0 + width])
+        results = keep.tile([P, 2, S], F32, name="results", tag="y_last3", align_bytes=64)
+        for n, c0, width in on_vector:
+            finish(n, c0, nc.vector, gates[:, n, c0 : c0 + width], results[:, n - 2, c0 : c0 + width])

@@ -28,10 +28,15 @@ HALF = N // 2
 SCALE_ROWS = 96
 PLANE = S + H
 W1_AT = 4 * T
-TANH_BUFFERS, TERM_BUFFERS = 4, 6
+THIRD_AT = W1_AT + 4 * H
+WOVEN_AT = THIRD_AT + 2 * HALF * PACK
+FIRST_AT = WOVEN_AT + 2 * WIDTH * PACK
+THIRD_WORDS_AT = FIRST_AT + 2 * HALF * PACK
+TANH_BUFFERS = 4
 RUN = 4
 PER_COLUMN = 16
-A_BANKS, Y_BANKS = 5, 3
+BANKS = 8
+AHEAD = 3
 
 
 def tile_list_sorted_poem_gates_kernel(
@@ -42,8 +47,12 @@ def tile_list_sorted_poem_gates_kernel(
         keep = ctx.enter_context(tc.tile_pool(name="keep", bufs=1))
         reuse = ctx.enter_context(tc.tile_pool(name="reuse", bufs=1))
         work = ctx.enter_context(tc.tile_pool(name="work", bufs=2))
-        psum_a = ctx.enter_context(tc.psum_pool(name="psum_a", bufs=A_BANKS))
-        psum_y = ctx.enter_context(tc.psum_pool(name="psum_y", bufs=Y_BANKS))
+        psum = ctx.enter_context(tc.psum_pool(name="psum", bufs=1))
+        taken = []
+
+        def next_bank(width):
+            taken.append(psum.tile([P, width], F32, name="bank", tag="bank%d" % (len(taken) % BANKS)))
+            return taken[-1]
 
         offs_sb = keep.tile([P, S // PER_COLUMN], U16, name="offs_sb")
         offs2_sb = keep.tile([P, S // PER_COLUMN], U16, name="offs2_sb")
@@ -97,8 +106,8 @@ def tile_list_sorted_poem_gates_kernel(
             nc.vector.tensor_copy(words[:, j0:j1], window[:].bitcast(U32).indirect(entries))
 
         v_w = [keep.tile([P, S], U32, name="v_w%d" % a, align_bytes=64) for a in range(2)]
-        gather_words(v_w[0], tab_w0, S // 2, S)
-        gather_words(v_w[0], tab_w0, 0, S // 2)
+        for j0 in range(0, S, S // 2):
+            gather_words(v_w[0], tab_w0, j0, j0 + S // 2)
         gather_words(v_w[1], tab_w1, 0, WIDTH)
         gather_words(v_w[1], tab_w1, WIDTH, S)
 
@@ -110,21 +119,21 @@ def tile_list_sorted_poem_gates_kernel(
         identity = keep.tile([P, P], F32, name="identity", align_bytes=64)
         make_identity(nc, identity[:])
 
-        def into_psum(values, pool, name):
+        def into_psum(values):
             width = values.shape[1]
-            turned = pool.tile([P, width], F32, name=name)
+            turned = next_bank(width)
             for c0 in range(0, width, P):
                 nc.tensor.transpose(turned[:, c0 : c0 + P], values[:, c0 : c0 + P], identity[:])
             turned_sb = work.tile([P, width], F32, name="turned_sb")
             nc.scalar.copy(turned_sb[:], turned[:])
-            upright = pool.tile([P, width], F32, name=name)
+            upright = next_bank(width)
             for c0 in range(0, width, P):
                 nc.tensor.transpose(upright[:, c0 : c0 + P], turned_sb[:, c0 : c0 + P], identity[:])
             return upright
 
         gain_woven = keep.tile([P, 2, P // PACK, PACK], F32, name="gain_woven", align_bytes=64)
         nc.scalar.copy(gain_woven[:], gain_sb[:].unsqueeze(2).to_broadcast([P, 2, P // PACK, PACK]))
-        gain_psum = into_psum(gain_woven[:].rearrange("p b n t -> p (b n t)"), psum_y, "y_bank")
+        gain_psum = into_psum(gain_woven[:].rearrange("p b n t -> p (b n t)"))
 
         w2_rows = w2.rearrange("(b p t) (half n) -> half b p t n", b=2, t=PACK, half=2)
         w2_width = PACK * HALF
@@ -145,46 +154,65 @@ def tile_list_sorted_poem_gates_kernel(
             raw = w2_raw[half][b].rearrange("p (t n) -> p n t", t=PACK)
             nc.gpsimd.tensor_scalar(woven, raw, 1.0, 0.0, ALU.mult, ALU.add)
 
-        def quantise(woven, name, tag=None):
+        def weave_page(copy, woven, n):
+            raw = w2_raw[1][1].rearrange("p (t n) -> p t n", t=PACK)[:, :, P * (n - 2) : P * (n - 1)]
+            copy(woven.rearrange("p (c i) t -> p c t i", i=RUN), raw.rearrange("p t (c i) -> p c t i", i=RUN))
+
+        def quantise(woven, name, words=None):
             passes = woven.shape[1]
             count = passes * woven.shape[2]
-            words = keep.tile([P, count], U32, name=name + "_w", tag=tag or name + "_w", align_bytes=64)
+            if words is None:
+                words = keep.tile([P, count], U32, name=name + "_w", tag=name + "_w", align_bytes=64)
             scales = keep.tile([P, count], U8, name=name + "_sc", align_bytes=64)
             nc.vector.quantize_mx(
                 out=words[:].bitcast(FP8X4), scales=scales[:], in_=woven[:].rearrange("p b n t -> p (b n t)")
             )
             return [tile[:].rearrange("p (b n) -> p b n", b=passes) for tile in (words, scales)]
 
+        a_banks = []
+
+        def take_banks(count):
+            a_banks.extend([next_bank(BANK) for place in range(count)])
+
+        take_banks(PACK + AHEAD)
+
         def first_product(b, parts):
-            bank = psum_a.tile([P, BANK], F32, name="a_bank")
+            bank = a_banks.pop(0)
+            width = BANK // len(parts)
             for a in range(2):
                 for place, (t, j) in enumerate(parts):
                     c0 = PASS * b + P * t
                     nc.tensor.matmul_mx(
-                        out=bank[:, PART * place : PART * (place + 1)],
+                        out=bank[:, width * place : width * (place + 1)],
                         lhsT=w1_w[:, a, 2 * c0 : 2 * (c0 + P)].bitcast(FP4X4),
                         lhsT_scale=planes[:, PLANE * a + S + c0 : PLANE * a + S + c0 + P],
-                        rhs=v_w[a][:, j : j + PART].bitcast(FP8X4),
-                        rhs_scale=planes[:, PLANE * a + j : PLANE * a + j + PART],
+                        rhs=v_w[a][:, j : j + width].bitcast(FP8X4),
+                        rhs_scale=planes[:, PLANE * a + j : PLANE * a + j + width],
                         start=(a == 0 and place == 0),
                         stop=(a == 1 and place == len(parts) - 1),
                     )
             return bank
 
-        def make_h(h_out, j0, b, between=None):
+        def make_h(h_out, j0, b, between=None, room=None):
             width = h_out.shape[1]
-            gain_a = keep.tile([P, width // RUN, PACK, RUN], F32, name="gain_a", tag="gain_a%d_%d" % (j0, b), align_bytes=64)
-            gain_tanh = work.tile([P, width // RUN, PACK, RUN], F32, name="gain_tanh", bufs=TERM_BUFFERS)
+            shape = [P, width // RUN, PACK, RUN]
+            gain_tanh = keep.tile(shape, F32, name="gain_tanh", tag="gain_tanh%d_%d" % (j0, b), align_bytes=64)
+            if room is None:
+                gain_a = keep.tile(shape, F32, name="gain_a", tag="gain_a%d_%d" % (j0, b), align_bytes=64)[:]
+            else:
+                gain_a = room[:, PACK * width :].rearrange("p (c t i) -> p c t i", t=PACK, i=RUN)
             per_bank = BANK // width
             for t0 in range(0, PACK, per_bank):
                 ts = range(t0, t0 + per_bank)
-                bank = first_product(b, [(t, j) for t in ts for j in range(j0, j0 + width, PART)])
+                bank = first_product(b, [(t, j0) for t in ts])
                 marked = between is not None and t0 == 0
-                if marked:
-                    tanh_a = keep.tile([P, BANK], F32, name="tanh_mark", tag="tanh_mark%d" % j0, align_bytes=64)
+                if room is not None:
+                    tanh_a = room[:, width * t0 : width * t0 + BANK]
+                elif marked:
+                    tanh_a = keep.tile([P, BANK], F32, name="tanh_mark", tag="tanh_mark%d" % j0, align_bytes=64)[:]
                 else:
-                    tanh_a = work.tile([P, BANK], F32, name="tanh_a", bufs=TANH_BUFFERS)
-                nc.scalar.activation(tanh_a[:], bank[:], ACT.Tanh)
+                    tanh_a = work.tile([P, BANK], F32, name="tanh_a", bufs=TANH_BUFFERS)[:]
+                nc.scalar.activation(tanh_a, bank[:], ACT.Tanh)
                 for t in ts:
                     cols = slice(width * (t - t0), width * (t - t0 + 1))
                     source = bank[:, cols].rearrange("p (c i) -> p c i", i=RUN)
@@ -195,21 +223,19 @@ def tile_list_sorted_poem_gates_kernel(
                     nc.scalar.activation(gain_tanh[:, :, t, :], source, ACT.Copy, scale=gain_sb[:, b, t : t + 1])
                 if marked:
                     between("tanh_mark%d" % j0)
-            nc.gpsimd.tensor_tensor(h_out.rearrange("p (c i) t -> p c t i", i=RUN), gain_a[:], gain_tanh[:], ALU.add)
+            nc.gpsimd.tensor_tensor(h_out.rearrange("p (c i) t -> p c t i", i=RUN), gain_a, gain_tanh[:], ALU.add)
 
-        pages = [keep.tile([P, S], F32, name="page%d" % n) for n in range(4)]
         h_q = []
         w2_q = {}
 
         def second_product(chosen):
-            bank = psum_y.tile([P, WIDTH * len(chosen)], F32, name="y_bank")
+            bank = next_bank(WIDTH * len(chosen))
             for place, (n, k) in enumerate(chosen):
-                cols = slice(P * (n % 2), P * (n % 2 + 1))
                 for b in range(2):
                     nc.tensor.matmul_mx(
                         out=bank[:, WIDTH * place : WIDTH * (place + 1)],
-                        lhsT=w2_q[n // 2, b][0][:, cols].bitcast(FP8X4),
-                        lhsT_scale=w2_q[n // 2, b][1][:, cols],
+                        lhsT=w2_q[n, b][0].bitcast(FP8X4),
+                        lhsT_scale=w2_q[n, b][1],
                         rhs=h_q[k][0][:, b, :].bitcast(FP8X4),
                         rhs_scale=h_q[k][1][:, b, :],
                         start=(b == 0),
@@ -228,53 +254,62 @@ def tile_list_sorted_poem_gates_kernel(
             nc.scalar.copy(y_sb[:], y_psum)
             return y_sb
 
-        def put_back(page, weighted, j0):
-            places = offs2_sb[:, j0 // PER_COLUMN : (j0 + weighted.shape[1]) // PER_COLUMN]
-            nc.vector.tensor_copy(pages[page][:].indirect(places), weighted[:])
+        def places(j0, width):
+            return offs2_sb[:, j0 // PER_COLUMN : (j0 + width) // PER_COLUMN]
 
-        w2_first = keep.tile([P, 2, HALF, PACK], BF16, name="w2_first", align_bytes=64)
-        w2_third = keep.tile([P, 1, HALF, PACK], BF16, name="w2_third", align_bytes=64)
+        def put_back(page, weighted, j0):
+            nc.vector.tensor_copy(pages[page][:].indirect(places(j0, weighted.shape[1])), weighted[:])
+
+        w2_first = reuse.tile([P, 2, HALF, PACK], BF16, name="w2_first", offset=FIRST_AT, align_bytes=64)
+        w2_third = reuse.tile([P, 1, HALF + P, PACK], BF16, name="w2_third", offset=THIRD_AT, align_bytes=64)
         for b in range(2):
             weave_on_gpsimd(w2_first[:, b], 0, b)
-        weave_on_gpsimd(w2_third[:, 0], 1, 0)
-        banks = [(b, n0) for b in range(2) for n0 in range(0, WIDTH, PART)]
-        sum_tags = ["total0", "total1", "total2", "woven"]
-        sums = []
-        for (b, n0), tag in zip(banks, sum_tags):
-            woven_a = first_product(b, [(t, n0) for t in range(PACK)])[:].rearrange("p (t j) -> p j t", t=PACK)
-            tanh_a = work.tile([P, PART, PACK], F32, name="tanh_a", bufs=TANH_BUFFERS)
-            nc.scalar.activation(tanh_a[:], woven_a, ACT.Tanh)
-            total = keep.tile([P, PART, PACK], F32, name="total", tag=tag, align_bytes=64)
-            nc.vector.tensor_tensor(total[:], woven_a, tanh_a[:], ALU.add)
-            sums.append(total)
+        weave_on_gpsimd(w2_third[:, 0, 0:HALF], 1, 0)
+        sums = [keep.tile([P, WIDTH, PACK], F32, name="total", tag=tag, align_bytes=64) for tag in ("total0", "total1")]
+        for b in range(2):
+            for n0 in range(0, WIDTH, PART):
+                woven_a = first_product(b, [(t, n0) for t in range(PACK)])[:].rearrange("p (t j) -> p j t", t=PACK)
+                tanh_a = work.tile([P, PART, PACK], F32, name="tanh_a", bufs=TANH_BUFFERS)
+                nc.scalar.activation(tanh_a[:], woven_a, ACT.Tanh)
+                nc.vector.tensor_tensor(sums[b][:, n0 : n0 + PART, :], woven_a, tanh_a[:], ALU.add)
+        weave_page(nc.scalar.copy, w2_third[:, 0, HALF:], 2)
         woven = keep.tile([P, 2, WIDTH, PACK], BF16, name="woven_first", align_bytes=64)
-        for (b, n0), total in zip(banks, sums):
+
+        runs = WIDTH * PACK // P
+        for b in range(2):
             nc.vector.tensor_tensor(
-                woven[:, b, n0 : n0 + PART, :].rearrange("p (m n) t -> p m (n t)", m=PACK),
-                total[:].rearrange("p (m n) t -> p m (n t)", m=PACK),
-                gain_psum[:, P * b : P * (b + 1)].unsqueeze(1).to_broadcast([P, PACK, P]),
+                woven[:, b].rearrange("p (m n) t -> p m (n t)", m=runs),
+                sums[b][:].rearrange("p (m n) t -> p m (n t)", m=runs),
+                gain_psum[:, P * b : P * (b + 1)].unsqueeze(1).to_broadcast([P, runs, P]),
                 ALU.mult,
             )
-        words, scales = quantise(w2_first, "w2_first", "total2")
-        for b in range(2):
-            w2_q[0, b] = (words[:, b], scales[:, b])
+        first_words = keep.tile([P, N], U32, name="w2_first_w", tag="total0", align_bytes=64)
+        words, scales = quantise(w2_first, "w2_first", first_words)
+        for n in range(2):
+            for b in range(2):
+                w2_q[n, b] = (words[:, b, P * n : P * (n + 1)], scales[:, b, P * n : P * (n + 1)])
         h_q.append(quantise(woven, "h0"))
-        w2_fourth = keep.tile([P, 1, HALF, PACK], BF16, name="w2_fourth", tag="woven", align_bytes=64)
-        nc.vector.tensor_copy(
-            w2_fourth[:, 0].rearrange("p (c i) t -> p c t i", i=RUN),
-            w2_raw[1][1].rearrange("p (t c i) -> p c t i", t=PACK, i=RUN),
-        )
-        for b, (piece, tag) in enumerate([(w2_third, "total1"), (w2_fourth, None)]):
-            words, scales = quantise(piece, "w2_rest%d" % b, tag)
-            w2_q[1, b] = (words[:, 0], scales[:, 0])
+        w2_fourth = reuse.tile([P, 1, P, PACK], BF16, name="w2_fourth", offset=FIRST_AT, align_bytes=64)
+        weave_page(nc.vector.tensor_copy, w2_fourth[:, 0], 3)
+        third_words = reuse.tile([P, HALF + P], U32, name="w2_third_w", offset=THIRD_WORDS_AT, align_bytes=64)
+        words, scales = quantise(w2_third, "w2_third", third_words)
+        for place, key in enumerate([(2, 0), (3, 0), (2, 1)]):
+            w2_q[key] = (words[:, 0, P * place : P * (place + 1)], scales[:, 0, P * place : P * (place + 1)])
+        words, scales = quantise(w2_fourth, "w2_fourth")
+        w2_q[3, 1] = (words[:, 0], scales[:, 0])
 
         last = SLICES - 1
+        pages = [keep.tile([P, S], F32, name="page", tag="h0_w" if n == 1 else "page%d" % n, align_bytes=64) for n in range(4)]
 
         def first_two(k):
-            bank = second_product([(0, k), (1, k)])
+            if k == 0:
+                ys = [second_product([(n, k)])[:] for n in range(2)]
+            else:
+                bank = second_product([(0, k), (1, k)])
+                ys = [bank[:, WIDTH * n : WIDTH * (n + 1)] for n in range(2)]
             ready = [weighted_tile("page%d_next" % n) for n in range(2)]
             for n in range(2):
-                weigh(nc.vector, ready[n][:], bank[:, WIDTH * n : WIDTH * (n + 1)], WIDTH * k)
+                weigh(nc.vector, ready[n][:], ys[n], WIDTH * k)
             return ready
 
         def by_gpsimd(page, y_psum, j0, tag):
@@ -287,6 +322,7 @@ def tile_list_sorted_poem_gates_kernel(
             ready = first_two(k)
             held_page = 2 if k == last - 1 else 3
             other = second_product([(n, k) for n in range(2, held_page + 1)])
+            take_banks(min(PACK, PACK * (last - k) - AHEAD))
             put_back(0, ready[0], j0)
             if k == 0:
                 third = weighted_tile("page2_next")
@@ -294,20 +330,31 @@ def tile_list_sorted_poem_gates_kernel(
             put_back(1, ready[1], j0)
             if k == 0:
                 put_back(2, third, j0)
-            woven = keep.tile([P, 2, WIDTH, PACK], BF16, name="woven", tag="woven", align_bytes=64)
-            make_h(woven[:, 0], j1, 0)
+            woven = reuse.tile([P, 2, WIDTH, PACK], BF16, name="woven", offset=WOVEN_AT, align_bytes=64)
             if k == last - 1:
+                rooms = [
+                    keep.tile([P, 2 * PACK * WIDTH], F32, name="room", tag="%s%d_0" % (term, j0), align_bytes=64)
+                    for term in ("gain_tanh", "gain_a")
+                ]
+                make_h(woven[:, 0], j1, 0, room=rooms[0][:])
                 for n0 in range(0, WIDTH, PART):
-                    make_h(woven[:, 1, n0 : n0 + PART], j1 + n0, 1)
-                last_term = "gain_a%d_1" % (j1 + PART)
+                    make_h(woven[:, 1, n0 : n0 + PART], j1 + n0, 1, room=rooms[1][:, 2 * PACK * n0 : 2 * PACK * (n0 + PART)])
+                last_term = "gain_tanh%d_1" % (j1 + PART)
             else:
+                make_h(woven[:, 0], j1, 0)
                 between = (lambda tag: by_gpsimd(2, other[:, 0:WIDTH], j0, tag)) if k > 0 else None
                 make_h(woven[:, 1], j1, 1, between)
                 last_term = "gain_a%d_1" % j1
-            held = weighted_tile(last_term)
-            weigh(nc.vector, held[:], other[:, WIDTH * (held_page - 2) : WIDTH * (held_page - 1)], j0)
-            h_q.append(quantise(woven, "h%d" % (k + 1)))
-            put_back(held_page, held, j0)
+            held_y = other[:, WIDTH * (held_page - 2) : WIDTH * (held_page - 1)]
+            if k < last - 1:
+                held = weighted_tile(last_term)
+                weigh(nc.vector, held[:], held_y, j0)
+                h_q.append(quantise(woven, "h%d" % (k + 1)))
+                put_back(held_page, held, j0)
+            else:
+                held = copy_out(held_y, last_term)
+                h_q.append(quantise(woven, "h%d" % (k + 1)))
+                weigh(nc.vector, pages[held_page][:].indirect(places(j0, WIDTH)), held[:], j0)
 
         ready = first_two(last)
         for n in range(2):

@@ -29,14 +29,14 @@ SCALE_ROWS = 96
 PLANE = S + H
 W1_AT = 4 * T
 THIRD_AT = W1_AT + 4 * H
-WOVEN_AT = THIRD_AT + 2 * HALF * PACK
+WOVEN_AT = THIRD_AT + HALF * PACK
 FIRST_AT = WOVEN_AT + 2 * WIDTH * PACK
 THIRD_WORDS_AT = FIRST_AT + 2 * HALF * PACK
-TANH_BUFFERS = 4
+NEXT_AT = THIRD_WORDS_AT + 4 * HALF
+TANH_BUFFERS = 6
 RUN = 4
 PER_COLUMN = 16
-BANKS = 8
-AHEAD = 3
+A_BANKS, Y_BANKS = 5, 3
 
 
 def tile_list_sorted_poem_gates_kernel(
@@ -47,12 +47,8 @@ def tile_list_sorted_poem_gates_kernel(
         keep = ctx.enter_context(tc.tile_pool(name="keep", bufs=1))
         reuse = ctx.enter_context(tc.tile_pool(name="reuse", bufs=1))
         work = ctx.enter_context(tc.tile_pool(name="work", bufs=2))
-        psum = ctx.enter_context(tc.psum_pool(name="psum", bufs=1))
-        taken = []
-
-        def next_bank(width):
-            taken.append(psum.tile([P, width], F32, name="bank", tag="bank%d" % (len(taken) % BANKS)))
-            return taken[-1]
+        psum_a = ctx.enter_context(tc.psum_pool(name="psum_a", bufs=A_BANKS))
+        psum_y = ctx.enter_context(tc.psum_pool(name="psum_y", bufs=Y_BANKS))
 
         offs_sb = keep.tile([P, S // PER_COLUMN], U16, name="offs_sb")
         offs2_sb = keep.tile([P, S // PER_COLUMN], U16, name="offs2_sb")
@@ -106,8 +102,8 @@ def tile_list_sorted_poem_gates_kernel(
             nc.vector.tensor_copy(words[:, j0:j1], window[:].bitcast(U32).indirect(entries))
 
         v_w = [keep.tile([P, S], U32, name="v_w%d" % a, align_bytes=64) for a in range(2)]
-        for j0 in range(0, S, S // 2):
-            gather_words(v_w[0], tab_w0, j0, j0 + S // 2)
+        gather_words(v_w[0], tab_w0, S // 2, S)
+        gather_words(v_w[0], tab_w0, 0, S // 2)
         gather_words(v_w[1], tab_w1, 0, WIDTH)
         gather_words(v_w[1], tab_w1, WIDTH, S)
 
@@ -121,19 +117,20 @@ def tile_list_sorted_poem_gates_kernel(
 
         def into_psum(values):
             width = values.shape[1]
-            turned = next_bank(width)
+            turned = psum_y.tile([P, width], F32, name="y_bank")
             for c0 in range(0, width, P):
                 nc.tensor.transpose(turned[:, c0 : c0 + P], values[:, c0 : c0 + P], identity[:])
             turned_sb = work.tile([P, width], F32, name="turned_sb")
             nc.scalar.copy(turned_sb[:], turned[:])
-            upright = next_bank(width)
+            upright = psum_y.tile([P, width], F32, name="y_bank")
             for c0 in range(0, width, P):
                 nc.tensor.transpose(upright[:, c0 : c0 + P], turned_sb[:, c0 : c0 + P], identity[:])
             return upright
 
         gain_woven = keep.tile([P, 2, P // PACK, PACK], F32, name="gain_woven", align_bytes=64)
         nc.scalar.copy(gain_woven[:], gain_sb[:].unsqueeze(2).to_broadcast([P, 2, P // PACK, PACK]))
-        gain_psum = into_psum(gain_woven[:].rearrange("p b n t -> p (b n t)"))
+        gain_flat = gain_woven[:].rearrange("p b n t -> p (b n t)")
+        gain_psum = into_psum(gain_flat)
 
         w2_rows = w2.rearrange("(b p t) (half n) -> half b p t n", b=2, t=PACK, half=2)
         w2_width = PACK * HALF
@@ -154,10 +151,6 @@ def tile_list_sorted_poem_gates_kernel(
             raw = w2_raw[half][b].rearrange("p (t n) -> p n t", t=PACK)
             nc.gpsimd.tensor_scalar(woven, raw, 1.0, 0.0, ALU.mult, ALU.add)
 
-        def weave_page(copy, woven, n):
-            raw = w2_raw[1][1].rearrange("p (t n) -> p t n", t=PACK)[:, :, P * (n - 2) : P * (n - 1)]
-            copy(woven.rearrange("p (c i) t -> p c t i", i=RUN), raw.rearrange("p t (c i) -> p c t i", i=RUN))
-
         def quantise(woven, name, words=None):
             passes = woven.shape[1]
             count = passes * woven.shape[2]
@@ -169,15 +162,8 @@ def tile_list_sorted_poem_gates_kernel(
             )
             return [tile[:].rearrange("p (b n) -> p b n", b=passes) for tile in (words, scales)]
 
-        a_banks = []
-
-        def take_banks(count):
-            a_banks.extend([next_bank(BANK) for place in range(count)])
-
-        take_banks(PACK + AHEAD)
-
         def first_product(b, parts):
-            bank = a_banks.pop(0)
+            bank = psum_a.tile([P, BANK], F32, name="a_bank")
             width = BANK // len(parts)
             for a in range(2):
                 for place, (t, j) in enumerate(parts):
@@ -229,7 +215,7 @@ def tile_list_sorted_poem_gates_kernel(
         w2_q = {}
 
         def second_product(chosen):
-            bank = next_bank(WIDTH * len(chosen))
+            bank = psum_y.tile([P, WIDTH * len(chosen)], F32, name="y_bank")
             for place, (n, k) in enumerate(chosen):
                 for b in range(2):
                     nc.tensor.matmul_mx(
@@ -261,52 +247,58 @@ def tile_list_sorted_poem_gates_kernel(
             nc.vector.tensor_copy(pages[page][:].indirect(places(j0, weighted.shape[1])), weighted[:])
 
         w2_first = reuse.tile([P, 2, HALF, PACK], BF16, name="w2_first", offset=FIRST_AT, align_bytes=64)
-        w2_third = reuse.tile([P, 1, HALF + P, PACK], BF16, name="w2_third", offset=THIRD_AT, align_bytes=64)
+        w2_third = reuse.tile([P, 1, HALF, PACK], BF16, name="w2_third", offset=THIRD_AT, align_bytes=64)
         for b in range(2):
             weave_on_gpsimd(w2_first[:, b], 0, b)
         weave_on_gpsimd(w2_third[:, 0, 0:HALF], 1, 0)
-        sums = [keep.tile([P, WIDTH, PACK], F32, name="total", tag=tag, align_bytes=64) for tag in ("total0", "total1")]
-        for b in range(2):
+
+        def sum_on_vector(total, b, j0):
             for n0 in range(0, WIDTH, PART):
-                woven_a = first_product(b, [(t, n0) for t in range(PACK)])[:].rearrange("p (t j) -> p j t", t=PACK)
+                woven_a = first_product(b, [(t, j0 + n0) for t in range(PACK)])[:].rearrange("p (t j) -> p j t", t=PACK)
                 tanh_a = work.tile([P, PART, PACK], F32, name="tanh_a", bufs=TANH_BUFFERS)
                 nc.scalar.activation(tanh_a[:], woven_a, ACT.Tanh)
-                nc.vector.tensor_tensor(sums[b][:, n0 : n0 + PART, :], woven_a, tanh_a[:], ALU.add)
-        weave_page(nc.scalar.copy, w2_third[:, 0, HALF:], 2)
-        woven = keep.tile([P, 2, WIDTH, PACK], BF16, name="woven_first", align_bytes=64)
+                nc.vector.tensor_tensor(total[:, n0 : n0 + PART, :], woven_a, tanh_a[:], ALU.add)
 
-        runs = WIDTH * PACK // P
-        for b in range(2):
-            nc.vector.tensor_tensor(
-                woven[:, b].rearrange("p (m n) t -> p m (n t)", m=runs),
-                sums[b][:].rearrange("p (m n) t -> p m (n t)", m=runs),
-                gain_psum[:, P * b : P * (b + 1)].unsqueeze(1).to_broadcast([P, runs, P]),
+        def times_gain(engine, h_out, total, gains, b):
+            runs = total.shape[1] * PACK // P
+            engine.tensor_tensor(
+                h_out.rearrange("p (m n) t -> p m (n t)", m=runs),
+                total[:].rearrange("p (m n) t -> p m (n t)", m=runs),
+                gains[:, P * b : P * (b + 1)].unsqueeze(1).to_broadcast([P, runs, P]),
                 ALU.mult,
             )
+
+        sums = [keep.tile([P, WIDTH, PACK], F32, name="total", tag="total%d" % b, align_bytes=64) for b in range(2)]
+        for b in range(2):
+            sum_on_vector(sums[b], b, 0)
+        woven = keep.tile([P, 2, WIDTH, PACK], BF16, name="woven_first", align_bytes=64)
+        for b in range(2):
+            times_gain(nc.vector, woven[:, b], sums[b], gain_psum, b)
         first_words = keep.tile([P, N], U32, name="w2_first_w", tag="total0", align_bytes=64)
         words, scales = quantise(w2_first, "w2_first", first_words)
         for n in range(2):
             for b in range(2):
                 w2_q[n, b] = (words[:, b, P * n : P * (n + 1)], scales[:, b, P * n : P * (n + 1)])
         h_q.append(quantise(woven, "h0"))
-        w2_fourth = reuse.tile([P, 1, P, PACK], BF16, name="w2_fourth", offset=FIRST_AT, align_bytes=64)
-        weave_page(nc.vector.tensor_copy, w2_fourth[:, 0], 3)
-        third_words = reuse.tile([P, HALF + P], U32, name="w2_third_w", offset=THIRD_WORDS_AT, align_bytes=64)
-        words, scales = quantise(w2_third, "w2_third", third_words)
-        for place, key in enumerate([(2, 0), (3, 0), (2, 1)]):
-            w2_q[key] = (words[:, 0, P * place : P * (place + 1)], scales[:, 0, P * place : P * (place + 1)])
-        words, scales = quantise(w2_fourth, "w2_fourth")
-        w2_q[3, 1] = (words[:, 0], scales[:, 0])
+        next_slice = reuse.tile([P, WIDTH, PACK], F32, name="next_slice", offset=NEXT_AT, align_bytes=64)
+        sum_on_vector(next_slice, 0, WIDTH)
+        w2_fourth = reuse.tile([P, 1, HALF, PACK], BF16, name="w2_fourth", offset=FIRST_AT, align_bytes=64)
+        nc.vector.tensor_copy(
+            w2_fourth[:, 0].rearrange("p (c i) t -> p c t i", i=RUN),
+            w2_raw[1][1].rearrange("p (t c i) -> p c t i", t=PACK, i=RUN),
+        )
+        third_words = reuse.tile([P, HALF], U32, name="w2_third_w", offset=THIRD_WORDS_AT, align_bytes=64)
+        for b, (piece, words) in enumerate([(w2_third, third_words), (w2_fourth, None)]):
+            words, scales = quantise(piece, "w2_rest%d" % b, words)
+            for n in range(2):
+                w2_q[2 + n, b] = (words[:, 0, P * n : P * (n + 1)], scales[:, 0, P * n : P * (n + 1)])
 
         last = SLICES - 1
         pages = [keep.tile([P, S], F32, name="page", tag="h0_w" if n == 1 else "page%d" % n, align_bytes=64) for n in range(4)]
 
         def first_two(k):
-            if k == 0:
-                ys = [second_product([(n, k)])[:] for n in range(2)]
-            else:
-                bank = second_product([(0, k), (1, k)])
-                ys = [bank[:, WIDTH * n : WIDTH * (n + 1)] for n in range(2)]
+            bank = second_product([(0, k), (1, k)])
+            ys = [bank[:, WIDTH * n : WIDTH * (n + 1)] for n in range(2)]
             ready = [weighted_tile("page%d_next" % n) for n in range(2)]
             for n in range(2):
                 weigh(nc.vector, ready[n][:], ys[n], WIDTH * k)
@@ -321,8 +313,7 @@ def tile_list_sorted_poem_gates_kernel(
             j0, j1 = WIDTH * k, WIDTH * (k + 1)
             ready = first_two(k)
             held_page = 2 if k == last - 1 else 3
-            other = second_product([(n, k) for n in range(2, held_page + 1)])
-            take_banks(min(PACK, PACK * (last - k) - AHEAD))
+            other = second_product([(2, k), (3, k)])
             put_back(0, ready[0], j0)
             if k == 0:
                 third = weighted_tile("page2_next")
@@ -341,7 +332,10 @@ def tile_list_sorted_poem_gates_kernel(
                     make_h(woven[:, 1, n0 : n0 + PART], j1 + n0, 1, room=rooms[1][:, 2 * PACK * n0 : 2 * PACK * (n0 + PART)])
                 last_term = "gain_tanh%d_1" % (j1 + PART)
             else:
-                make_h(woven[:, 0], j1, 0)
+                if k == 0:
+                    times_gain(nc.gpsimd, woven[:, 0], next_slice, gain_flat, 0)
+                else:
+                    make_h(woven[:, 0], j1, 0)
                 between = (lambda tag: by_gpsimd(2, other[:, 0:WIDTH], j0, tag)) if k > 0 else None
                 make_h(woven[:, 1], j1, 1, between)
                 last_term = "gain_a%d_1" % j1
@@ -355,12 +349,16 @@ def tile_list_sorted_poem_gates_kernel(
                 held = copy_out(held_y, last_term)
                 h_q.append(quantise(woven, "h%d" % (k + 1)))
                 weigh(nc.vector, pages[held_page][:].indirect(places(j0, WIDTH)), held[:], j0)
+                closing = reuse.tile([P, 2 * WIDTH], F32, name="closing", offset=WOVEN_AT, align_bytes=64)
+                weigh(nc.gpsimd, closing[:, 0:WIDTH], copy_out(other[:, WIDTH:], "y_kept")[:], j0)
 
         ready = first_two(last)
         for n in range(2):
             put_back(n, ready[n], WIDTH * last)
-        by_gpsimd(2, second_product([(2, last)])[:], WIDTH * last, "y_last2")
-        by_gpsimd(3, second_product([(3, last - 1), (3, last)])[:], WIDTH * (last - 1), "y_last3")
+        other = second_product([(2, last), (3, last)])
+        by_gpsimd(2, other[:, 0:WIDTH], WIDTH * last, "y_last2")
+        weigh(nc.gpsimd, closing[:, WIDTH:], copy_out(other[:, WIDTH:], "y_last3")[:], WIDTH * last)
+        put_back(3, closing, WIDTH * (last - 1))
 
         def finish(n, c0, engine, gate, result):
             width = result.shape[1]

@@ -32,8 +32,7 @@ THIRD_AT = W1_AT + 4 * H
 WOVEN_AT = THIRD_AT + HALF * PACK
 FIRST_AT = WOVEN_AT + 2 * WIDTH * PACK
 THIRD_WORDS_AT = FIRST_AT + 2 * HALF * PACK
-NEXT_AT = THIRD_WORDS_AT + 4 * HALF
-TANH_BUFFERS = 6
+TANH_BUFFERS = 4
 RUN = 4
 PER_COLUMN = 16
 A_BANKS, Y_BANKS = 5, 3
@@ -129,8 +128,7 @@ def tile_list_sorted_poem_gates_kernel(
 
         gain_woven = keep.tile([P, 2, P // PACK, PACK], F32, name="gain_woven", align_bytes=64)
         nc.scalar.copy(gain_woven[:], gain_sb[:].unsqueeze(2).to_broadcast([P, 2, P // PACK, PACK]))
-        gain_flat = gain_woven[:].rearrange("p b n t -> p (b n t)")
-        gain_psum = into_psum(gain_flat)
+        gain_psum = into_psum(gain_woven[:].rearrange("p b n t -> p (b n t)"))
 
         w2_rows = w2.rearrange("(b p t) (half n) -> half b p t n", b=2, t=PACK, half=2)
         w2_width = PACK * HALF
@@ -253,35 +251,34 @@ def tile_list_sorted_poem_gates_kernel(
         weave_on_gpsimd(w2_third[:, 0, 0:HALF], 1, 0)
 
         def sum_on_vector(total, b, j0):
-            for n0 in range(0, WIDTH, PART):
+            for n0 in range(0, total.shape[1], PART):
                 woven_a = first_product(b, [(t, j0 + n0) for t in range(PACK)])[:].rearrange("p (t j) -> p j t", t=PACK)
                 tanh_a = work.tile([P, PART, PACK], F32, name="tanh_a", bufs=TANH_BUFFERS)
                 nc.scalar.activation(tanh_a[:], woven_a, ACT.Tanh)
                 nc.vector.tensor_tensor(total[:, n0 : n0 + PART, :], woven_a, tanh_a[:], ALU.add)
 
-        def times_gain(engine, h_out, total, gains, b):
+        def times_gain(h_out, total, b):
             runs = total.shape[1] * PACK // P
-            engine.tensor_tensor(
+            nc.vector.tensor_tensor(
                 h_out.rearrange("p (m n) t -> p m (n t)", m=runs),
                 total[:].rearrange("p (m n) t -> p m (n t)", m=runs),
-                gains[:, P * b : P * (b + 1)].unsqueeze(1).to_broadcast([P, runs, P]),
+                gain_psum[:, P * b : P * (b + 1)].unsqueeze(1).to_broadcast([P, runs, P]),
                 ALU.mult,
             )
 
-        sums = [keep.tile([P, WIDTH, PACK], F32, name="total", tag="total%d" % b, align_bytes=64) for b in range(2)]
-        for b in range(2):
-            sum_on_vector(sums[b], b, 0)
+        parts = [(0, 0, WIDTH), (1, 0, PART), (1, PART, PART)]
+        sums = [keep.tile([P, count, PACK], F32, name="total", tag="total%d_%d" % (b, n0), align_bytes=64) for b, n0, count in parts]
+        for total, (b, n0, count) in zip(sums, parts):
+            sum_on_vector(total, b, n0)
         woven = keep.tile([P, 2, WIDTH, PACK], BF16, name="woven_first", align_bytes=64)
-        for b in range(2):
-            times_gain(nc.vector, woven[:, b], sums[b], gain_psum, b)
-        first_words = keep.tile([P, N], U32, name="w2_first_w", tag="total0", align_bytes=64)
+        for total, (b, n0, count) in zip(sums, parts):
+            times_gain(woven[:, b, n0 : n0 + count], total, b)
+        first_words = keep.tile([P, N], U32, name="w2_first_w", tag="total1_0", align_bytes=64)
         words, scales = quantise(w2_first, "w2_first", first_words)
         for n in range(2):
             for b in range(2):
                 w2_q[n, b] = (words[:, b, P * n : P * (n + 1)], scales[:, b, P * n : P * (n + 1)])
         h_q.append(quantise(woven, "h0"))
-        next_slice = reuse.tile([P, WIDTH, PACK], F32, name="next_slice", offset=NEXT_AT, align_bytes=64)
-        sum_on_vector(next_slice, 0, WIDTH)
         w2_fourth = reuse.tile([P, 1, HALF, PACK], BF16, name="w2_fourth", offset=FIRST_AT, align_bytes=64)
         nc.vector.tensor_copy(
             w2_fourth[:, 0].rearrange("p (c i) t -> p c t i", i=RUN),
@@ -332,10 +329,7 @@ def tile_list_sorted_poem_gates_kernel(
                     make_h(woven[:, 1, n0 : n0 + PART], j1 + n0, 1, room=rooms[1][:, 2 * PACK * n0 : 2 * PACK * (n0 + PART)])
                 last_term = "gain_tanh%d_1" % (j1 + PART)
             else:
-                if k == 0:
-                    times_gain(nc.gpsimd, woven[:, 0], next_slice, gain_flat, 0)
-                else:
-                    make_h(woven[:, 0], j1, 0)
+                make_h(woven[:, 0], j1, 0)
                 between = (lambda tag: by_gpsimd(2, other[:, 0:WIDTH], j0, tag)) if k > 0 else None
                 make_h(woven[:, 1], j1, 1, between)
                 last_term = "gain_a%d_1" % j1

@@ -248,7 +248,7 @@ def tile_list_sorted_poem_gates_kernel(
         w2_third = reuse.tile([P, 1, HALF, PACK], BF16, name="w2_third", offset=THIRD_AT, align_bytes=64)
         for b in range(2):
             weave_on_gpsimd(w2_first[:, b], 0, b)
-        weave_on_gpsimd(w2_third[:, 0, 0:HALF], 1, 0)
+        weave_on_gpsimd(w2_third[:, 0], 1, 0)
 
         def sum_on_vector(total, b, j0):
             for n0 in range(0, total.shape[1], PART):
@@ -266,32 +266,37 @@ def tile_list_sorted_poem_gates_kernel(
                 ALU.mult,
             )
 
-        parts = [(0, 0, WIDTH), (1, 0, PART), (1, PART, PART)]
-        sums = [keep.tile([P, count, PACK], F32, name="total", tag="total%d_%d" % (b, n0), align_bytes=64) for b, n0, count in parts]
-        for total, (b, n0, count) in zip(sums, parts):
+        pieces = [(0, 0, WIDTH), (1, 0, PART), (1, PART, PART)]
+        sums = [
+            keep.tile([P, count, PACK], F32, name="total", tag="total%d_%d" % (b, n0), align_bytes=64)
+            for b, n0, count in pieces
+        ]
+        for total, (b, n0, count) in zip(sums, pieces):
             sum_on_vector(total, b, n0)
-        woven = keep.tile([P, 2, WIDTH, PACK], BF16, name="woven_first", align_bytes=64)
-        for total, (b, n0, count) in zip(sums, parts):
-            times_gain(woven[:, b, n0 : n0 + count], total, b)
+        woven_first = keep.tile([P, 2, WIDTH, PACK], BF16, name="woven_first", align_bytes=64)
+        for total, (b, n0, count) in zip(sums, pieces):
+            times_gain(woven_first[:, b, n0 : n0 + count], total, b)
         first_words = keep.tile([P, N], U32, name="w2_first_w", tag="total1_0", align_bytes=64)
         words, scales = quantise(w2_first, "w2_first", first_words)
         for n in range(2):
             for b in range(2):
                 w2_q[n, b] = (words[:, b, P * n : P * (n + 1)], scales[:, b, P * n : P * (n + 1)])
-        h_q.append(quantise(woven, "h0"))
+        h_q.append(quantise(woven_first, "h0"))
         w2_fourth = reuse.tile([P, 1, HALF, PACK], BF16, name="w2_fourth", offset=FIRST_AT, align_bytes=64)
         nc.vector.tensor_copy(
             w2_fourth[:, 0].rearrange("p (c i) t -> p c t i", i=RUN),
             w2_raw[1][1].rearrange("p (t c i) -> p c t i", t=PACK, i=RUN),
         )
         third_words = reuse.tile([P, HALF], U32, name="w2_third_w", offset=THIRD_WORDS_AT, align_bytes=64)
-        for b, (piece, words) in enumerate([(w2_third, third_words), (w2_fourth, None)]):
-            words, scales = quantise(piece, "w2_rest%d" % b, words)
+        for b, (quarter, target) in enumerate([(w2_third, third_words), (w2_fourth, None)]):
+            words, scales = quantise(quarter, "w2_rest%d" % b, target)
             for n in range(2):
                 w2_q[2 + n, b] = (words[:, 0, P * n : P * (n + 1)], scales[:, 0, P * n : P * (n + 1)])
 
         last = SLICES - 1
-        pages = [keep.tile([P, S], F32, name="page", tag="h0_w" if n == 1 else "page%d" % n, align_bytes=64) for n in range(4)]
+        pages = [
+            keep.tile([P, S], F32, name="page", tag="h0_w" if n == 1 else "page%d" % n, align_bytes=64) for n in range(4)
+        ]
 
         def first_two(k):
             bank = second_product([(0, k), (1, k)])
@@ -313,11 +318,11 @@ def tile_list_sorted_poem_gates_kernel(
             other = second_product([(2, k), (3, k)])
             put_back(0, ready[0], j0)
             if k == 0:
-                third = weighted_tile("page2_next")
-                weigh(nc.vector, third[:], other[:, 0:WIDTH], j0)
+                page2 = weighted_tile("page2_next")
+                weigh(nc.vector, page2[:], other[:, 0:WIDTH], j0)
             put_back(1, ready[1], j0)
             if k == 0:
-                put_back(2, third, j0)
+                put_back(2, page2, j0)
             woven = reuse.tile([P, 2, WIDTH, PACK], BF16, name="woven", offset=WOVEN_AT, align_bytes=64)
             if k == last - 1:
                 rooms = [
@@ -326,7 +331,8 @@ def tile_list_sorted_poem_gates_kernel(
                 ]
                 make_h(woven[:, 0], j1, 0, room=rooms[0][:])
                 for n0 in range(0, WIDTH, PART):
-                    make_h(woven[:, 1, n0 : n0 + PART], j1 + n0, 1, room=rooms[1][:, 2 * PACK * n0 : 2 * PACK * (n0 + PART)])
+                    room = rooms[1][:, 2 * PACK * n0 : 2 * PACK * (n0 + PART)]
+                    make_h(woven[:, 1, n0 : n0 + PART], j1 + n0, 1, room=room)
                 last_term = "gain_tanh%d_1" % (j1 + PART)
             else:
                 make_h(woven[:, 0], j1, 0)
@@ -349,9 +355,8 @@ def tile_list_sorted_poem_gates_kernel(
         ready = first_two(last)
         for n in range(2):
             put_back(n, ready[n], WIDTH * last)
-        other = second_product([(2, last), (3, last)])
-        by_gpsimd(2, other[:, 0:WIDTH], WIDTH * last, "y_last2")
-        weigh(nc.gpsimd, closing[:, WIDTH:], copy_out(other[:, WIDTH:], "y_last3")[:], WIDTH * last)
+        by_gpsimd(2, second_product([(2, last)])[:], WIDTH * last, "y_last2")
+        weigh(nc.gpsimd, closing[:, WIDTH:], copy_out(second_product([(3, last)])[:], "y_last3")[:], WIDTH * last)
         put_back(3, closing, WIDTH * (last - 1))
 
         def finish(n, c0, engine, gate, result):
@@ -361,8 +366,8 @@ def tile_list_sorted_poem_gates_kernel(
             nc.sync.dma_start(out[P * n : P * (n + 1), c0 : c0 + width], result)
 
         gates = keep.tile([P, 4, S], F32, name="gates", tag="y_last2", align_bytes=64)
-        on_gpsimd = [(0, 0, WIDTH), (0, WIDTH, WIDTH), (0, BANK, BANK), (1, 0, BANK), (1, BANK, BANK), (2, 0, WIDTH)]
-        on_vector = [(2, WIDTH, WIDTH), (2, BANK, BANK), (3, 0, BANK), (3, BANK, WIDTH), (3, BANK + WIDTH, WIDTH)]
+        on_gpsimd = [(0, 0, WIDTH), (0, WIDTH, WIDTH), (0, BANK, BANK), (1, 0, BANK), (1, BANK, BANK), (2, 0, PART)]
+        on_vector = [(2, PART, BANK - PART), (2, BANK, BANK), (3, 0, BANK), (3, BANK, WIDTH), (3, BANK + WIDTH, WIDTH)]
         last_gate = keep.tile([P, on_gpsimd[-1][2]], F32, name="last_gate", tag="y_last3", align_bytes=64)
         for n, c0, width in on_gpsimd:
             gate = last_gate[:] if (n, c0, width) == on_gpsimd[-1] else gates[:, n, c0 : c0 + width]

@@ -314,8 +314,8 @@ def tile_list_sorted_poem_gates_kernel(
         for k in range(last):
             j0, j1 = WIDTH * k, WIDTH * (k + 1)
             ready = first_two(k)
-            held_page = 2 if k == last - 1 else 3
-            other = second_product([(2, k), (3, k)])
+            held_page = 3 if k == 0 else 2
+            other = second_product([(2, k), (3, k)] if k == 0 else [(2, k)])
             put_back(0, ready[0], j0)
             if k == 0:
                 page2 = weighted_tile("page2_next")
@@ -336,8 +336,7 @@ def tile_list_sorted_poem_gates_kernel(
                 last_term = "gain_tanh%d_1" % (j1 + PART)
             else:
                 make_h(woven[:, 0], j1, 0)
-                between = (lambda tag: by_gpsimd(2, other[:, 0:WIDTH], j0, tag)) if k > 0 else None
-                make_h(woven[:, 1], j1, 1, between)
+                make_h(woven[:, 1], j1, 1)
                 last_term = "gain_a%d_1" % j1
             held_y = other[:, WIDTH * (held_page - 2) : WIDTH * (held_page - 1)]
             if k < last - 1:
@@ -349,15 +348,17 @@ def tile_list_sorted_poem_gates_kernel(
                 held = copy_out(held_y, last_term)
                 h_q.append(quantise(woven, "h%d" % (k + 1)))
                 weigh(nc.vector, pages[held_page][:].indirect(places(j0, WIDTH)), held[:], j0)
-                closing = reuse.tile([P, 2 * WIDTH], F32, name="closing", offset=WOVEN_AT, align_bytes=64)
-                weigh(nc.gpsimd, closing[:, 0:WIDTH], copy_out(other[:, WIDTH:], "y_kept")[:], j0)
+                kept = keep.tile([P, last * WIDTH], F32, name="kept", tag="y_last3", align_bytes=64)
+                nc.scalar.copy(kept[:, 0 : j0], second_product([(3, k - 1), (3, k)])[:])
 
         ready = first_two(last)
         for n in range(2):
             put_back(n, ready[n], WIDTH * last)
         by_gpsimd(2, second_product([(2, last)])[:], WIDTH * last, "y_last2")
-        weigh(nc.gpsimd, closing[:, WIDTH:], copy_out(second_product([(3, last)])[:], "y_last3")[:], WIDTH * last)
-        put_back(3, closing, WIDTH * (last - 1))
+        nc.scalar.copy(kept[:, WIDTH * (last - 1) :], second_product([(3, last)])[:])
+        closing = keep.tile([P, last * WIDTH], F32, name="closing", align_bytes=64)
+        weigh(nc.gpsimd, closing[:], kept[:], WIDTH)
+        put_back(3, closing, WIDTH)
 
         def finish(n, c0, engine, gate, result):
             width = result.shape[1]
@@ -366,8 +367,8 @@ def tile_list_sorted_poem_gates_kernel(
             nc.sync.dma_start(out[P * n : P * (n + 1), c0 : c0 + width], result)
 
         gates = keep.tile([P, 4, S], F32, name="gates", tag="y_last2", align_bytes=64)
-        on_gpsimd = [(0, 0, WIDTH), (0, WIDTH, WIDTH), (0, BANK, BANK), (1, 0, BANK), (1, BANK, BANK), (2, 0, PART)]
-        on_vector = [(2, PART, BANK - PART), (2, BANK, BANK), (3, 0, BANK), (3, BANK, WIDTH), (3, BANK + WIDTH, WIDTH)]
+        on_gpsimd = [(0, 0, WIDTH), (0, WIDTH, S - WIDTH), (1, 0, BANK), (1, BANK, BANK), (2, 0, BANK + PART)]
+        on_vector = [(2, BANK + PART, BANK - PART), (3, 0, BANK), (3, BANK, WIDTH), (3, BANK + WIDTH, WIDTH)]
         last_gate = keep.tile([P, on_gpsimd[-1][2]], F32, name="last_gate", tag="y_last3", align_bytes=64)
         for n, c0, width in on_gpsimd:
             gate = last_gate[:] if (n, c0, width) == on_gpsimd[-1] else gates[:, n, c0 : c0 + width]

@@ -348,16 +348,15 @@ def tile_list_sorted_poem_gates_kernel(
                 held = copy_out(held_y, last_term)
                 h_q.append(quantise(woven, "h%d" % (k + 1)))
                 weigh(nc.vector, pages[held_page][:].indirect(places(j0, WIDTH)), held[:], j0)
-                kept = keep.tile([P, last * WIDTH], F32, name="kept", tag="y_last3", align_bytes=64)
-                nc.scalar.copy(kept[:, 0 : j0], second_product([(3, k - 1), (3, k)])[:])
+                closing = reuse.tile([P, last * WIDTH], F32, name="closing", offset=WOVEN_AT, align_bytes=64)
+                kept = copy_out(second_product([(3, k - 1), (3, k)])[:], "y_kept")
+                weigh(nc.gpsimd, closing[:, 0:j0], kept[:], WIDTH)
 
         ready = first_two(last)
         for n in range(2):
             put_back(n, ready[n], WIDTH * last)
         by_gpsimd(2, second_product([(2, last)])[:], WIDTH * last, "y_last2")
-        nc.scalar.copy(kept[:, WIDTH * (last - 1) :], second_product([(3, last)])[:])
-        closing = keep.tile([P, last * WIDTH], F32, name="closing", align_bytes=64)
-        weigh(nc.gpsimd, closing[:], kept[:], WIDTH)
+        weigh(nc.gpsimd, closing[:, WIDTH * (last - 1) :], copy_out(second_product([(3, last)])[:], "y_last3")[:], WIDTH * last)
         put_back(3, closing, WIDTH)
 
         def finish(n, c0, engine, gate, result):
@@ -367,8 +366,8 @@ def tile_list_sorted_poem_gates_kernel(
             nc.sync.dma_start(out[P * n : P * (n + 1), c0 : c0 + width], result)
 
         gates = keep.tile([P, 4, S], F32, name="gates", tag="y_last2", align_bytes=64)
-        on_gpsimd = [(0, 0, WIDTH), (0, WIDTH, S - WIDTH), (1, 0, BANK), (1, BANK, BANK), (2, 0, BANK + PART)]
-        on_vector = [(2, BANK + PART, BANK - PART), (3, 0, BANK), (3, BANK, WIDTH), (3, BANK + WIDTH, WIDTH)]
+        on_gpsimd = [(0, 0, WIDTH), (0, WIDTH, S - WIDTH), (1, 0, S), (2, 0, BANK)]
+        on_vector = [(2, BANK, BANK), (3, 0, 3 * PART), (3, 3 * PART, 3 * PART), (3, S - WIDTH, WIDTH)]
         last_gate = keep.tile([P, on_gpsimd[-1][2]], F32, name="last_gate", tag="y_last3", align_bytes=64)
         for n, c0, width in on_gpsimd:
             gate = last_gate[:] if (n, c0, width) == on_gpsimd[-1] else gates[:, n, c0 : c0 + width]

@@ -177,26 +177,17 @@ def tile_list_sorted_poem_gates_kernel(
                     )
             return bank
 
-        def make_h(h_out, j0, b, between=None, room=None):
+        def make_h(h_out, j0, b):
             width = h_out.shape[1]
             shape = [P, width // RUN, PACK, RUN]
             gain_tanh = keep.tile(shape, F32, name="gain_tanh", tag="gain_tanh%d_%d" % (j0, b), align_bytes=64)
-            if room is None:
-                gain_a = keep.tile(shape, F32, name="gain_a", tag="gain_a%d_%d" % (j0, b), align_bytes=64)[:]
-            else:
-                gain_a = room[:, PACK * width :].rearrange("p (c t i) -> p c t i", t=PACK, i=RUN)
+            gain_a = keep.tile(shape, F32, name="gain_a", tag="gain_a%d_%d" % (j0, b), align_bytes=64)
             per_bank = BANK // width
             for t0 in range(0, PACK, per_bank):
                 ts = range(t0, t0 + per_bank)
                 bank = first_product(b, [(t, j0) for t in ts])
-                marked = between is not None and t0 == 0
-                if room is not None:
-                    tanh_a = room[:, width * t0 : width * t0 + BANK]
-                elif marked:
-                    tanh_a = keep.tile([P, BANK], F32, name="tanh_mark", tag="tanh_mark%d" % j0, align_bytes=64)[:]
-                else:
-                    tanh_a = work.tile([P, BANK], F32, name="tanh_a", bufs=TANH_BUFFERS)[:]
-                nc.scalar.activation(tanh_a, bank[:], ACT.Tanh)
+                tanh_a = work.tile([P, BANK], F32, name="tanh_a", bufs=TANH_BUFFERS)
+                nc.scalar.activation(tanh_a[:], bank[:], ACT.Tanh)
                 for t in ts:
                     cols = slice(width * (t - t0), width * (t - t0 + 1))
                     source = bank[:, cols].rearrange("p (c i) -> p c i", i=RUN)
@@ -205,9 +196,7 @@ def tile_list_sorted_poem_gates_kernel(
                     cols = slice(width * (t - t0), width * (t - t0 + 1))
                     source = tanh_a[:, cols].rearrange("p (c i) -> p c i", i=RUN)
                     nc.scalar.activation(gain_tanh[:, :, t, :], source, ACT.Copy, scale=gain_sb[:, b, t : t + 1])
-                if marked:
-                    between("tanh_mark%d" % j0)
-            nc.gpsimd.tensor_tensor(h_out.rearrange("p (c i) t -> p c t i", i=RUN), gain_a, gain_tanh[:], ALU.add)
+            nc.gpsimd.tensor_tensor(h_out.rearrange("p (c i) t -> p c t i", i=RUN), gain_a[:], gain_tanh[:], ALU.add)
 
         h_q = []
         w2_q = {}
@@ -266,16 +255,43 @@ def tile_list_sorted_poem_gates_kernel(
                 ALU.mult,
             )
 
-        pieces = [(0, 0, WIDTH), (1, 0, PART), (1, PART, PART)]
+        def sum_on_tensor(b, j0):
+            bank = psum_a.tile([P, BANK], F32, name="a_bank")
+            for a in range(2):
+                nc.tensor.matmul_mx(
+                    out=bank[:],
+                    lhsT=v_w[a][:, j0 : j0 + P].bitcast(FP8X4),
+                    lhsT_scale=planes[:, PLANE * a + j0 : PLANE * a + j0 + P],
+                    rhs=w1_w[:, a, 2 * PASS * b : 2 * PASS * (b + 1)].bitcast(FP4X4),
+                    rhs_scale=planes[:, PLANE * a + S + PASS * b : PLANE * a + S + PASS * (b + 1)],
+                    start=(a == 0),
+                    stop=(a == 1),
+                )
+            terms = [keep.tile([P, BANK], F32, name="term%d" % i, align_bytes=64) for i in range(2)]
+            nc.scalar.activation(terms[0][:], bank[:], ACT.Tanh)
+            nc.scalar.copy(terms[1][:], bank[:])
+            total = psum_y.tile([P, BANK], F32, name="y_bank")
+            for i, term in enumerate(terms):
+                for t in range(PACK):
+                    cols = slice(P * t, P * (t + 1))
+                    first, final = (i, t) == (0, 0), (i, t) == (1, PACK - 1)
+                    nc.tensor.matmul(total[:, cols], term[:, cols], identity[:], start=first, stop=final, is_transpose=True)
+            return total[:].rearrange("p (t j) -> p j t", t=PACK)
+
+        pieces = [(0, 0, WIDTH), (1, 0, PART)]
         sums = [
             keep.tile([P, count, PACK], F32, name="total", tag="total%d_%d" % (b, n0), align_bytes=64)
             for b, n0, count in pieces
         ]
         for total, (b, n0, count) in zip(sums, pieces):
             sum_on_vector(total, b, n0)
+        turned_sum = sum_on_tensor(1, PART)
         woven_first = keep.tile([P, 2, WIDTH, PACK], BF16, name="woven_first", align_bytes=64)
         for total, (b, n0, count) in zip(sums, pieces):
             times_gain(woven_first[:, b, n0 : n0 + count], total, b)
+        nc.vector.tensor_tensor(
+            woven_first[:, 1, PART:], turned_sum, gain_sb[:, 1:2, :].to_broadcast([P, PART, PACK]), ALU.mult
+        )
         first_words = keep.tile([P, N], U32, name="w2_first_w", tag="total1_0", align_bytes=64)
         words, scales = quantise(w2_first, "w2_first", first_words)
         for n in range(2):
@@ -325,14 +341,9 @@ def tile_list_sorted_poem_gates_kernel(
                 put_back(2, page2, j0)
             woven = reuse.tile([P, 2, WIDTH, PACK], BF16, name="woven", offset=WOVEN_AT, align_bytes=64)
             if k == last - 1:
-                rooms = [
-                    keep.tile([P, 2 * PACK * WIDTH], F32, name="room", tag="%s%d_0" % (term, j0), align_bytes=64)
-                    for term in ("gain_tanh", "gain_a")
-                ]
-                make_h(woven[:, 0], j1, 0, room=rooms[0][:])
+                make_h(woven[:, 0], j1, 0)
                 for n0 in range(0, WIDTH, PART):
-                    room = rooms[1][:, 2 * PACK * n0 : 2 * PACK * (n0 + PART)]
-                    make_h(woven[:, 1, n0 : n0 + PART], j1 + n0, 1, room=room)
+                    make_h(woven[:, 1, n0 : n0 + PART], j1 + n0, 1)
                 last_term = "gain_tanh%d_1" % (j1 + PART)
             else:
                 make_h(woven[:, 0], j1, 0)

from contextlib import ExitStack

import concourse.mybir as mybir
from concourse.masks import make_identity

K, T, S, H, N = 1024, 4096, 1024, 1024, 512
FLOPS = 2 * K * H * S + 2 * H * N * S

F32 = mybir.dt.float32
BF16 = mybir.dt.bfloat16
I32 = mybir.dt.int32
U32 = mybir.dt.uint32
U16 = mybir.dt.uint16
U8 = mybir.dt.uint8
FP8X4 = mybir.dt.float8_e4m3fn_x4
FP4X4 = mybir.dt.float4_e2m1fn_x4
ACT = mybir.ActivationFunctionType
ALU = mybir.AluOpType

P = 128
PACK = 4
PASS = P * PACK
BANK = 512
PART = 128
WIDTH = 256
SLICES = S // WIDTH
HALF = N // 2
SCALE_ROWS = 96
PLANE = S + H
W1_AT = 4 * T
THIRD_AT = W1_AT + 4 * H
WOVEN_AT = THIRD_AT + HALF * PACK
FIRST_AT = WOVEN_AT + 2 * WIDTH * PACK
THIRD_WORDS_AT = FIRST_AT + 2 * HALF * PACK
TANH_BUFFERS = 4
RUN = 4
PER_COLUMN = 16
A_BANKS, Y_BANKS = 5, 3


def tile_list_sorted_poem_gates_kernel(
    tc, tab_words, tab_scales, offs, w1_words, w1_scales, gain, w2, offs2, wgo, x0, out
):
    nc = tc.nc
    with ExitStack() as ctx:
        keep = ctx.enter_context(tc.tile_pool(name="keep", bufs=1))
        reuse = ctx.enter_context(tc.tile_pool(name="reuse", bufs=1))
        work = ctx.enter_context(tc.tile_pool(name="work", bufs=2))
        psum_a = ctx.enter_context(tc.psum_pool(name="psum_a", bufs=A_BANKS))
        psum_y = ctx.enter_context(tc.psum_pool(name="psum_y", bufs=Y_BANKS))

        offs_sb = keep.tile([P, S // PER_COLUMN], U16, name="offs_sb")
        offs2_sb = keep.tile([P, S // PER_COLUMN], U16, name="offs2_sb")
        tab_sc = keep.tile([P, T], U8, name="tab_sc", align_bytes=64)
        w1_sc_raw = keep.tile([P, H], U8, name="w1_sc_raw", align_bytes=64)
        planes = keep.tile([P, 2 * PLANE], U8, name="planes", align_bytes=64)
        nc.vector.memset(tab_sc[0:SCALE_ROWS, :].bitcast(I32), 0)
        nc.vector.memset(w1_sc_raw[0:SCALE_ROWS, :].bitcast(I32), 0)
        nc.vector.memset(planes[:].bitcast(I32), 0)

        nc.sync.dma_start(offs_sb[:], offs)
        nc.sync.dma_start(tab_sc[SCALE_ROWS:P, :].bitcast(I32), tab_scales.bitcast(I32).rearrange("a q t -> (a q) t"))
        nc.sync.dma_start(w1_sc_raw[SCALE_ROWS:P, :].bitcast(I32), w1_scales.bitcast(I32).rearrange("a q c -> (a q) c"))
        nc.sync.dma_start(offs2_sb[:], offs2)
        gain_sb = keep.tile([P, 2, PACK], F32, name="gain_sb", align_bytes=64)
        nc.sync.dma_start(gain_sb[:], gain.rearrange("(b p t) -> p b t", b=2, t=PACK))
        w1_raw = keep.tile([P, 2, 2 * H], U8, name="w1_raw", tag="after_w1_raw", align_bytes=64)
        nc.sync.dma_start(w1_raw[:].bitcast(I32), w1_words.bitcast(I32).rearrange("a p c -> p a c"))
        tab_w0 = keep.tile([P, T], I32, name="tab_w0", tag="after_tab_w0", align_bytes=64)
        nc.sync.dma_start(tab_w0[:], tab_words[0].rearrange("p t i -> p (t i)").bitcast(I32))
        v_sc_rows = reuse.tile([P, S], U8, name="v_sc_rows", offset=W1_AT - S // 2, align_bytes=64)
        nc.vector.tensor_copy(v_sc_rows[:], tab_sc[:].indirect(offs_sb[:]))
        sc_rows = keep.tile([P, PLANE], U8, name="sc_rows", align_bytes=64)
        nc.vector.tensor_copy(
            sc_rows[:, S:].rearrange("p (g t h l) -> p g h t l", g=2, t=4, l=16),
            w1_sc_raw[:].rearrange("p (g h l t) -> p g h t l", g=2, t=4, l=16),
        )
        nc.vector.tensor_copy(sc_rows[:, 0:S].bitcast(I32), v_sc_rows[:].bitcast(I32))

        def move_rows(a):
            for quadrant in range(4):
                row = SCALE_ROWS + 16 * a + 4 * quadrant
                nc.sync.dma_start(
                    planes[32 * quadrant : 32 * quadrant + 4, PLANE * a : PLANE * (a + 1)].bitcast(I32),
                    sc_rows[row : row + 4, :].bitcast(I32),
                )

        move_rows(0)

        w1_w = reuse.tile([P, 2, 2 * H], U8, name="w1_w", offset=W1_AT, align_bytes=64)
        nc.vector.tensor_copy(
            w1_w[:].rearrange("p a c -> p (a c)").bitcast(U16).rearrange("p (g t h l) -> p g h t l", g=4, t=4, l=8),
            w1_raw[:].rearrange("p a c -> p (a c)").bitcast(U16).rearrange("p (g h l t) -> p g h t l", g=4, t=4, l=8),
        )
        tab_w1 = reuse.tile([P, T], I32, name="tab_w1", offset=0, align_bytes=64)
        nc.sync.dma_start(tab_w1[:], tab_words[1].rearrange("p t i -> p (t i)").bitcast(I32))
        move_rows(1)

        def gather_words(words, window, j0, j1):
            entries = offs_sb[:, j0 // PER_COLUMN : j1 // PER_COLUMN]
            nc.vector.tensor_copy(words[:, j0:j1], window[:].bitcast(U32).indirect(entries))

        v_w = [keep.tile([P, S], U32, name="v_w%d" % a, align_bytes=64) for a in range(2)]
        gather_words(v_w[0], tab_w0, S // 2, S)
        gather_words(v_w[0], tab_w0, 0, S // 2)
        gather_words(v_w[1], tab_w1, 0, WIDTH)
        gather_words(v_w[1], tab_w1, WIDTH, S)

        warm_in = keep.tile([P, 1], F32, name="warm_in")
        warm_out = keep.tile([P, 1], F32, name="warm_out")
        nc.gpsimd.memset(warm_in[:], 0.0)
        nc.scalar.activation(warm_out[:], warm_in[:], ACT.Sigmoid)

        identity = keep.tile([P, P], F32, name="identity", align_bytes=64)
        make_identity(nc, identity[:])

        def into_psum(values):
            width = values.shape[1]
            turned = psum_y.tile([P, width], F32, name="y_bank")
            for c0 in range(0, width, P):
                nc.tensor.transpose(turned[:, c0 : c0 + P], values[:, c0 : c0 + P], identity[:])
            turned_sb = work.tile([P, width], F32, name="turned_sb")
            nc.scalar.copy(turned_sb[:], turned[:])
            upright = psum_y.tile([P, width], F32, name="y_bank")
            for c0 in range(0, width, P):
                nc.tensor.transpose(upright[:, c0 : c0 + P], turned_sb[:, c0 : c0 + P], identity[:])
            return upright

        gain_woven = keep.tile([P, 2, P // PACK, PACK], F32, name="gain_woven", align_bytes=64)
        nc.scalar.copy(gain_woven[:], gain_sb[:].unsqueeze(2).to_broadcast([P, 2, P // PACK, PACK]))
        gain_psum = into_psum(gain_woven[:].rearrange("p b n t -> p (b n t)"))

        w2_rows = w2.rearrange("(b p t) (half n) -> half b p t n", b=2, t=PACK, half=2)
        w2_width = PACK * HALF
        early = keep.tile([P, 2 * w2_width], F32, name="early", tag="after_w1_raw", align_bytes=64)
        late = keep.tile([P, 2 * w2_width + S], F32, name="late", tag="after_tab_w0", align_bytes=64)
        w2_raw = [[tile[:, w2_width * b : w2_width * (b + 1)] for b in range(2)] for tile in (early, late)]
        for half in range(2):
            for b in range(2):
                nc.sync.dma_start(w2_raw[half][b].rearrange("p (t n) -> p t n", t=PACK), w2_rows[half, b])
        wgo_sb = late[:, 2 * w2_width : 2 * w2_width + S]
        nc.sync.dma_start(wgo_sb, wgo)
        x0_all = reuse.tile([P, 4 * S], F32, name="x0_all", offset=0, align_bytes=64)
        x0_sb = [x0_all[:, S * n : S * (n + 1)] for n in range(4)]
        for n in range(4):
            nc.sync.dma_start(x0_sb[n], x0[P * n : P * (n + 1), :])

        def weave_on_gpsimd(woven, half, b):
            raw = w2_raw[half][b].rearrange("p (t n) -> p n t", t=PACK)
            nc.gpsimd.tensor_scalar(woven, raw, 1.0, 0.0, ALU.mult, ALU.add)

        def quantise(woven, name, words=None):
            passes = woven.shape[1]
            count = passes * woven.shape[2]
            if words is None:
                words = keep.tile([P, count], U32, name=name + "_w", tag=name + "_w", align_bytes=64)
            scales = keep.tile([P, count], U8, name=name + "_sc", align_bytes=64)
            nc.vector.quantize_mx(
                out=words[:].bitcast(FP8X4), scales=scales[:], in_=woven[:].rearrange("p b n t -> p (b n t)")
            )
            return [tile[:].rearrange("p (b n) -> p b n", b=passes) for tile in (words, scales)]

        def first_product(b, parts):
            bank = psum_a.tile([P, BANK], F32, name="a_bank")
            width = BANK // len(parts)
            for a in range(2):
                for place, (t, j) in enumerate(parts):
                    c0 = PASS * b + P * t
                    nc.tensor.matmul_mx(
                        out=bank[:, width * place : width * (place + 1)],
                        lhsT=w1_w[:, a, 2 * c0 : 2 * (c0 + P)].bitcast(FP4X4),
                        lhsT_scale=planes[:, PLANE * a + S + c0 : PLANE * a + S + c0 + P],
                        rhs=v_w[a][:, j : j + width].bitcast(FP8X4),
                        rhs_scale=planes[:, PLANE * a + j : PLANE * a + j + width],
                        start=(a == 0 and place == 0),
                        stop=(a == 1 and place == len(parts) - 1),
                    )
            return bank

        def make_h(h_out, j0, b):
            width = h_out.shape[1]
            shape = [P, width // RUN, PACK, RUN]
            gain_tanh = keep.tile(shape, F32, name="gain_tanh", tag="gain_tanh%d_%d" % (j0, b), align_bytes=64)
            gain_a = keep.tile(shape, F32, name="gain_a", tag="gain_a%d_%d" % (j0, b), align_bytes=64)
            per_bank = BANK // width
            for t0 in range(0, PACK, per_bank):
                ts = range(t0, t0 + per_bank)
                bank = first_product(b, [(t, j0) for t in ts])
                tanh_a = work.tile([P, BANK], F32, name="tanh_a", bufs=TANH_BUFFERS)
                nc.scalar.activation(tanh_a[:], bank[:], ACT.Tanh)
                for t in ts:
                    cols = slice(width * (t - t0), width * (t - t0 + 1))
                    source = bank[:, cols].rearrange("p (c i) -> p c i", i=RUN)
                    nc.scalar.activation(gain_a[:, :, t, :], source, ACT.Copy, scale=gain_sb[:, b, t : t + 1])
                for t in ts:
                    cols = slice(width * (t - t0), width * (t - t0 + 1))
                    source = tanh_a[:, cols].rearrange("p (c i) -> p c i", i=RUN)
                    nc.scalar.activation(gain_tanh[:, :, t, :], source, ACT.Copy, scale=gain_sb[:, b, t : t + 1])
            nc.gpsimd.tensor_tensor(h_out.rearrange("p (c i) t -> p c t i", i=RUN), gain_a[:], gain_tanh[:], ALU.add)

        h_q = []
        w2_q = {}

        def second_product(chosen):
            bank = psum_y.tile([P, WIDTH * len(chosen)], F32, name="y_bank")
            for place, (n, k) in enumerate(chosen):
                for b in range(2):
                    nc.tensor.matmul_mx(
                        out=bank[:, WIDTH * place : WIDTH * (place + 1)],
                        lhsT=w2_q[n, b][0].bitcast(FP8X4),
                        lhsT_scale=w2_q[n, b][1],
                        rhs=h_q[k][0][:, b, :].bitcast(FP8X4),
                        rhs_scale=h_q[k][1][:, b, :],
                        start=(b == 0),
                        stop=(b == 1),
                    )
            return bank

        def weighted_tile(tag, width=WIDTH):
            return keep.tile([P, width], F32, name="weighted", tag=tag, align_bytes=64)

        def weigh(engine, weighted, y, j0):
            engine.tensor_tensor(weighted, y, wgo_sb[:, j0 : j0 + y.shape[1]], ALU.mult)

        def copy_out(y_psum, tag):
            y_sb = keep.tile([P, y_psum.shape[1]], F32, name="y_sb", tag=tag, align_bytes=64)
            nc.scalar.copy(y_sb[:], y_psum)
            return y_sb

        def places(j0, width):
            return offs2_sb[:, j0 // PER_COLUMN : (j0 + width) // PER_COLUMN]

        def put_back(page, weighted, j0):
            nc.vector.tensor_copy(pages[page][:].indirect(places(j0, weighted.shape[1])), weighted[:])

        w2_first = reuse.tile([P, 2, HALF, PACK], BF16, name="w2_first", offset=FIRST_AT, align_bytes=64)
        w2_third = reuse.tile([P, 1, HALF, PACK], BF16, name="w2_third", offset=THIRD_AT, align_bytes=64)
        for b in range(2):
            weave_on_gpsimd(w2_first[:, b], 0, b)
        weave_on_gpsimd(w2_third[:, 0], 1, 0)

        def sum_on_vector(total, b, j0):
            for n0 in range(0, total.shape[1], PART):
                woven_a = first_product(b, [(t, j0 + n0) for t in range(PACK)])[:].rearrange("p (t j) -> p j t", t=PACK)
                tanh_a = work.tile([P, PART, PACK], F32, name="tanh_a", bufs=TANH_BUFFERS)
                nc.scalar.activation(tanh_a[:], woven_a, ACT.Tanh)
                nc.vector.tensor_tensor(total[:, n0 : n0 + PART, :], woven_a, tanh_a[:], ALU.add)

        def times_gain(h_out, total, b):
            runs = total.shape[1] * PACK // P
            nc.vector.tensor_tensor(
                h_out.rearrange("p (m n) t -> p m (n t)", m=runs),
                total[:].rearrange("p (m n) t -> p m (n t)", m=runs),
                gain_psum[:, P * b : P * (b + 1)].unsqueeze(1).to_broadcast([P, runs, P]),
                ALU.mult,
            )

        def sum_on_tensor(b, j0):
            bank = psum_a.tile([P, BANK], F32, name="a_bank")
            for a in range(2):
                nc.tensor.matmul_mx(
                    out=bank[:],
                    lhsT=v_w[a][:, j0 : j0 + P].bitcast(FP8X4),
                    lhsT_scale=planes[:, PLANE * a + j0 : PLANE * a + j0 + P],
                    rhs=w1_w[:, a, 2 * PASS * b : 2 * PASS * (b + 1)].bitcast(FP4X4),
                    rhs_scale=planes[:, PLANE * a + S + PASS * b : PLANE * a + S + PASS * (b + 1)],
                    start=(a == 0),
                    stop=(a == 1),
                )
            terms = [keep.tile([P, BANK], F32, name="term%d" % i, align_bytes=64) for i in range(2)]
            nc.scalar.activation(terms[0][:], bank[:], ACT.Tanh)
            nc.scalar.copy(terms[1][:], bank[:])
            total = psum_y.tile([P, BANK], F32, name="y_bank")
            for i, term in enumerate(terms):
                for t in range(PACK):
                    cols = slice(P * t, P * (t + 1))
                    first, final = (i, t) == (0, 0), (i, t) == (1, PACK - 1)
                    nc.tensor.matmul(total[:, cols], term[:, cols], identity[:], start=first, stop=final, is_transpose=True)
            return total[:].rearrange("p (t j) -> p j t", t=PACK)

        pieces = [(0, 0, WIDTH), (1, 0, PART)]
        sums = [
            keep.tile([P, count, PACK], F32, name="total", tag="total%d_%d" % (b, n0), align_bytes=64)
            for b, n0, count in pieces
        ]
        for total, (b, n0, count) in zip(sums, pieces):
            sum_on_vector(total, b, n0)
        turned_sum = sum_on_tensor(1, PART)
        woven_first = keep.tile([P, 2, WIDTH, PACK], BF16, name="woven_first", align_bytes=64)
        for total, (b, n0, count) in zip(sums, pieces):
            times_gain(woven_first[:, b, n0 : n0 + count], total, b)
        nc.vector.tensor_tensor(
            woven_first[:, 1, PART:], turned_sum, gain_sb[:, 1:2, :].to_broadcast([P, PART, PACK]), ALU.mult
        )
        first_words = keep.tile([P, N], U32, name="w2_first_w", tag="total1_0", align_bytes=64)
        words, scales = quantise(w2_first, "w2_first", first_words)
        for n in range(2):
            for b in range(2):
                w2_q[n, b] = (words[:, b, P * n : P * (n + 1)], scales[:, b, P * n : P * (n + 1)])
        h_q.append(quantise(woven_first, "h0"))
        w2_fourth = reuse.tile([P, 1, HALF, PACK], BF16, name="w2_fourth", offset=FIRST_AT, align_bytes=64)
        nc.vector.tensor_copy(
            w2_fourth[:, 0].rearrange("p (c i) t -> p c t i", i=RUN),
            w2_raw[1][1].rearrange("p (t c i) -> p c t i", t=PACK, i=RUN),
        )
        third_words = reuse.tile([P, HALF], U32, name="w2_third_w", offset=THIRD_WORDS_AT, align_bytes=64)
        for b, (quarter, target) in enumerate([(w2_third, third_words), (w2_fourth, None)]):
            words, scales = quantise(quarter, "w2_rest%d" % b, target)
            for n in range(2):
                w2_q[2 + n, b] = (words[:, 0, P * n : P * (n + 1)], scales[:, 0, P * n : P * (n + 1)])

        last = SLICES - 1
        pages = [
            keep.tile([P, S], F32, name="page", tag="h0_w" if n == 1 else "page%d" % n, align_bytes=64) for n in range(4)
        ]

        def first_two(k):
            bank = second_product([(0, k), (1, k)])
            ys = [bank[:, WIDTH * n : WIDTH * (n + 1)] for n in range(2)]
            ready = [weighted_tile("page%d_next" % n) for n in range(2)]
            for n in range(2):
                weigh(nc.vector, ready[n][:], ys[n], WIDTH * k)
            return ready

        def by_gpsimd(page, y_psum, j0, tag):
            weighted = weighted_tile("by_gpsimd%d" % page, y_psum.shape[1])
            weigh(nc.gpsimd, weighted[:], copy_out(y_psum, tag)[:], j0)
            put_back(page, weighted, j0)

        for k in range(last):
            j0, j1 = WIDTH * k, WIDTH * (k + 1)
            ready = first_two(k)
            held_page = 3 if k == 0 else 2
            other = second_product([(2, k), (3, k)] if k == 0 else [(2, k)])
            put_back(0, ready[0], j0)
            if k == 0:
                page2 = weighted_tile("page2_next")
                weigh(nc.vector, page2[:], other[:, 0:WIDTH], j0)
            put_back(1, ready[1], j0)
            if k == 0:
                put_back(2, page2, j0)
            woven = reuse.tile([P, 2, WIDTH, PACK], BF16, name="woven", offset=WOVEN_AT, align_bytes=64)
            if k == last - 1:
                make_h(woven[:, 0], j1, 0)
                for n0 in range(0, WIDTH, PART):
                    make_h(woven[:, 1, n0 : n0 + PART], j1 + n0, 1)
                last_term = "gain_tanh%d_1" % (j1 + PART)
            else:
                make_h(woven[:, 0], j1, 0)
                make_h(woven[:, 1], j1, 1)
                last_term = "gain_a%d_1" % j1
            held_y = other[:, WIDTH * (held_page - 2) : WIDTH * (held_page - 1)]
            if k < last - 1:
                held = weighted_tile(last_term)
                weigh(nc.vector, held[:], held_y, j0)
                h_q.append(quantise(woven, "h%d" % (k + 1)))
                put_back(held_page, held, j0)
            else:
                held = copy_out(held_y, last_term)
                h_q.append(quantise(woven, "h%d" % (k + 1)))
                weigh(nc.vector, pages[held_page][:].indirect(places(j0, WIDTH)), held[:], j0)
                closing = reuse.tile([P, last * WIDTH], F32, name="closing", offset=WOVEN_AT, align_bytes=64)
                kept = copy_out(second_product([(3, k - 1), (3, k)])[:], "y_kept")
                weigh(nc.gpsimd, closing[:, 0:j0], kept[:], WIDTH)

        ready = first_two(last)
        for n in range(2):
            put_back(n, ready[n], WIDTH * last)
        by_gpsimd(2, second_product([(2, last)])[:], WIDTH * last, "y_last2")
        weigh(nc.gpsimd, closing[:, WIDTH * (last - 1) :], copy_out(second_product([(3, last)])[:], "y_last3")[:], WIDTH * last)
        put_back(3, closing, WIDTH)

        def finish(n, c0, engine, gate, result):
            width = result.shape[1]
            nc.scalar.activation(gate, pages[n][:, c0 : c0 + width], ACT.Sigmoid)
            engine.tensor_tensor(result, gate, x0_sb[n][:, c0 : c0 + width], ALU.mult)
            nc.sync.dma_start(out[P * n : P * (n + 1), c0 : c0 + width], result)

        gates = keep.tile([P, 4, S], F32, name="gates", tag="y_last2", align_bytes=64)
        on_gpsimd = [(0, 0, WIDTH), (0, WIDTH, S - WIDTH), (1, 0, S), (2, 0, BANK)]
        on_vector = [(2, BANK, BANK), (3, 0, 3 * PART), (3, 3 * PART, 3 * PART), (3, S - WIDTH, WIDTH)]
        last_gate = keep.tile([P, on_gpsimd[-1][2]], F32, name="last_gate", tag="y_last3", align_bytes=64)
        for n, c0, width in on_gpsimd:
            gate = last_gate[:] if (n, c0, width) == on_gpsimd[-1] else gates[:, n, c0 : c0 + width]
            finish(n, c0, nc.gpsimd, gate, x0_sb[n][:, c0 : c0 + width])
        results = keep.tile([P, 2, S], F32, name="results", tag="y_last3", align_bytes=64)
        for n, c0, width in on_vector:
            finish(n, c0, nc.vector, gates[:, n, c0 : c0 + width], results[:, n - 2, c0 : c0 + width])
